import numpy as np
import ml_dtypes


def mxq(x, axis, fmt="e4m3"):
    dtype, down = {"e4m3": (ml_dtypes.float8_e4m3fn, 7), "e5m2": (ml_dtypes.float8_e5m2, 14)}[fmt]
    v = np.moveaxis(np.asarray(x, np.float32).astype(ml_dtypes.bfloat16).astype(np.float64), axis, -1)
    blocks = v.reshape(v.shape[:-1] + (-1, 32))
    amax = np.abs(blocks).max(-1, keepdims=True)
    byte = np.maximum(np.where(amax > 0, np.frexp(amax)[1] - 1 + 127, 0) - down, 1)
    scale = np.exp2(byte - 127.0)
    codes = (blocks / scale).astype(np.float32).astype(dtype).astype(np.float64)
    return np.moveaxis((codes * scale).reshape(v.shape), -1, axis)


WIDE = False


def mx_kscale(k):
    if not WIDE:
        return np.ones(k)
    levels = np.array([10, -10, 5, -5, 0])
    if k % 512:
        return np.exp2(np.random.permutation(np.resize(levels, k // 32))).repeat(32)
    a = np.empty((k // 512, 16))
    for p in range(k // 512):
        a[p, :8] = np.random.permutation(np.resize(levels, 8))
        for g in range(8):
            far = levels[np.abs(levels - a[p, g]) >= 10]
            a[p, g + 8] = far[np.random.randint(len(far))]
    return np.exp2(a.ravel()).repeat(32)


def f64(x):
    return np.asarray(x).astype(np.float64)


def striped(idx):
    return np.tile(idx.reshape(-1, 16).T, (8, 1)).astype(np.uint16)


def unstriped(offs):
    return offs[:16].T.reshape(-1).astype(np.int64)


E2M1 = np.array([0.0, 0.5, 1.0, 1.5, 2.0, 3.0, 4.0, 6.0, -0.0, -0.5, -1.0, -1.5, -2.0, -3.0, -4.0, -6.0])


def pack_weight(w, fmt):
    k, n = w.shape
    w = f64(np.asarray(w, np.float32).astype(ml_dtypes.bfloat16)).reshape(k // 32, 32, n)
    amax = np.abs(w).max(1)
    if fmt == "e4m3":
        byte = np.frexp(amax)[1] - 1 + 127 - 7
    else:
        mant, ex = np.frexp(amax / 6.0)
        byte = np.where(mant > 0.5, ex, ex - 1) + 127
    byte = np.clip(np.where(amax > 0, byte, 1), 1, 254)
    scaled = (w * np.exp2(127.0 - byte)[:, None, :]).reshape(k, n).astype(np.float32)
    by_word = np.ascontiguousarray(scaled.reshape(k // 512, 128, 4, n).transpose(0, 1, 3, 2))
    if fmt == "e4m3":
        words = by_word.astype(ml_dtypes.float8_e4m3fn).view(np.uint8)
    else:
        c = by_word.astype(ml_dtypes.float4_e2m1fn).view(np.uint8) & 0xF
        words = (c[..., 0::2] | (c[..., 1::2] << 4)).reshape(k // 512, 128, 2 * n)
    return np.ascontiguousarray(words), np.ascontiguousarray(byte.astype(np.uint8).reshape(k // 512, 16, n))


def unpack_weight(words, scales, fmt):
    g, _, n = scales.shape
    words = np.ascontiguousarray(words).reshape(g, 128, n, -1)
    if fmt == "e4m3":
        vals = words.view(ml_dtypes.float8_e4m3fn).astype(np.float64)
    else:
        nib = np.empty((g, 128, n, 4), np.uint8)
        nib[..., 0::2] = words & 0xF
        nib[..., 1::2] = words >> 4
        vals = E2M1[nib]
    vals = vals * np.repeat(np.exp2(scales.astype(np.float64) - 127.0), 8, axis=1)[..., None]
    return vals.transpose(0, 1, 3, 2).reshape(g * 512, n)


def gelu(v):
    return 0.5 * v * (1.0 + np.tanh(np.sqrt(2.0 / np.pi) * (v + 0.044715 * v**3)))


def often(T, S):
    return np.random.permutation(T)[(T * np.random.uniform(0, 1, S) ** 4).astype(np.int64)]


K, H, N, T, S, T2, P = 1024, 1024, 512, 4096, 1024, 2048, 512

def setup_inputs():
    n = np.random.standard_normal
    s = mx_kscale(K)[:, None]
    u = mx_kscale(H)[:, None]
    tab_words, tab_scales = pack_weight(n((K, T)) * s, "e4m3")
    tab2_words, tab2_scales = pack_weight(n((K, T2)) * s, "e4m3")
    w1_words, w1_scales = pack_weight(n((K, H)) / np.sqrt(K) / s, "e2m1")
    w3_words, w3_scales = pack_weight(n((H, N)) / np.sqrt(H) / u, "e4m3")
    return {
        "tab_words": tab_words, "tab_scales": tab_scales,
        "offs": striped(np.random.permutation(T)[:S]),
        "pos1": striped(often(S, P)),
        "tab2_words": tab2_words, "tab2_scales": tab2_scales,
        "offs2": striped(np.random.permutation(T2)[:P]),
        "w1_words": w1_words, "w1_scales": w1_scales,
        "w2": (n((K, H)) / np.sqrt(K) / s).astype(np.float32),
        "gain": (np.exp(0.3 * n(H)) * u[:, 0]).astype(np.float32),
        "w3_words": w3_words, "w3_scales": w3_scales,
    }

def reference(tab_words, tab_scales, offs, pos1, tab2_words, tab2_scales, offs2,
              w1_words, w1_scales, w2, gain, w3_words, w3_scales):
    v = unpack_weight(tab_words, tab_scales, "e4m3")[:, unstriped(offs)]
    v2 = unpack_weight(tab2_words, tab2_scales, "e4m3")[:, unstriped(offs2)]
    w1 = unpack_weight(w1_words, w1_scales, "e2m1")
    w3 = unpack_weight(w3_words, w3_scales, "e4m3")
    x1 = w1.T @ v
    b = mxq(f64(w2), 0, "e4m3").T @ v2
    d = b - x1[:, unstriped(pos1)]
    z = f64(gain)[:, None] * d / np.sqrt(1.0 + d * d)
    return w3.T @ mxq(z, 0, "e4m3")

@@ -1,0 +1,290 @@
+from contextlib import ExitStack
+
+import concourse.mybir as mybir
+
+K, H, N, T, S, T2, M = 1024, 1024, 512, 4096, 1024, 2048, 512
+FLOPS = 2 * K * H * S + 2 * K * H * M + 2 * H * N * M
+
+F32 = mybir.dt.float32
+BF16 = mybir.dt.bfloat16
+I32 = mybir.dt.int32
+U32 = mybir.dt.uint32
+U16 = mybir.dt.uint16
+U8 = mybir.dt.uint8
+FP8X4 = mybir.dt.float8_e4m3fn_x4
+FP4X4 = mybir.dt.float4_e2m1fn_x4
+ALU = mybir.AluOpType
+ACT = mybir.ActivationFunctionType
+
+P = 128
+PACK = 4
+PASS = 512
+BANK = 512
+CHUNK = 128
+KIB = 1024
+PLACE = {
+    "v_sc0": 0, "w1_raw": 0, "tab_w1": KIB, "w2_raw01": KIB, "w3_w": KIB,
+    "v_w0": 17 * KIB, "tab_sc": 19 * KIB, "tab2_w0": 21 * KIB, "w2_raw10": 21 * KIB,
+    "tab_w0": 29 * KIB, "w1_sc": 29 * KIB,
+    "v2_sc": 45 * KIB, "w1_sc_raw": 45 * KIB, "tab2_w1": 46 * KIB, "w2_raw11": 46 * KIB,
+    "v_w1": 54 * KIB, "tab2_sc": 57 * KIB, "w2_raw00": 58 * KIB,
+}
+
+
+def tile_list_tract_county_audit_kernel(
+    tc, tab_words, tab_scales, offs, pos1, tab2_words, tab2_scales, offs2,
+    w1_words, w1_scales, w2, gain, w3_words, w3_scales, out,
+):
+    nc = tc.nc
+    with ExitStack() as ctx:
+        lists = ctx.enter_context(tc.tile_pool(name="lists", bufs=1))
+        keep = ctx.enter_context(tc.tile_pool(name="keep", bufs=1))
+        stage = ctx.enter_context(tc.tile_pool(name="stage", bufs=1))
+        ring = ctx.enter_context(tc.tile_pool(name="ring", bufs=3))
+        psum = ctx.enter_context(tc.psum_pool(name="psum", bufs=1))
+
+        def placed(name, shape, dtype):
+            return stage.tile(shape, dtype, name=name, align_bytes=64, offset=PLACE[name])
+
+        def bank(index, shape):
+            return psum.tile(shape, F32, name="bank", tag="bank%d" % index)
+
+        def words(dram, a):
+            return dram[a].rearrange("p t i -> p (t i)").bitcast(I32)
+
+        def load_packed_scales(queue, plane, dram):
+            for q in range(4):
+                queue.dma_start(out=plane[32 * q : 32 * q + 8, :].bitcast(I32),
+                                in_=dram.bitcast(I32)[:, 4 * q : 4 * q + 4, :])
+
+        offs_sb = lists.tile([P, S // 16], U16, name="offs_sb")
+        offs2_sb = lists.tile([P, M // 16], U16, name="offs2_sb")
+        pos_sb = lists.tile([P, M // 16], U16, name="pos_sb")
+        nc.sync.dma_start(offs_sb[:], offs)
+        nc.sync.dma_start(offs2_sb[:], offs2)
+        nc.sync.dma_start(pos_sb[:], pos1)
+
+        g = keep.tile([P, 2, PACK], F32, name="g")
+        nc.gpsimd.dma_start(out=g[:], in_=gain.rearrange("(a p t) -> p a t", a=2, t=PACK))
+        tab_sc = placed("tab_sc", [P, T], U8)
+        nc.vector.memset(tab_sc[:].bitcast(I32), 0)
+        load_packed_scales(nc.scalar, tab_sc, tab_scales)
+
+        w1_raw = placed("w1_raw", [P, 2, 2 * H], U8)
+        nc.sync.dma_start(out=w1_raw[:].bitcast(I32), in_=w1_words.bitcast(I32).rearrange("a p c -> p a c"))
+
+        def load_words(dram, a, name):
+            tile = placed(name, [P, dram.shape[2]], U32)
+            nc.sync.dma_start(out=tile[:].bitcast(I32), in_=words(dram, a))
+            return tile
+
+        tab_w = [load_words(tab_words, 0, "tab_w0")]
+        w1_sc_raw = placed("w1_sc_raw", [P, 2, H], U8)
+        tab2_sc = placed("tab2_sc", [P, T2], U8)
+        w3_sc = keep.tile([P, N], U8, name="w3_sc", align_bytes=64)
+        v_sc1 = keep.tile([P, S], U8, name="v_sc1", align_bytes=64)
+        nc.vector.memset(w1_sc_raw[:].rearrange("p a c -> p (a c)").bitcast(I32), 0)
+        nc.vector.memset(tab2_sc[:].bitcast(I32), 0)
+        nc.vector.memset(w3_sc[:].bitcast(I32), 0)
+        nc.vector.memset(v_sc1[:].bitcast(I32), 0)
+        for q in range(4):
+            nc.scalar.dma_start(out=w1_sc_raw[32 * q : 32 * q + 4, :, :].bitcast(I32),
+                                in_=w1_scales.bitcast(I32)[:, 4 * q : 4 * q + 4, :].rearrange("a r c -> r a c"))
+        load_packed_scales(nc.gpsimd, tab2_sc, tab2_scales)
+        load_packed_scales(nc.gpsimd, w3_sc, w3_scales)
+
+        warm = keep.tile([P, 1], F32, name="warm")
+        nc.scalar.activation(warm[:], g[:, 0, 0:1], ACT.Abs_reciprocal_sqrt, bias=1.0)
+
+        w1_w = keep.tile([P, 2, 2 * H], U8, name="w1_w", align_bytes=64)
+        nc.vector.tensor_copy(
+            out=w1_w[:].bitcast(U16).rearrange("p a (h t m) -> p (a h) t m", h=2, t=PACK),
+            in_=w1_raw[:].bitcast(U16).rearrange("p a (h m t) -> p (a h) t m", h=2, t=PACK))
+        tab_w.append(load_words(tab_words, 1, "tab_w1"))
+
+        v_sc0 = placed("v_sc0", [P, S], U8)
+        nc.vector.tensor_copy(out=v_sc0[:], in_=tab_sc[:].indirect(offs_sb[:]))
+        nc.scalar.dma_start(out=v_sc1[0:100, :].bitcast(I32), in_=v_sc0[4:104, :].bitcast(I32))
+        v_sc = [v_sc0, v_sc1]
+
+        tab2_w = [load_words(tab2_words, 0, "tab2_w0")]
+
+        v_w = [placed("v_w0", [P, S], U32)]
+        nc.vector.tensor_copy(out=v_w[0][:], in_=tab_w[0][:].indirect(offs_sb[:]))
+
+        w1_sc = placed("w1_sc", [P, 2, H], U8)
+        nc.vector.tensor_copy(
+            out=w1_sc[:].rearrange("p a (h t m) -> p (a h) t m", h=2, t=PACK),
+            in_=w1_sc_raw[:].rearrange("p a (h m t) -> p (a h) t m", h=2, t=PACK))
+        tab2_w.append(load_words(tab2_words, 1, "tab2_w1"))
+
+        g_safe = keep.tile([P, 2, PACK], F32, name="g_safe")
+        g_inv = keep.tile([P, 2, PACK], F32, name="g_inv")
+        nc.vector.scalar_tensor_tensor(out=g_safe[:], in0=g[:], scalar=0.0, in1=g[:], op0=ALU.is_equal, op1=ALU.add)
+        nc.vector.reciprocal(out=g_inv[:], in_=g_safe[:])
+
+        w2_raw = {}
+
+        def w2_load(h, a):
+            tile = placed("w2_raw%d%d" % (h, a), [P, PACK, PASS], F32)
+            nc.sync.dma_start(
+                out=tile[:],
+                in_=w2[PASS * a : PASS * (a + 1), PASS * h : PASS * (h + 1)].rearrange("(p j) c -> p j c", j=PACK))
+            w2_raw[h, a] = tile
+
+        v2_sc = placed("v2_sc", [P, M], U8)
+        nc.vector.tensor_copy(out=v2_sc[:], in_=tab2_sc[:].indirect(offs2_sb[:]))
+        w2_load(0, 0)
+        v_w.append(placed("v_w1", [P, S], U32))
+        for half in range(2):
+            nc.vector.tensor_copy(out=v_w[1][:, BANK * half : BANK * (half + 1)],
+                                  in_=tab_w[1][:].indirect(offs_sb[:, 32 * half : 32 * (half + 1)]))
+        w2_load(0, 1)
+
+        X_BANKS = 6
+        x_banks = {}
+
+        def x_pass(i, half, a):
+            if a == 0:
+                x_banks[i, half] = bank((2 * i + half) % X_BANKS, [P, BANK])
+            cols = slice(BANK * half, BANK * (half + 1))
+            nc.tensor.matmul_mx(
+                out=x_banks[i, half][:],
+                lhsT=w1_w[:, a, 2 * P * i : 2 * P * (i + 1)].bitcast(FP4X4),
+                lhsT_scale=w1_sc[:, a, P * i : P * (i + 1)],
+                rhs=v_w[a][:, cols].bitcast(FP8X4), rhs_scale=v_sc[a][:, cols],
+                start=(a == 0), stop=(a == 1))
+
+        picked = {}
+
+        def x_tile(i):
+            h, t = divmod(i, PACK)
+            x_sb = ring.tile([P, S], F32, name="x_sb", bufs=8)
+            for half in range(2):
+                if (i, half) not in x_banks:
+                    x_pass(i, half, 0)
+                x_pass(i, half, 1)
+                nc.scalar.activation(x_sb[:, BANK * half : BANK * (half + 1)], x_banks[i, half][:], ACT.Copy,
+                                     scale=g[:, h, t : t + 1])
+            picked[i] = keep.tile([P, M], F32, name="picked%d" % i)
+            nc.vector.tensor_copy(out=picked[i][:], in_=x_sb[:].indirect(pos_sb[:]))
+
+        v2_w = [keep.tile([P, M], U32, name="v2_w%d" % a, align_bytes=64) for a in range(2)]
+
+        def gather2(a):
+            nc.vector.tensor_copy(out=v2_w[a][:], in_=tab2_w[a][:].indirect(offs2_sb[:]))
+
+        w2_bf, w2_w, w2_sc = {}, {}, {}
+
+        def w2_round(h, a, copy):
+            bf = ring.tile([P, PACK, P, PACK], BF16, name="w2_bf", bufs=4, align_bytes=64)
+            dst = bf[:].rearrange("p t m j -> p m j t")
+            src = w2_raw[h, a][:].rearrange("p j (m t) -> p m j t", t=PACK)
+            copy(out=dst, in_=src)
+            w2_bf[h, a] = bf
+
+        def w2_quantize(h, a):
+            w2_w[h, a] = keep.tile([P, PASS], U32, name="w2_w%d%d" % (h, a), align_bytes=64)
+            w2_sc[h, a] = keep.tile([P, PASS], U8, name="w2_sc%d%d" % (h, a), align_bytes=64)
+            nc.vector.quantize_mx(out=w2_w[h, a][:].bitcast(FP8X4), scales=w2_sc[h, a][:],
+                                  in_=w2_bf[h, a][:].rearrange("p t m j -> p (t m j)"))
+
+        e = [keep.tile([P, PACK, M], F32, name="e%d" % h) for h in range(2)]
+        r = [keep.tile([P, PACK, M], F32, name="r%d" % h) for h in range(2)]
+        sq = r
+        B_BANKS = (6, 7, 4, 5)
+
+        def diff_tile(i):
+            h, t = divmod(i, PACK)
+            b = bank(B_BANKS[t], [P, M])
+            cols = slice(P * t, P * (t + 1))
+            for a in range(2):
+                nc.tensor.matmul_mx(
+                    out=b[:], lhsT=w2_w[h, a][:, cols].bitcast(FP8X4), lhsT_scale=w2_sc[h, a][:, cols],
+                    rhs=v2_w[a][:].bitcast(FP8X4), rhs_scale=v2_sc[4 * a :, :], start=(a == 0), stop=(a == 1))
+            nc.vector.scalar_tensor_tensor(out=e[h][:, t, :], in0=b[:], scalar=g[:, h, t : t + 1], in1=picked[i][:],
+                                           op0=ALU.mult, op1=ALU.subtract)
+            nc.scalar.activation(sq[h][:, t, :], e[h][:, t, :], ACT.Square, scale=g_inv[:, h, t : t + 1])
+
+        def root(h, lo, hi):
+            nc.scalar.activation(r[h][:, :, lo:hi], sq[h][:, :, lo:hi], ACT.Abs_reciprocal_sqrt, bias=1.0)
+
+        z_bf = [keep.tile([P, M, PACK], BF16, name="z_bf%d" % h, align_bytes=64) for h in range(2)]
+        z_w = [keep.tile([P, M], U32, name="z_w%d" % h, align_bytes=64) for h in range(2)]
+        z_sc = [keep.tile([P, M], U8, name="z_sc%d" % h, align_bytes=64) for h in range(2)]
+
+        def z_round(h, lo, hi):
+            nc.vector.tensor_tensor(
+                out=z_bf[h][:, lo:hi, :].rearrange("p (u i) t -> p u t i", i=4),
+                in0=e[h][:, :, lo:hi].rearrange("p t (u i) -> p u t i", i=4),
+                in1=r[h][:, :, lo:hi].rearrange("p t (u i) -> p u t i", i=4), op=ALU.mult)
+
+        def z_quantize(h, lo, hi):
+            nc.vector.quantize_mx(out=z_w[h][:, lo:hi].bitcast(FP8X4), scales=z_sc[h][:, lo:hi],
+                                  in_=z_bf[h][:, lo:hi, :].rearrange("p m t -> p (m t)"))
+
+        out_banks = {}
+
+        def out_pass(c, h):
+            if h == 0:
+                out_banks[c] = bank(c, [P, N // P, CHUNK])
+            cols = slice(CHUNK * c, CHUNK * (c + 1))
+            for n in range(N // P):
+                nc.tensor.matmul_mx(
+                    out=out_banks[c][:, n, :], lhsT=w3_w[:, h, P * n : P * (n + 1)].bitcast(FP8X4),
+                    lhsT_scale=w3_sc[4 * h :, P * n : P * (n + 1)],
+                    rhs=z_w[h][:, cols].bitcast(FP8X4), rhs_scale=z_sc[h][:, cols],
+                    start=(h == 0 and n == 0), stop=(h == 1 and n == N // P - 1))
+
+        def store(c):
+            res = keep.tile([P, N // P, CHUNK], F32, name="res%d" % c)
+            nc.scalar.copy(out=res[:], in_=out_banks[c][:])
+            nc.sync.dma_start(out=out[:, CHUNK * c : CHUNK * (c + 1)].rearrange("(n p) m -> p n m", p=P), in_=res[:])
+
+        for i in range(X_BANKS // 2):
+            for half in range(2):
+                x_pass(i, half, 0)
+        x_tile(0)
+        gather2(0)
+        w2_load(1, 0)
+        x_tile(1)
+        x_tile(2)
+        gather2(1)
+        w2_load(1, 1)
+        x_tile(3)
+        x_tile(4)
+        w2_round(0, 0, nc.scalar.copy)
+        x_tile(5)
+        x_tile(6)
+        x_tile(7)
+        w2_quantize(0, 0)
+        w2_round(0, 1, nc.scalar.copy)
+        w3_w = placed("w3_w", [P, 2, N], U32)
+        nc.sync.dma_start(out=w3_w[:].bitcast(I32),
+                          in_=w3_words.rearrange("a p c i -> p a (c i)").bitcast(I32))
+        w2_round(1, 0, nc.vector.tensor_copy)
+        w2_round(1, 1, nc.scalar.copy)
+        w2_quantize(0, 1)
+        w2_quantize(1, 0)
+        for t in range(PACK):
+            diff_tile(t)
+        w2_quantize(1, 1)
+        for half in range(2):
+            root(0, half * M // 2, (half + 1) * M // 2)
+        for t in range(PACK):
+            diff_tile(PACK + t)
+        chunks = M // CHUNK
+        for c in range(chunks):
+            root(1, CHUNK * c, CHUNK * (c + 1))
+        for half in range(2):
+            z_round(0, half * M // 2, (half + 1) * M // 2)
+        z_round(1, 0, CHUNK)
+        z_quantize(0, 0, M)
+        for c in range(chunks):
+            out_pass(c, 0)
+        for c in range(1, chunks + 1):
+            if c < chunks:
+                z_round(1, CHUNK * c, CHUNK * (c + 1))
+            z_quantize(1, CHUNK * (c - 1), CHUNK * c)
+            out_pass(c - 1, 1)
+            store(c - 1)

@@ -23,11 +23,11 @@ BANK = 512
 CHUNK = 128
 KIB = 1024
 PLACE = {
-    "v_sc0": 0, "w1_raw": 0, "tab_w1": KIB, "w2_raw01": KIB, "w3_w": KIB,
-    "v_w0": 17 * KIB, "tab_sc": 19 * KIB, "tab2_w0": 21 * KIB, "w2_raw10": 21 * KIB,
-    "tab_w0": 29 * KIB, "w1_sc": 29 * KIB,
-    "v2_sc": 45 * KIB, "w1_sc_raw": 45 * KIB, "tab2_w1": 46 * KIB, "w2_raw11": 46 * KIB,
-    "v_w1": 54 * KIB, "tab2_sc": 57 * KIB, "w2_raw00": 58 * KIB,
+    "w2_raw11": 0, "tab2_sc": 8 * KIB - 64, "v_w10": 8 * KIB, "tab_sc": 10 * KIB, "tab2_w": 10 * KIB,
+    "tab_w0": 26 * KIB, "w1_w": 26 * KIB, "w2_raw00": 30 * KIB,
+    "w1_raw": 42 * KIB, "w1_sc": 42 * KIB, "w2_raw01": 44 * KIB,
+    "w1_sc_raw": 52 * KIB, "v2_sc": 52 * KIB, "w2_raw10": 53 * KIB,
+    "tab_w1": 61 * KIB, "w3_w": 61 * KIB, "w3_sc": 65 * KIB,
 }
 
 
@@ -52,76 +52,15 @@ def tile_list_tract_county_audit_kernel(
         def words(dram, a):
             return dram[a].rearrange("p t i -> p (t i)").bitcast(I32)
 
-        def load_packed_scales(queue, plane, dram):
+        def load_packed_scales(queue, plane, dram, row):
             for q in range(4):
-                queue.dma_start(out=plane[32 * q : 32 * q + 8, :].bitcast(I32),
+                queue.dma_start(out=plane[32 * q + row : 32 * q + row + 8, :].bitcast(I32),
                                 in_=dram.bitcast(I32)[:, 4 * q : 4 * q + 4, :])
 
-        offs_sb = lists.tile([P, S // 16], U16, name="offs_sb")
-        offs2_sb = lists.tile([P, M // 16], U16, name="offs2_sb")
-        pos_sb = lists.tile([P, M // 16], U16, name="pos_sb")
-        nc.sync.dma_start(offs_sb[:], offs)
-        nc.sync.dma_start(offs2_sb[:], offs2)
-        nc.sync.dma_start(pos_sb[:], pos1)
-
-        g = keep.tile([P, 2, PACK], F32, name="g")
-        nc.gpsimd.dma_start(out=g[:], in_=gain.rearrange("(a p t) -> p a t", a=2, t=PACK))
-        tab_sc = placed("tab_sc", [P, T], U8)
-        nc.vector.memset(tab_sc[:].bitcast(I32), 0)
-        load_packed_scales(nc.scalar, tab_sc, tab_scales)
-
-        w1_raw = placed("w1_raw", [P, 2, 2 * H], U8)
-        nc.sync.dma_start(out=w1_raw[:].bitcast(I32), in_=w1_words.bitcast(I32).rearrange("a p c -> p a c"))
-
-        def load_words(dram, a, name):
-            tile = placed(name, [P, dram.shape[2]], U32)
-            nc.sync.dma_start(out=tile[:].bitcast(I32), in_=words(dram, a))
+        def load_words(a):
+            tile = placed("tab_w%d" % a, [P, T], U32)
+            nc.sync.dma_start(out=tile[:].bitcast(I32), in_=words(tab_words, a))
             return tile
-
-        tab_w = [load_words(tab_words, 0, "tab_w0")]
-        w1_sc_raw = placed("w1_sc_raw", [P, 2, H], U8)
-        tab2_sc = placed("tab2_sc", [P, T2], U8)
-        w3_sc = keep.tile([P, N], U8, name="w3_sc", align_bytes=64)
-        v_sc1 = keep.tile([P, S], U8, name="v_sc1", align_bytes=64)
-        nc.vector.memset(w1_sc_raw[:].rearrange("p a c -> p (a c)").bitcast(I32), 0)
-        nc.vector.memset(tab2_sc[:].bitcast(I32), 0)
-        nc.vector.memset(w3_sc[:].bitcast(I32), 0)
-        nc.vector.memset(v_sc1[:].bitcast(I32), 0)
-        for q in range(4):
-            nc.scalar.dma_start(out=w1_sc_raw[32 * q : 32 * q + 4, :, :].bitcast(I32),
-                                in_=w1_scales.bitcast(I32)[:, 4 * q : 4 * q + 4, :].rearrange("a r c -> r a c"))
-        load_packed_scales(nc.gpsimd, tab2_sc, tab2_scales)
-        load_packed_scales(nc.gpsimd, w3_sc, w3_scales)
-
-        warm = keep.tile([P, 1], F32, name="warm")
-        nc.scalar.activation(warm[:], g[:, 0, 0:1], ACT.Abs_reciprocal_sqrt, bias=1.0)
-
-        w1_w = keep.tile([P, 2, 2 * H], U8, name="w1_w", align_bytes=64)
-        nc.vector.tensor_copy(
-            out=w1_w[:].bitcast(U16).rearrange("p a (h t m) -> p (a h) t m", h=2, t=PACK),
-            in_=w1_raw[:].bitcast(U16).rearrange("p a (h m t) -> p (a h) t m", h=2, t=PACK))
-        tab_w.append(load_words(tab_words, 1, "tab_w1"))
-
-        v_sc0 = placed("v_sc0", [P, S], U8)
-        nc.vector.tensor_copy(out=v_sc0[:], in_=tab_sc[:].indirect(offs_sb[:]))
-        nc.scalar.dma_start(out=v_sc1[0:100, :].bitcast(I32), in_=v_sc0[4:104, :].bitcast(I32))
-        v_sc = [v_sc0, v_sc1]
-
-        tab2_w = [load_words(tab2_words, 0, "tab2_w0")]
-
-        v_w = [placed("v_w0", [P, S], U32)]
-        nc.vector.tensor_copy(out=v_w[0][:], in_=tab_w[0][:].indirect(offs_sb[:]))
-
-        w1_sc = placed("w1_sc", [P, 2, H], U8)
-        nc.vector.tensor_copy(
-            out=w1_sc[:].rearrange("p a (h t m) -> p (a h) t m", h=2, t=PACK),
-            in_=w1_sc_raw[:].rearrange("p a (h m t) -> p (a h) t m", h=2, t=PACK))
-        tab2_w.append(load_words(tab2_words, 1, "tab2_w1"))
-
-        g_safe = keep.tile([P, 2, PACK], F32, name="g_safe")
-        g_inv = keep.tile([P, 2, PACK], F32, name="g_inv")
-        nc.vector.scalar_tensor_tensor(out=g_safe[:], in0=g[:], scalar=0.0, in1=g[:], op0=ALU.is_equal, op1=ALU.add)
-        nc.vector.reciprocal(out=g_inv[:], in_=g_safe[:])
 
         w2_raw = {}
 
@@ -132,14 +71,81 @@ def tile_list_tract_county_audit_kernel(
                 in_=w2[PASS * a : PASS * (a + 1), PASS * h : PASS * (h + 1)].rearrange("(p j) c -> p j c", j=PACK))
             w2_raw[h, a] = tile
 
+        offs_sb = lists.tile([P, S // 16], U16, name="offs_sb")
+        offs2_sb = lists.tile([P, M // 16], U16, name="offs2_sb")
+        pos_sb = lists.tile([P, M // 16], U16, name="pos_sb")
+        tab_sc = placed("tab_sc", [P, T], U8)
+        w1_raw = placed("w1_raw", [P, 2, 2 * H], U8)
+        nc.sync.dma_start(offs_sb[:], offs)
+        load_packed_scales(nc.sync, tab_sc, tab_scales, 24)
+        tab_w = [load_words(0)]
+        nc.sync.dma_start(offs2_sb[:], offs2)
+        nc.sync.dma_start(pos_sb[:], pos1)
+        nc.sync.dma_start(out=w1_raw[:].bitcast(I32), in_=w1_words.bitcast(I32).rearrange("a p c -> p a c"))
+        tab_w.append(load_words(1))
+
+        w1_sc_raw = placed("w1_sc_raw", [P, 2, H], U8)
+        nc.gpsimd.memset(w1_sc_raw[:].rearrange("p a c -> p (a c)").bitcast(I32), 0)
+        for q in range(4):
+            engine = nc.gpsimd if q == 3 else nc.vector
+            engine.memset(tab_sc[32 * q : 32 * q + 24, :].bitcast(I32), 0)
+        for q in range(4):
+            nc.gpsimd.dma_start(out=w1_sc_raw[32 * q : 32 * q + 4, :, :].bitcast(I32),
+                                in_=w1_scales.bitcast(I32)[:, 4 * q : 4 * q + 4, :].rearrange("a r c -> r a c"))
+        g = keep.tile([P, 2, PACK], F32, name="g")
+        nc.gpsimd.dma_start(out=g[:], in_=gain.rearrange("(a p t) -> p a t", a=2, t=PACK))
+
+        warm = keep.tile([P, 1], F32, name="warm")
+        warm_out = keep.tile([P, 1], F32, name="warm_out")
+        nc.vector.memset(warm[:], 1.0)
+        nc.scalar.activation(warm_out[:], warm[:], ACT.Abs_reciprocal_sqrt, bias=1.0)
+
+        tab2_sc = placed("tab2_sc", [P, T2], U8)
+        nc.vector.memset(tab2_sc[:].bitcast(I32), 0)
+        load_packed_scales(nc.scalar, tab2_sc, tab2_scales, 0)
+        v_sc = keep.tile([P, 2, S], U8, name="v_sc", align_bytes=64)
+        nc.vector.memset(v_sc[:].rearrange("p a c -> p (a c)").bitcast(I32), 0)
+
+        v_sc_packed = keep.tile([P, S], U8, name="v_sc_packed", align_bytes=64)
+        nc.vector.tensor_copy(out=v_sc_packed[:], in_=tab_sc[:].indirect(offs_sb[:]))
+        for a in range(2):
+            nc.scalar.dma_start(out=v_sc[0:100, a, :].bitcast(I32),
+                                in_=v_sc_packed[24 + 4 * a : 124 + 4 * a, :].bitcast(I32))
+
+        tab2_w = placed("tab2_w", [P, 2, T2], U32)
+        nc.sync.dma_start(out=tab2_w[:].bitcast(I32), in_=tab2_words.rearrange("a p t i -> p a (t i)").bitcast(I32))
+
+        v_w0 = keep.tile([P, S], U32, name="v_w0", align_bytes=64)
+        nc.vector.tensor_copy(out=v_w0[:], in_=tab_w[0][:].indirect(offs_sb[:]))
+        w2_load(0, 0)
+
+        w1_w = placed("w1_w", [P, 2, 2 * H], U8)
+        nc.vector.tensor_copy(
+            out=w1_w[:].bitcast(U16).rearrange("p a (h t m) -> p (a h) t m", h=2, t=PACK),
+            in_=w1_raw[:].bitcast(U16).rearrange("p a (h m t) -> p (a h) t m", h=2, t=PACK))
+        w2_load(0, 1)
+
+        w1_sc = placed("w1_sc", [P, 2, H], U8)
+        nc.vector.tensor_copy(
+            out=w1_sc[:].rearrange("p a (h t m) -> p (a h) t m", h=2, t=PACK),
+            in_=w1_sc_raw[:].rearrange("p a (h m t) -> p (a h) t m", h=2, t=PACK))
+        w2_load(1, 0)
+
         v2_sc = placed("v2_sc", [P, M], U8)
         nc.vector.tensor_copy(out=v2_sc[:], in_=tab2_sc[:].indirect(offs2_sb[:]))
-        w2_load(0, 0)
-        v_w.append(placed("v_w1", [P, S], U32))
+        w2_load(1, 1)
+        v_w = {(0, half): v_w0[:, BANK * half : BANK * (half + 1)] for half in range(2)}
+        v_w[1, 0] = placed("v_w10", [P, BANK], U32)[:]
+        v_w[1, 1] = keep.tile([P, BANK], U32, name="v_w11", align_bytes=64)[:]
         for half in range(2):
-            nc.vector.tensor_copy(out=v_w[1][:, BANK * half : BANK * (half + 1)],
+            nc.vector.tensor_copy(out=v_w[1, half],
                                   in_=tab_w[1][:].indirect(offs_sb[:, 32 * half : 32 * (half + 1)]))
-        w2_load(0, 1)
+        w3_sc = placed("w3_sc", [P, N], U8)
+        nc.vector.memset(w3_sc[:].bitcast(I32), 0)
+        load_packed_scales(nc.sync, w3_sc, w3_scales, 0)
+        w3_w = placed("w3_w", [P, 2, N], U32)
+        nc.sync.dma_start(out=w3_w[:].bitcast(I32),
+                          in_=w3_words.rearrange("a p c i -> p a (c i)").bitcast(I32))
 
         X_BANKS = 6
         x_banks = {}
@@ -152,32 +158,30 @@ def tile_list_tract_county_audit_kernel(
                 out=x_banks[i, half][:],
                 lhsT=w1_w[:, a, 2 * P * i : 2 * P * (i + 1)].bitcast(FP4X4),
                 lhsT_scale=w1_sc[:, a, P * i : P * (i + 1)],
-                rhs=v_w[a][:, cols].bitcast(FP8X4), rhs_scale=v_sc[a][:, cols],
+                rhs=v_w[a, half].bitcast(FP8X4), rhs_scale=v_sc[:, a, cols],
                 start=(a == 0), stop=(a == 1))
 
         picked = {}
 
         def x_tile(i):
-            h, t = divmod(i, PACK)
-            x_sb = ring.tile([P, S], F32, name="x_sb", bufs=8)
+            x_sb = ring.tile([P, S], F32, name="x_sb", bufs=6)
             for half in range(2):
                 if (i, half) not in x_banks:
                     x_pass(i, half, 0)
                 x_pass(i, half, 1)
-                nc.scalar.activation(x_sb[:, BANK * half : BANK * (half + 1)], x_banks[i, half][:], ACT.Copy,
-                                     scale=g[:, h, t : t + 1])
+                nc.scalar.copy(out=x_sb[:, BANK * half : BANK * (half + 1)], in_=x_banks[i, half][:])
             picked[i] = keep.tile([P, M], F32, name="picked%d" % i)
             nc.vector.tensor_copy(out=picked[i][:], in_=x_sb[:].indirect(pos_sb[:]))
 
         v2_w = [keep.tile([P, M], U32, name="v2_w%d" % a, align_bytes=64) for a in range(2)]
 
         def gather2(a):
-            nc.vector.tensor_copy(out=v2_w[a][:], in_=tab2_w[a][:].indirect(offs2_sb[:]))
+            nc.vector.tensor_copy(out=v2_w[a][:], in_=tab2_w[:, a, :].indirect(offs2_sb[:]))
 
         w2_bf, w2_w, w2_sc = {}, {}, {}
 
         def w2_round(h, a, copy):
-            bf = ring.tile([P, PACK, P, PACK], BF16, name="w2_bf", bufs=4, align_bytes=64)
+            bf = ring.tile([P, PACK, P, PACK], BF16, name="w2_bf", bufs=3, align_bytes=64)
             dst = bf[:].rearrange("p t m j -> p m j t")
             src = w2_raw[h, a][:].rearrange("p j (m t) -> p m j t", t=PACK)
             copy(out=dst, in_=src)
@@ -190,8 +194,7 @@ def tile_list_tract_county_audit_kernel(
                                   in_=w2_bf[h, a][:].rearrange("p t m j -> p (t m j)"))
 
         e = [keep.tile([P, PACK, M], F32, name="e%d" % h) for h in range(2)]
-        r = [keep.tile([P, PACK, M], F32, name="r%d" % h) for h in range(2)]
-        sq = r
+        sq = {}
         B_BANKS = (6, 7, 4, 5)
 
         def diff_tile(i):
@@ -202,38 +205,45 @@ def tile_list_tract_county_audit_kernel(
                 nc.tensor.matmul_mx(
                     out=b[:], lhsT=w2_w[h, a][:, cols].bitcast(FP8X4), lhsT_scale=w2_sc[h, a][:, cols],
                     rhs=v2_w[a][:].bitcast(FP8X4), rhs_scale=v2_sc[4 * a :, :], start=(a == 0), stop=(a == 1))
-            nc.vector.scalar_tensor_tensor(out=e[h][:, t, :], in0=b[:], scalar=g[:, h, t : t + 1], in1=picked[i][:],
-                                           op0=ALU.mult, op1=ALU.subtract)
-            nc.scalar.activation(sq[h][:, t, :], e[h][:, t, :], ACT.Square, scale=g_inv[:, h, t : t + 1])
+            nc.vector.tensor_tensor(out=e[h][:, t, :], in0=b[:], in1=picked[i][:], op=ALU.subtract)
+            if t == 0:
+                sq[h] = keep.tile([P, PACK, M], F32, name="sq")
+            nc.scalar.activation(sq[h][:, t, :], e[h][:, t, :], ACT.Square)
+
+        r, z_rows, z_bf, z_w, z_sc = {}, {}, {}, {}, {}
 
         def root(h, lo, hi):
-            nc.scalar.activation(r[h][:, :, lo:hi], sq[h][:, :, lo:hi], ACT.Abs_reciprocal_sqrt, bias=1.0)
-
-        z_bf = [keep.tile([P, M, PACK], BF16, name="z_bf%d" % h, align_bytes=64) for h in range(2)]
-        z_w = [keep.tile([P, M], U32, name="z_w%d" % h, align_bytes=64) for h in range(2)]
-        z_sc = [keep.tile([P, M], U8, name="z_sc%d" % h, align_bytes=64) for h in range(2)]
+            r[h, lo] = keep.tile([P, PACK, hi - lo], F32, name="r%d_%d" % (h, lo))
+            nc.scalar.activation(r[h, lo][:], sq[h][:, :, lo:hi], ACT.Abs_reciprocal_sqrt, bias=1.0)
 
         def z_round(h, lo, hi):
-            nc.vector.tensor_tensor(
-                out=z_bf[h][:, lo:hi, :].rearrange("p (u i) t -> p u t i", i=4),
-                in0=e[h][:, :, lo:hi].rearrange("p t (u i) -> p u t i", i=4),
-                in1=r[h][:, :, lo:hi].rearrange("p t (u i) -> p u t i", i=4), op=ALU.mult)
+            z_rows[h, lo] = keep.tile([P, PACK, hi - lo], BF16, name="z_rows%d_%d" % (h, lo), align_bytes=64)
+            for t in range(PACK):
+                nc.vector.scalar_tensor_tensor(
+                    out=z_rows[h, lo][:, t, :], in0=e[h][:, t, lo:hi], scalar=g[:, h, t : t + 1],
+                    in1=r[h, lo][:, t, :], op0=ALU.mult, op1=ALU.mult)
+
+        def z_weave(h, lo, hi):
+            z_bf[h, lo] = keep.tile([P, hi - lo, PACK], BF16, name="z_bf%d_%d" % (h, lo), align_bytes=64)
+            nc.vector.tensor_copy(out=z_bf[h, lo][:], in_=z_rows[h, lo][:].rearrange("p t m -> p m t"))
 
         def z_quantize(h, lo, hi):
-            nc.vector.quantize_mx(out=z_w[h][:, lo:hi].bitcast(FP8X4), scales=z_sc[h][:, lo:hi],
-                                  in_=z_bf[h][:, lo:hi, :].rearrange("p m t -> p (m t)"))
+            z_w[h, lo] = keep.tile([P, hi - lo], U32, name="z_w%d_%d" % (h, lo), align_bytes=64)
+            z_sc[h, lo] = keep.tile([P, hi - lo], U8, name="z_sc%d_%d" % (h, lo), align_bytes=64)
+            nc.vector.quantize_mx(out=z_w[h, lo][:].bitcast(FP8X4), scales=z_sc[h, lo][:],
+                                  in_=z_bf[h, lo][:].rearrange("p m t -> p (m t)"))
 
         out_banks = {}
 
         def out_pass(c, h):
             if h == 0:
                 out_banks[c] = bank(c, [P, N // P, CHUNK])
-            cols = slice(CHUNK * c, CHUNK * (c + 1))
+            piece, cols = ((0, 0), slice(CHUNK * c, CHUNK * (c + 1))) if h == 0 else ((1, CHUNK * c), slice(0, CHUNK))
             for n in range(N // P):
                 nc.tensor.matmul_mx(
                     out=out_banks[c][:, n, :], lhsT=w3_w[:, h, P * n : P * (n + 1)].bitcast(FP8X4),
                     lhsT_scale=w3_sc[4 * h :, P * n : P * (n + 1)],
-                    rhs=z_w[h][:, cols].bitcast(FP8X4), rhs_scale=z_sc[h][:, cols],
+                    rhs=z_w[piece][:, cols].bitcast(FP8X4), rhs_scale=z_sc[piece][:, cols],
                     start=(h == 0 and n == 0), stop=(h == 1 and n == N // P - 1))
 
         def store(c):
@@ -245,12 +255,10 @@ def tile_list_tract_county_audit_kernel(
             for half in range(2):
                 x_pass(i, half, 0)
         x_tile(0)
-        gather2(0)
-        w2_load(1, 0)
         x_tile(1)
+        gather2(0)
         x_tile(2)
         gather2(1)
-        w2_load(1, 1)
         x_tile(3)
         x_tile(4)
         w2_round(0, 0, nc.scalar.copy)
@@ -259,9 +267,6 @@ def tile_list_tract_county_audit_kernel(
         x_tile(7)
         w2_quantize(0, 0)
         w2_round(0, 1, nc.scalar.copy)
-        w3_w = placed("w3_w", [P, 2, N], U32)
-        nc.sync.dma_start(out=w3_w[:].bitcast(I32),
-                          in_=w3_words.rearrange("a p c i -> p a (c i)").bitcast(I32))
         w2_round(1, 0, nc.vector.tensor_copy)
         w2_round(1, 1, nc.scalar.copy)
         w2_quantize(0, 1)
@@ -269,22 +274,25 @@ def tile_list_tract_county_audit_kernel(
         for t in range(PACK):
             diff_tile(t)
         w2_quantize(1, 1)
-        for half in range(2):
-            root(0, half * M // 2, (half + 1) * M // 2)
+        root(0, 0, M)
         for t in range(PACK):
             diff_tile(PACK + t)
         chunks = M // CHUNK
         for c in range(chunks):
             root(1, CHUNK * c, CHUNK * (c + 1))
-        for half in range(2):
-            z_round(0, half * M // 2, (half + 1) * M // 2)
+        z_round(0, 0, M)
+        z_weave(0, 0, M)
         z_round(1, 0, CHUNK)
         z_quantize(0, 0, M)
         for c in range(chunks):
             out_pass(c, 0)
-        for c in range(1, chunks + 1):
-            if c < chunks:
-                z_round(1, CHUNK * c, CHUNK * (c + 1))
-            z_quantize(1, CHUNK * (c - 1), CHUNK * c)
-            out_pass(c - 1, 1)
-            store(c - 1)
+        for step in range(1, chunks + 2):
+            if step <= chunks:
+                z_weave(1, CHUNK * (step - 1), CHUNK * step)
+            if step < chunks:
+                z_round(1, CHUNK * step, CHUNK * (step + 1))
+            if step >= 2:
+                c = step - 2
+                z_quantize(1, CHUNK * c, CHUNK * (c + 1))
+                out_pass(c, 1)
+                store(c)

@@ -22,12 +22,13 @@ PASS = 512
 BANK = 512
 CHUNK = 128
 KIB = 1024
+LIVE = 96
 PLACE = {
-    "w2_raw11": 0, "tab2_sc": 8 * KIB - 64, "v_w10": 8 * KIB, "tab_sc": 10 * KIB, "tab2_w": 10 * KIB,
-    "tab_w0": 26 * KIB, "w1_w": 26 * KIB, "w2_raw00": 30 * KIB,
-    "w1_raw": 42 * KIB, "w1_sc": 42 * KIB, "w2_raw01": 44 * KIB,
-    "w1_sc_raw": 52 * KIB, "v2_sc": 52 * KIB, "w2_raw10": 53 * KIB,
-    "tab_w1": 61 * KIB, "w3_w": 61 * KIB, "w3_sc": 65 * KIB,
+    "tab_sc": 0, "rows": 0, "w1_sc_raw": 4 * KIB, "g": 4 * KIB,
+    "w2_raw00": 8 * KIB + 64, "tab_w0": 16 * KIB, "tab2_w": 16 * KIB + 64,
+    "w2_raw01": 33 * KIB + 64, "tab_w1": 41 * KIB, "w2_raw10": 41 * KIB + 64, "w3_w": 49 * KIB + 64,
+    "w2_raw11": 57 * KIB - 64,
+    "sq0": 8 * KIB + 64, "sq1": 41 * KIB + 64, "r0": 16 * KIB + 64, "r1": 24 * KIB + 64,
 }
 
 
@@ -75,103 +76,104 @@ def tile_list_tract_county_audit_kernel(
         offs2_sb = lists.tile([P, M // 16], U16, name="offs2_sb")
         pos_sb = lists.tile([P, M // 16], U16, name="pos_sb")
         tab_sc = placed("tab_sc", [P, T], U8)
-        w1_raw = placed("w1_raw", [P, 2, 2 * H], U8)
+        w1_sc_raw = placed("w1_sc_raw", [P, H], U8)
+        w1_raw = keep.tile([P, 2, 2 * H], U8, name="w1_raw", align_bytes=64)
         nc.sync.dma_start(offs_sb[:], offs)
-        load_packed_scales(nc.sync, tab_sc, tab_scales, 24)
-        tab_w = [load_words(0)]
-        nc.sync.dma_start(offs2_sb[:], offs2)
+        nc.sync.dma_start(out=tab_sc[LIVE:, :].bitcast(I32), in_=tab_scales.bitcast(I32).rearrange("a q c -> (a q) c"))
+        nc.sync.dma_start(out=w1_sc_raw[LIVE:, :].bitcast(I32), in_=w1_scales.bitcast(I32).rearrange("a q c -> (a q) c"))
         nc.sync.dma_start(pos_sb[:], pos1)
+        nc.sync.dma_start(offs2_sb[:], offs2)
         nc.sync.dma_start(out=w1_raw[:].bitcast(I32), in_=w1_words.bitcast(I32).rearrange("a p c -> p a c"))
-        tab_w.append(load_words(1))
+        tab_w = [load_words(0), load_words(1)]
 
-        w1_sc_raw = placed("w1_sc_raw", [P, 2, H], U8)
-        nc.gpsimd.memset(w1_sc_raw[:].rearrange("p a c -> p (a c)").bitcast(I32), 0)
-        for q in range(4):
-            engine = nc.gpsimd if q == 3 else nc.vector
-            engine.memset(tab_sc[32 * q : 32 * q + 24, :].bitcast(I32), 0)
-        for q in range(4):
-            nc.gpsimd.dma_start(out=w1_sc_raw[32 * q : 32 * q + 4, :, :].bitcast(I32),
-                                in_=w1_scales.bitcast(I32)[:, 4 * q : 4 * q + 4, :].rearrange("a r c -> r a c"))
-        g = keep.tile([P, 2, PACK], F32, name="g")
-        nc.gpsimd.dma_start(out=g[:], in_=gain.rearrange("(a p t) -> p a t", a=2, t=PACK))
-
+        nc.vector.memset(tab_sc[:LIVE, :].bitcast(I32), 0)
+        nc.vector.memset(w1_sc_raw[:LIVE, :].bitcast(I32), 0)
         warm = keep.tile([P, 1], F32, name="warm")
         warm_out = keep.tile([P, 1], F32, name="warm_out")
         nc.vector.memset(warm[:], 1.0)
         nc.scalar.activation(warm_out[:], warm[:], ACT.Abs_reciprocal_sqrt, bias=1.0)
+        planes = keep.tile([P, 2, S + H], U8, name="planes", align_bytes=64)
+        nc.vector.memset(planes[:].rearrange("p a c -> p (a c)").bitcast(I32), 0)
 
-        tab2_sc = placed("tab2_sc", [P, T2], U8)
-        nc.vector.memset(tab2_sc[:].bitcast(I32), 0)
-        load_packed_scales(nc.scalar, tab2_sc, tab2_scales, 0)
-        v_sc = keep.tile([P, 2, S], U8, name="v_sc", align_bytes=64)
-        nc.vector.memset(v_sc[:].rearrange("p a c -> p (a c)").bitcast(I32), 0)
+        tab2_sc = keep.tile([P, T2], U8, name="tab2_sc", align_bytes=64)
+        nc.gpsimd.memset(tab2_sc[:].bitcast(I32), 0)
+        load_packed_scales(nc.gpsimd, tab2_sc, tab2_scales, 0)
 
-        v_sc_packed = keep.tile([P, S], U8, name="v_sc_packed", align_bytes=64)
-        nc.vector.tensor_copy(out=v_sc_packed[:], in_=tab_sc[:].indirect(offs_sb[:]))
+        v_sc_rows = keep.tile([P, S], U8, name="v_sc_rows", align_bytes=64)
+        nc.vector.tensor_copy(out=v_sc_rows[:], in_=tab_sc[:].indirect(offs_sb[:]))
+        rows = placed("rows", [P, S + H], U8)
+        nc.vector.tensor_copy(out=rows[LIVE:, :S].bitcast(I32), in_=v_sc_rows[LIVE:, :].bitcast(I32))
+        nc.vector.tensor_copy(
+            out=rows[:, S:].rearrange("p (h t m) -> p h t m", h=2, t=PACK),
+            in_=w1_sc_raw[:].rearrange("p (h m t) -> p h t m", h=2, t=PACK))
         for a in range(2):
-            nc.scalar.dma_start(out=v_sc[0:100, a, :].bitcast(I32),
-                                in_=v_sc_packed[24 + 4 * a : 124 + 4 * a, :].bitcast(I32))
+            for q in range(4):
+                queue = nc.gpsimd if (a, q) == (1, 3) else nc.scalar
+                first = LIVE + 16 * a + 4 * q
+                queue.dma_start(out=planes[32 * q : 32 * q + 4, a, :].bitcast(I32),
+                                in_=rows[first : first + 4, :].bitcast(I32))
+        g = placed("g", [P, 2, PACK], F32)
+        nc.scalar.dma_start(out=g[:], in_=gain.rearrange("(a p t) -> p a t", a=2, t=PACK))
 
-        tab2_w = placed("tab2_w", [P, 2, T2], U32)
-        nc.sync.dma_start(out=tab2_w[:].bitcast(I32), in_=tab2_words.rearrange("a p t i -> p a (t i)").bitcast(I32))
+        w3_sc = keep.tile([P, N], U8, name="w3_sc", align_bytes=64)
+        nc.gpsimd.memset(w3_sc[:].bitcast(I32), 0)
+        load_packed_scales(nc.gpsimd, w3_sc, w3_scales, 0)
 
-        v_w0 = keep.tile([P, S], U32, name="v_w0", align_bytes=64)
-        nc.vector.tensor_copy(out=v_w0[:], in_=tab_w[0][:].indirect(offs_sb[:]))
-        w2_load(0, 0)
-
-        w1_w = placed("w1_w", [P, 2, 2 * H], U8)
+        w1_w = keep.tile([P, 2, 2 * H], U8, name="w1_w", align_bytes=64)
         nc.vector.tensor_copy(
             out=w1_w[:].bitcast(U16).rearrange("p a (h t m) -> p (a h) t m", h=2, t=PACK),
             in_=w1_raw[:].bitcast(U16).rearrange("p a (h m t) -> p (a h) t m", h=2, t=PACK))
-        w2_load(0, 1)
 
-        w1_sc = placed("w1_sc", [P, 2, H], U8)
-        nc.vector.tensor_copy(
-            out=w1_sc[:].rearrange("p a (h t m) -> p (a h) t m", h=2, t=PACK),
-            in_=w1_sc_raw[:].rearrange("p a (h m t) -> p (a h) t m", h=2, t=PACK))
-        w2_load(1, 0)
+        v_w = {}
 
-        v2_sc = placed("v2_sc", [P, M], U8)
+        def gather1(a, half):
+            v_w[a, half] = keep.tile([P, BANK], U32, name="v_w%d%d" % (a, half), align_bytes=64)
+            nc.vector.tensor_copy(out=v_w[a, half][:],
+                                  in_=tab_w[a][:].indirect(offs_sb[:, 32 * half : 32 * (half + 1)]))
+
+        gather1(0, 0)
+        gather1(0, 1)
+        tab2_w = placed("tab2_w", [P, 2, T2], U32)
+        nc.sync.dma_start(out=tab2_w[:].bitcast(I32), in_=tab2_words.rearrange("a p t i -> p a (t i)").bitcast(I32))
+        w2_load(0, 0)
+        v2_sc = keep.tile([P, M], U8, name="v2_sc", align_bytes=64)
         nc.vector.tensor_copy(out=v2_sc[:], in_=tab2_sc[:].indirect(offs2_sb[:]))
+        gather1(1, 0)
+        gather1(1, 1)
+        w2_load(0, 1)
+        w2_load(1, 0)
         w2_load(1, 1)
-        v_w = {(0, half): v_w0[:, BANK * half : BANK * (half + 1)] for half in range(2)}
-        v_w[1, 0] = placed("v_w10", [P, BANK], U32)[:]
-        v_w[1, 1] = keep.tile([P, BANK], U32, name="v_w11", align_bytes=64)[:]
-        for half in range(2):
-            nc.vector.tensor_copy(out=v_w[1, half],
-                                  in_=tab_w[1][:].indirect(offs_sb[:, 32 * half : 32 * (half + 1)]))
-        w3_sc = placed("w3_sc", [P, N], U8)
-        nc.vector.memset(w3_sc[:].bitcast(I32), 0)
-        load_packed_scales(nc.sync, w3_sc, w3_scales, 0)
         w3_w = placed("w3_w", [P, 2, N], U32)
         nc.sync.dma_start(out=w3_w[:].bitcast(I32),
                           in_=w3_words.rearrange("a p c i -> p a (c i)").bitcast(I32))
 
-        X_BANKS = 6
+        X_BANKS = 8
         x_banks = {}
+        x_sb = [keep.tile([P, S], F32, name="x_sb%d" % i) for i in range(2 * PACK)]
 
         def x_pass(i, half, a):
             if a == 0:
                 x_banks[i, half] = bank((2 * i + half) % X_BANKS, [P, BANK])
-            cols = slice(BANK * half, BANK * (half + 1))
             nc.tensor.matmul_mx(
                 out=x_banks[i, half][:],
                 lhsT=w1_w[:, a, 2 * P * i : 2 * P * (i + 1)].bitcast(FP4X4),
-                lhsT_scale=w1_sc[:, a, P * i : P * (i + 1)],
-                rhs=v_w[a, half].bitcast(FP8X4), rhs_scale=v_sc[:, a, cols],
+                lhsT_scale=planes[:, a, S + P * i : S + P * (i + 1)],
+                rhs=v_w[a, half][:].bitcast(FP8X4), rhs_scale=planes[:, a, BANK * half : BANK * (half + 1)],
                 start=(a == 0), stop=(a == 1))
+
+        def x_copy(i, half, copy):
+            copy(out=x_sb[i][:, BANK * half : BANK * (half + 1)], in_=x_banks[i, half][:])
 
         picked = {}
 
         def x_tile(i):
-            x_sb = ring.tile([P, S], F32, name="x_sb", bufs=6)
             for half in range(2):
-                if (i, half) not in x_banks:
+                if i >= PACK:
                     x_pass(i, half, 0)
-                x_pass(i, half, 1)
-                nc.scalar.copy(out=x_sb[:, BANK * half : BANK * (half + 1)], in_=x_banks[i, half][:])
+                    x_pass(i, half, 1)
+                x_copy(i, half, nc.vector.tensor_copy if (i, half) == (0, 1) else nc.scalar.copy)
             picked[i] = keep.tile([P, M], F32, name="picked%d" % i)
-            nc.vector.tensor_copy(out=picked[i][:], in_=x_sb[:].indirect(pos_sb[:]))
+            nc.vector.tensor_copy(out=picked[i][:], in_=x_sb[i][:].indirect(pos_sb[:]))
 
         v2_w = [keep.tile([P, M], U32, name="v2_w%d" % a, align_bytes=64) for a in range(2)]
 
@@ -181,7 +183,7 @@ def tile_list_tract_county_audit_kernel(
         w2_bf, w2_w, w2_sc = {}, {}, {}
 
         def w2_round(h, a, copy):
-            bf = ring.tile([P, PACK, P, PACK], BF16, name="w2_bf", bufs=3, align_bytes=64)
+            bf = ring.tile([P, PACK, P, PACK], BF16, name="w2_bf", bufs=4, align_bytes=64)
             dst = bf[:].rearrange("p t m j -> p m j t")
             src = w2_raw[h, a][:].rearrange("p j (m t) -> p m j t", t=PACK)
             copy(out=dst, in_=src)
@@ -195,11 +197,10 @@ def tile_list_tract_county_audit_kernel(
 
         e = [keep.tile([P, PACK, M], F32, name="e%d" % h) for h in range(2)]
         sq = {}
-        B_BANKS = (6, 7, 4, 5)
 
         def diff_tile(i):
             h, t = divmod(i, PACK)
-            b = bank(B_BANKS[t], [P, M])
+            b = bank(i, [P, M])
             cols = slice(P * t, P * (t + 1))
             for a in range(2):
                 nc.tensor.matmul_mx(
@@ -207,13 +208,14 @@ def tile_list_tract_county_audit_kernel(
                     rhs=v2_w[a][:].bitcast(FP8X4), rhs_scale=v2_sc[4 * a :, :], start=(a == 0), stop=(a == 1))
             nc.vector.tensor_tensor(out=e[h][:, t, :], in0=b[:], in1=picked[i][:], op=ALU.subtract)
             if t == 0:
-                sq[h] = keep.tile([P, PACK, M], F32, name="sq")
+                sq[h] = placed("sq%d" % h, [P, PACK, M], F32)
             nc.scalar.activation(sq[h][:, t, :], e[h][:, t, :], ACT.Square)
 
         r, z_rows, z_bf, z_w, z_sc = {}, {}, {}, {}, {}
 
         def root(h, lo, hi):
-            r[h, lo] = keep.tile([P, PACK, hi - lo], F32, name="r%d_%d" % (h, lo))
+            r[h, lo] = stage.tile([P, PACK, hi - lo], F32, name="r%d_%d" % (h, lo), align_bytes=64,
+                                  offset=PLACE["r%d" % h] + 4 * PACK * lo)
             nc.scalar.activation(r[h, lo][:], sq[h][:, :, lo:hi], ACT.Abs_reciprocal_sqrt, bias=1.0)
 
         def z_round(h, lo, hi):
@@ -251,24 +253,19 @@ def tile_list_tract_county_audit_kernel(
             nc.scalar.copy(out=res[:], in_=out_banks[c][:])
             nc.sync.dma_start(out=out[:, CHUNK * c : CHUNK * (c + 1)].rearrange("(n p) m -> p n m", p=P), in_=res[:])
 
-        for i in range(X_BANKS // 2):
+        for a in range(2):
             for half in range(2):
-                x_pass(i, half, 0)
-        x_tile(0)
-        x_tile(1)
+                for i in range(PACK):
+                    x_pass(i, half, a)
+        for i in range(2 * PACK):
+            x_tile(i)
         gather2(0)
-        x_tile(2)
         gather2(1)
-        x_tile(3)
-        x_tile(4)
         w2_round(0, 0, nc.scalar.copy)
-        x_tile(5)
-        x_tile(6)
-        x_tile(7)
-        w2_quantize(0, 0)
-        w2_round(0, 1, nc.scalar.copy)
-        w2_round(1, 0, nc.vector.tensor_copy)
+        w2_round(0, 1, nc.vector.tensor_copy)
+        w2_round(1, 0, nc.scalar.copy)
         w2_round(1, 1, nc.scalar.copy)
+        w2_quantize(0, 0)
         w2_quantize(0, 1)
         w2_quantize(1, 0)
         for t in range(PACK):

@@ -186,7 +186,8 @@ def tile_list_tract_county_audit_kernel(
             bf = ring.tile([P, PACK, P, PACK], BF16, name="w2_bf", bufs=4, align_bytes=64)
             dst = bf[:].rearrange("p t m j -> p m j t")
             src = w2_raw[h, a][:].rearrange("p j (m t) -> p m j t", t=PACK)
-            copy(out=dst, in_=src)
+            for t in range(0, PACK, 2):
+                copy(out=dst[:, :, :, t : t + 2], in_=src[:, :, :, t : t + 2])
             w2_bf[h, a] = bf
 
         def w2_quantize(h, a):
@@ -227,7 +228,8 @@ def tile_list_tract_county_audit_kernel(
 
         def z_weave(h, lo, hi):
             z_bf[h, lo] = keep.tile([P, hi - lo, PACK], BF16, name="z_bf%d_%d" % (h, lo), align_bytes=64)
-            nc.vector.tensor_copy(out=z_bf[h, lo][:], in_=z_rows[h, lo][:].rearrange("p t m -> p m t"))
+            nc.vector.tensor_copy(out=z_bf[h, lo][:].rearrange("p (c i) t -> p c t i", i=PACK),
+                                  in_=z_rows[h, lo][:].rearrange("p t (c i) -> p c t i", i=PACK))
 
         def z_quantize(h, lo, hi):
             z_w[h, lo] = keep.tile([P, hi - lo], U32, name="z_w%d_%d" % (h, lo), align_bytes=64)

@@ -22,11 +22,13 @@ PASS = 512
 BANK = 512
 CHUNK = 128
 KIB = 1024
-LIVE = 96
+LIVE = 32
 PLACE = {
-    "tab_sc": 0, "rows": 0, "w1_sc_raw": 4 * KIB, "g": 4 * KIB,
+    "v2_sc_rows": 0, "g": 0,
     "w2_raw00": 8 * KIB + 64, "tab_w0": 16 * KIB, "tab2_w": 16 * KIB + 64,
     "w2_raw01": 33 * KIB + 64, "tab_w1": 41 * KIB, "w2_raw10": 41 * KIB + 64, "w3_w": 49 * KIB + 64,
+    "x_sb": 66 * KIB, "w2_bf00": 78 * KIB, "v2_w0": 82 * KIB, "v2_w1": 84 * KIB,
+    "w2_bf01": 24 * KIB + 64, "w2_bf10": 16 * KIB + 64, "w2_bf11": 20 * KIB + 64,
     "w2_raw11": 57 * KIB - 64,
     "sq0": 8 * KIB + 64, "sq1": 41 * KIB + 64, "r0": 16 * KIB + 64, "r1": 24 * KIB + 64,
 }
@@ -41,7 +43,6 @@ def tile_list_tract_county_audit_kernel(
         lists = ctx.enter_context(tc.tile_pool(name="lists", bufs=1))
         keep = ctx.enter_context(tc.tile_pool(name="keep", bufs=1))
         stage = ctx.enter_context(tc.tile_pool(name="stage", bufs=1))
-        ring = ctx.enter_context(tc.tile_pool(name="ring", bufs=3))
         psum = ctx.enter_context(tc.psum_pool(name="psum", bufs=1))
 
         def placed(name, shape, dtype):
@@ -52,11 +53,6 @@ def tile_list_tract_county_audit_kernel(
 
         def words(dram, a):
             return dram[a].rearrange("p t i -> p (t i)").bitcast(I32)
-
-        def load_packed_scales(queue, plane, dram, row):
-            for q in range(4):
-                queue.dma_start(out=plane[32 * q + row : 32 * q + row + 8, :].bitcast(I32),
-                                in_=dram.bitcast(I32)[:, 4 * q : 4 * q + 4, :])
 
         def load_words(a):
             tile = placed("tab_w%d" % a, [P, T], U32)
@@ -75,49 +71,55 @@ def tile_list_tract_county_audit_kernel(
         offs_sb = lists.tile([P, S // 16], U16, name="offs_sb")
         offs2_sb = lists.tile([P, M // 16], U16, name="offs2_sb")
         pos_sb = lists.tile([P, M // 16], U16, name="pos_sb")
-        tab_sc = placed("tab_sc", [P, T], U8)
-        w1_sc_raw = placed("w1_sc_raw", [P, H], U8)
+        tab_sc = keep.tile([P, T], U8, name="tab_sc", align_bytes=64)
+        tab2_sc = keep.tile([P, T2], U8, name="tab2_sc", align_bytes=64)
+        w1_sc_raw = keep.tile([P, H], U8, name="w1_sc_raw", align_bytes=64)
         w1_raw = keep.tile([P, 2, 2 * H], U8, name="w1_raw", align_bytes=64)
-        nc.sync.dma_start(offs_sb[:], offs)
-        nc.sync.dma_start(out=tab_sc[LIVE:, :].bitcast(I32), in_=tab_scales.bitcast(I32).rearrange("a q c -> (a q) c"))
-        nc.sync.dma_start(out=w1_sc_raw[LIVE:, :].bitcast(I32), in_=w1_scales.bitcast(I32).rearrange("a q c -> (a q) c"))
-        nc.sync.dma_start(pos_sb[:], pos1)
-        nc.sync.dma_start(offs2_sb[:], offs2)
-        nc.sync.dma_start(out=w1_raw[:].bitcast(I32), in_=w1_words.bitcast(I32).rearrange("a p c -> p a c"))
-        tab_w = [load_words(0), load_words(1)]
+        planes = [keep.tile([P, S + H + M + N], U8, name="plane%d" % a, align_bytes=64) for a in range(2)]
+        V1, W1, V2, W3 = 0, S, S + H, S + H + M
 
-        nc.vector.memset(tab_sc[:LIVE, :].bitcast(I32), 0)
-        nc.vector.memset(w1_sc_raw[:LIVE, :].bitcast(I32), 0)
+        def load_rows(rows, dram):
+            nc.sync.dma_start(out=rows.bitcast(I32), in_=dram.bitcast(I32).rearrange("a q c -> (a q) c"))
+
+        nc.sync.dma_start(offs_sb[:], offs)
+        load_rows(tab_sc[:LIVE, :], tab_scales)
+        load_rows(w1_sc_raw[:LIVE, :], w1_scales)
+        nc.sync.dma_start(offs2_sb[:], offs2)
+        load_rows(tab2_sc[:LIVE, :], tab2_scales)
+        load_rows(planes[0][:LIVE, W3:], w3_scales)
+        nc.sync.dma_start(out=w1_raw[:].bitcast(I32), in_=w1_words.bitcast(I32).rearrange("a p c -> p a c"))
+        tab_w = [load_words(0)]
+        nc.sync.dma_start(pos_sb[:], pos1)
+        tab_w.append(load_words(1))
+
+        def clear_dead_rows(tile):
+            nc.vector.memset(tile[32:64, :].bitcast(I32), 0)
+            nc.vector.memset(tile[64:, :].bitcast(I32), 0)
+
+        clear_dead_rows(tab_sc)
         warm = keep.tile([P, 1], F32, name="warm")
         warm_out = keep.tile([P, 1], F32, name="warm_out")
         nc.vector.memset(warm[:], 1.0)
         nc.scalar.activation(warm_out[:], warm[:], ACT.Abs_reciprocal_sqrt, bias=1.0)
-        planes = keep.tile([P, 2, S + H], U8, name="planes", align_bytes=64)
-        nc.vector.memset(planes[:].rearrange("p a c -> p (a c)").bitcast(I32), 0)
-
-        tab2_sc = keep.tile([P, T2], U8, name="tab2_sc", align_bytes=64)
-        nc.gpsimd.memset(tab2_sc[:].bitcast(I32), 0)
-        load_packed_scales(nc.gpsimd, tab2_sc, tab2_scales, 0)
+        for tile in (w1_sc_raw, tab2_sc, planes[0][:, W3:]):
+            clear_dead_rows(tile)
+        nc.vector.memset(planes[1][:].bitcast(I32), 0)
 
         v_sc_rows = keep.tile([P, S], U8, name="v_sc_rows", align_bytes=64)
         nc.vector.tensor_copy(out=v_sc_rows[:], in_=tab_sc[:].indirect(offs_sb[:]))
-        rows = placed("rows", [P, S + H], U8)
-        nc.vector.tensor_copy(out=rows[LIVE:, :S].bitcast(I32), in_=v_sc_rows[LIVE:, :].bitcast(I32))
         nc.vector.tensor_copy(
-            out=rows[:, S:].rearrange("p (h t m) -> p h t m", h=2, t=PACK),
+            out=planes[0][:, W1:V2].rearrange("p (h t m) -> p h t m", h=2, t=PACK),
             in_=w1_sc_raw[:].rearrange("p (h m t) -> p h t m", h=2, t=PACK))
-        for a in range(2):
-            for q in range(4):
-                queue = nc.gpsimd if (a, q) == (1, 3) else nc.scalar
-                first = LIVE + 16 * a + 4 * q
-                queue.dma_start(out=planes[32 * q : 32 * q + 4, a, :].bitcast(I32),
-                                in_=rows[first : first + 4, :].bitcast(I32))
+        nc.vector.tensor_copy(out=planes[0][:, V1:W1].bitcast(I32), in_=v_sc_rows[:].bitcast(I32))
+        v2_sc_rows = placed("v2_sc_rows", [P, M], U8)
+        nc.vector.tensor_copy(out=v2_sc_rows[:], in_=tab2_sc[:].indirect(offs2_sb[:]))
+        nc.vector.tensor_copy(out=planes[0][:, V2:W3].bitcast(I32), in_=v2_sc_rows[:].bitcast(I32))
+        for group in range(1, 8):
+            a, q = divmod(group, 4)
+            nc.scalar.dma_start(out=planes[a][32 * q : 32 * q + 4, :].bitcast(I32),
+                                in_=planes[0][4 * group : 4 * group + 4, :].bitcast(I32))
         g = placed("g", [P, 2, PACK], F32)
         nc.scalar.dma_start(out=g[:], in_=gain.rearrange("(a p t) -> p a t", a=2, t=PACK))
-
-        w3_sc = keep.tile([P, N], U8, name="w3_sc", align_bytes=64)
-        nc.gpsimd.memset(w3_sc[:].bitcast(I32), 0)
-        load_packed_scales(nc.gpsimd, w3_sc, w3_scales, 0)
 
         w1_w = keep.tile([P, 2, 2 * H], U8, name="w1_w", align_bytes=64)
         nc.vector.tensor_copy(
@@ -136,8 +138,6 @@ def tile_list_tract_county_audit_kernel(
         tab2_w = placed("tab2_w", [P, 2, T2], U32)
         nc.sync.dma_start(out=tab2_w[:].bitcast(I32), in_=tab2_words.rearrange("a p t i -> p a (t i)").bitcast(I32))
         w2_load(0, 0)
-        v2_sc = keep.tile([P, M], U8, name="v2_sc", align_bytes=64)
-        nc.vector.tensor_copy(out=v2_sc[:], in_=tab2_sc[:].indirect(offs2_sb[:]))
         gather1(1, 0)
         gather1(1, 1)
         w2_load(0, 1)
@@ -149,7 +149,8 @@ def tile_list_tract_county_audit_kernel(
 
         X_BANKS = 8
         x_banks = {}
-        x_sb = [keep.tile([P, S], F32, name="x_sb%d" % i) for i in range(2 * PACK)]
+        x_sb = [stage.tile([P, S], F32, name="x_sb%d" % i, align_bytes=64, offset=PLACE["x_sb"] + 4 * S * i)
+                for i in range(2 * PACK)]
 
         def x_pass(i, half, a):
             if a == 0:
@@ -157,8 +158,8 @@ def tile_list_tract_county_audit_kernel(
             nc.tensor.matmul_mx(
                 out=x_banks[i, half][:],
                 lhsT=w1_w[:, a, 2 * P * i : 2 * P * (i + 1)].bitcast(FP4X4),
-                lhsT_scale=planes[:, a, S + P * i : S + P * (i + 1)],
-                rhs=v_w[a, half][:].bitcast(FP8X4), rhs_scale=planes[:, a, BANK * half : BANK * (half + 1)],
+                lhsT_scale=planes[a][:, W1 + P * i : W1 + P * (i + 1)],
+                rhs=v_w[a, half][:].bitcast(FP8X4), rhs_scale=planes[a][:, BANK * half : BANK * (half + 1)],
                 start=(a == 0), stop=(a == 1))
 
         def x_copy(i, half, copy):
@@ -175,15 +176,16 @@ def tile_list_tract_county_audit_kernel(
             picked[i] = keep.tile([P, M], F32, name="picked%d" % i)
             nc.vector.tensor_copy(out=picked[i][:], in_=x_sb[i][:].indirect(pos_sb[:]))
 
-        v2_w = [keep.tile([P, M], U32, name="v2_w%d" % a, align_bytes=64) for a in range(2)]
+        v2_w = {}
 
         def gather2(a):
+            v2_w[a] = placed("v2_w%d" % a, [P, M], U32)
             nc.vector.tensor_copy(out=v2_w[a][:], in_=tab2_w[:, a, :].indirect(offs2_sb[:]))
 
         w2_bf, w2_w, w2_sc = {}, {}, {}
 
         def w2_round(h, a, copy):
-            bf = ring.tile([P, PACK, P, PACK], BF16, name="w2_bf", bufs=4, align_bytes=64)
+            bf = placed("w2_bf%d%d" % (h, a), [P, PACK, P, PACK], BF16)
             dst = bf[:].rearrange("p t m j -> p m j t")
             src = w2_raw[h, a][:].rearrange("p j (m t) -> p m j t", t=PACK)
             for t in range(0, PACK, 2):
@@ -199,15 +201,21 @@ def tile_list_tract_county_audit_kernel(
         e = [keep.tile([P, PACK, M], F32, name="e%d" % h) for h in range(2)]
         sq = {}
 
+        b_banks = {}
+
+        def b_passes(h, a):
+            for t in range(PACK):
+                if a == 0:
+                    b_banks[PACK * h + t] = bank(PACK * h + t, [P, M])
+                cols = slice(P * t, P * (t + 1))
+                nc.tensor.matmul_mx(
+                    out=b_banks[PACK * h + t][:],
+                    lhsT=w2_w[h, a][:, cols].bitcast(FP8X4), lhsT_scale=w2_sc[h, a][:, cols],
+                    rhs=v2_w[a][:].bitcast(FP8X4), rhs_scale=planes[a][:, V2:W3], start=(a == 0), stop=(a == 1))
+
         def diff_tile(i):
             h, t = divmod(i, PACK)
-            b = bank(i, [P, M])
-            cols = slice(P * t, P * (t + 1))
-            for a in range(2):
-                nc.tensor.matmul_mx(
-                    out=b[:], lhsT=w2_w[h, a][:, cols].bitcast(FP8X4), lhsT_scale=w2_sc[h, a][:, cols],
-                    rhs=v2_w[a][:].bitcast(FP8X4), rhs_scale=v2_sc[4 * a :, :], start=(a == 0), stop=(a == 1))
-            nc.vector.tensor_tensor(out=e[h][:, t, :], in0=b[:], in1=picked[i][:], op=ALU.subtract)
+            nc.vector.tensor_tensor(out=e[h][:, t, :], in0=b_banks[i][:], in1=picked[i][:], op=ALU.subtract)
             if t == 0:
                 sq[h] = placed("sq%d" % h, [P, PACK, M], F32)
             nc.scalar.activation(sq[h][:, t, :], e[h][:, t, :], ACT.Square)
@@ -246,7 +254,7 @@ def tile_list_tract_county_audit_kernel(
             for n in range(N // P):
                 nc.tensor.matmul_mx(
                     out=out_banks[c][:, n, :], lhsT=w3_w[:, h, P * n : P * (n + 1)].bitcast(FP8X4),
-                    lhsT_scale=w3_sc[4 * h :, P * n : P * (n + 1)],
+                    lhsT_scale=planes[h][:, W3 + P * n : W3 + P * (n + 1)],
                     rhs=z_w[piece][:, cols].bitcast(FP8X4), rhs_scale=z_sc[piece][:, cols],
                     start=(h == 0 and n == 0), stop=(h == 1 and n == N // P - 1))
 
@@ -255,24 +263,33 @@ def tile_list_tract_county_audit_kernel(
             nc.scalar.copy(out=res[:], in_=out_banks[c][:])
             nc.sync.dma_start(out=out[:, CHUNK * c : CHUNK * (c + 1)].rearrange("(n p) m -> p n m", p=P), in_=res[:])
 
-        for a in range(2):
+        for half in range(2):
+            for i in range(PACK):
+                x_pass(i, half, 0)
+        for pair in range(0, PACK, 2):
             for half in range(2):
-                for i in range(PACK):
-                    x_pass(i, half, a)
-        for i in range(2 * PACK):
+                x_pass(pair, half, 1)
+                x_pass(pair + 1, half, 1)
+        for i in range(5):
             x_tile(i)
         gather2(0)
         gather2(1)
         w2_round(0, 0, nc.scalar.copy)
-        w2_round(0, 1, nc.vector.tensor_copy)
-        w2_round(1, 0, nc.scalar.copy)
-        w2_round(1, 1, nc.scalar.copy)
+        w2_round(0, 1, nc.scalar.copy)
         w2_quantize(0, 0)
         w2_quantize(0, 1)
+        for i in range(5, 2 * PACK):
+            x_tile(i)
+        b_passes(0, 0)
+        b_passes(0, 1)
+        w2_round(1, 0, nc.scalar.copy)
+        w2_round(1, 1, nc.scalar.copy)
         w2_quantize(1, 0)
+        b_passes(1, 0)
         for t in range(PACK):
             diff_tile(t)
         w2_quantize(1, 1)
+        b_passes(1, 1)
         root(0, 0, M)
         for t in range(PACK):
             diff_tile(PACK + t)

@@ -25,12 +25,13 @@ KIB = 1024
 LIVE = 32
 PLACE = {
     "v2_sc_rows": 0, "g": 0,
-    "w2_raw00": 8 * KIB + 64, "tab_w0": 16 * KIB, "tab2_w": 16 * KIB + 64,
-    "w2_raw01": 33 * KIB + 64, "tab_w1": 41 * KIB, "w2_raw10": 41 * KIB + 64, "w3_w": 49 * KIB + 64,
-    "x_sb": 66 * KIB, "w2_bf00": 78 * KIB, "v2_w0": 82 * KIB, "v2_w1": 84 * KIB,
-    "w2_bf01": 24 * KIB + 64, "w2_bf10": 16 * KIB + 64, "w2_bf11": 20 * KIB + 64,
-    "w2_raw11": 57 * KIB - 64,
-    "sq0": 8 * KIB + 64, "sq1": 41 * KIB + 64, "r0": 16 * KIB + 64, "r1": 24 * KIB + 64,
+    "w2_raw00_0": 8 * KIB + 64, "tab_w0": 16 * KIB, "tab2_w": 16 * KIB + 64,
+    "w2_raw01_0": 33 * KIB + 64, "tab_w1": 41 * KIB, "w2_raw10_0": 41 * KIB + 64, "w3_w": 66 * KIB,
+    "x_sb": 66 * KIB, "w2_bf00": 86 * KIB, "w2_bf01": 90 * KIB, "v2_w0": 94 * KIB, "v2_w1": 86 * KIB,
+    "w2_bf10": 16 * KIB + 64, "w2_bf11": 90 * KIB,
+    "w2_raw11_0": 57 * KIB - 64, "w2_raw11_64": 49 * KIB + 64,
+    "picked": 98 * KIB, "w2_w00": 114 * KIB, "w2_w01": 116 * KIB, "w2_w10": 100 * KIB, "w2_w11": 102 * KIB,
+    "sq0": 45 * KIB + 64, "sq1": 8 * KIB + 64, "e0": 57 * KIB - 64, "e1": 33 * KIB + 64, "r0": 16 * KIB + 64, "r1": 24 * KIB + 64,
 }
 
 
@@ -61,12 +62,11 @@ def tile_list_tract_county_audit_kernel(
 
         w2_raw = {}
 
-        def w2_load(h, a):
-            tile = placed("w2_raw%d%d" % (h, a), [P, PACK, PASS], F32)
-            nc.sync.dma_start(
-                out=tile[:],
-                in_=w2[PASS * a : PASS * (a + 1), PASS * h : PASS * (h + 1)].rearrange("(p j) c -> p j c", j=PACK))
-            w2_raw[h, a] = tile
+        def w2_load(h, a, lo=0, hi=P):
+            tile = placed("w2_raw%d%d_%d" % (h, a, lo), [P, PACK, PACK * (hi - lo)], F32)
+            cols = slice(PASS * h + PACK * lo, PASS * h + PACK * hi)
+            nc.sync.dma_start(out=tile[:], in_=w2[PASS * a : PASS * (a + 1), cols].rearrange("(p j) c -> p j c", j=PACK))
+            w2_raw[h, a, lo] = tile
 
         offs_sb = lists.tile([P, S // 16], U16, name="offs_sb")
         offs2_sb = lists.tile([P, M // 16], U16, name="offs2_sb")
@@ -142,10 +142,8 @@ def tile_list_tract_county_audit_kernel(
         gather1(1, 1)
         w2_load(0, 1)
         w2_load(1, 0)
-        w2_load(1, 1)
-        w3_w = placed("w3_w", [P, 2, N], U32)
-        nc.sync.dma_start(out=w3_w[:].bitcast(I32),
-                          in_=w3_words.rearrange("a p c i -> p a (c i)").bitcast(I32))
+        w2_load(1, 1, 0, P // 2)
+        w2_load(1, 1, P // 2, P)
 
         X_BANKS = 8
         x_banks = {}
@@ -173,7 +171,8 @@ def tile_list_tract_county_audit_kernel(
                     x_pass(i, half, 0)
                     x_pass(i, half, 1)
                 x_copy(i, half, nc.vector.tensor_copy if (i, half) == (0, 1) else nc.scalar.copy)
-            picked[i] = keep.tile([P, M], F32, name="picked%d" % i)
+            picked[i] = stage.tile([P, M], F32, name="picked%d" % i, align_bytes=64,
+                                   offset=PLACE["picked"] + 4 * M * i)
             nc.vector.tensor_copy(out=picked[i][:], in_=x_sb[i][:].indirect(pos_sb[:]))
 
         v2_w = {}
@@ -184,37 +183,40 @@ def tile_list_tract_county_audit_kernel(
 
         w2_bf, w2_w, w2_sc = {}, {}, {}
 
-        def w2_round(h, a, copy):
-            bf = placed("w2_bf%d%d" % (h, a), [P, PACK, P, PACK], BF16)
-            dst = bf[:].rearrange("p t m j -> p m j t")
-            src = w2_raw[h, a][:].rearrange("p j (m t) -> p m j t", t=PACK)
+        def w2_round(h, a, copy, lo=0, hi=P):
+            if lo == 0:
+                w2_bf[h, a] = placed("w2_bf%d%d" % (h, a), [P, PACK, P, PACK], BF16)
+            dst = w2_bf[h, a][:, :, lo:hi, :].rearrange("p t m j -> p m j t")
+            src = w2_raw[h, a, lo][:].rearrange("p j (m t) -> p m j t", t=PACK)
             for t in range(0, PACK, 2):
                 copy(out=dst[:, :, :, t : t + 2], in_=src[:, :, :, t : t + 2])
-            w2_bf[h, a] = bf
 
         def w2_quantize(h, a):
-            w2_w[h, a] = keep.tile([P, PASS], U32, name="w2_w%d%d" % (h, a), align_bytes=64)
+            w2_w[h, a] = placed("w2_w%d%d" % (h, a), [P, PASS], U32)
             w2_sc[h, a] = keep.tile([P, PASS], U8, name="w2_sc%d%d" % (h, a), align_bytes=64)
             nc.vector.quantize_mx(out=w2_w[h, a][:].bitcast(FP8X4), scales=w2_sc[h, a][:],
                                   in_=w2_bf[h, a][:].rearrange("p t m j -> p (t m j)"))
 
-        e = [keep.tile([P, PACK, M], F32, name="e%d" % h) for h in range(2)]
+        e = {}
         sq = {}
 
         b_banks = {}
 
         def b_passes(h, a):
+            first = a == 0
             for t in range(PACK):
-                if a == 0:
+                if first:
                     b_banks[PACK * h + t] = bank(PACK * h + t, [P, M])
                 cols = slice(P * t, P * (t + 1))
                 nc.tensor.matmul_mx(
                     out=b_banks[PACK * h + t][:],
                     lhsT=w2_w[h, a][:, cols].bitcast(FP8X4), lhsT_scale=w2_sc[h, a][:, cols],
-                    rhs=v2_w[a][:].bitcast(FP8X4), rhs_scale=planes[a][:, V2:W3], start=(a == 0), stop=(a == 1))
+                    rhs=v2_w[a][:].bitcast(FP8X4), rhs_scale=planes[a][:, V2:W3], start=first, stop=not first)
 
         def diff_tile(i):
             h, t = divmod(i, PACK)
+            if t == 0:
+                e[h] = placed("e%d" % h, [P, PACK, M], F32)
             nc.vector.tensor_tensor(out=e[h][:, t, :], in0=b_banks[i][:], in1=picked[i][:], op=ALU.subtract)
             if t == 0:
                 sq[h] = placed("sq%d" % h, [P, PACK, M], F32)
@@ -222,22 +224,22 @@ def tile_list_tract_county_audit_kernel(
 
         r, z_rows, z_bf, z_w, z_sc = {}, {}, {}, {}, {}
 
-        def root(h, lo, hi):
-            r[h, lo] = stage.tile([P, PACK, hi - lo], F32, name="r%d_%d" % (h, lo), align_bytes=64,
-                                  offset=PLACE["r%d" % h] + 4 * PACK * lo)
-            nc.scalar.activation(r[h, lo][:], sq[h][:, :, lo:hi], ACT.Abs_reciprocal_sqrt, bias=1.0)
+        def root(h, t):
+            if t == 0:
+                r[h] = placed("r%d" % h, [P, PACK, M], F32)
+            nc.scalar.activation(r[h][:, t, :], sq[h][:, t, :], ACT.Abs_reciprocal_sqrt, bias=1.0)
 
-        def z_round(h, lo, hi):
-            z_rows[h, lo] = keep.tile([P, PACK, hi - lo], BF16, name="z_rows%d_%d" % (h, lo), align_bytes=64)
-            for t in range(PACK):
-                nc.vector.scalar_tensor_tensor(
-                    out=z_rows[h, lo][:, t, :], in0=e[h][:, t, lo:hi], scalar=g[:, h, t : t + 1],
-                    in1=r[h, lo][:, t, :], op0=ALU.mult, op1=ALU.mult)
+        def z_round(h, t, lo, hi):
+            if h not in z_rows:
+                z_rows[h] = keep.tile([P, PACK, M], BF16, name="z_rows%d" % h, align_bytes=64)
+            nc.vector.scalar_tensor_tensor(
+                out=z_rows[h][:, t, lo:hi], in0=e[h][:, t, lo:hi], scalar=g[:, h, t : t + 1],
+                in1=r[h][:, t, lo:hi], op0=ALU.mult, op1=ALU.mult)
 
         def z_weave(h, lo, hi):
             z_bf[h, lo] = keep.tile([P, hi - lo, PACK], BF16, name="z_bf%d_%d" % (h, lo), align_bytes=64)
             nc.vector.tensor_copy(out=z_bf[h, lo][:].rearrange("p (c i) t -> p c t i", i=PACK),
-                                  in_=z_rows[h, lo][:].rearrange("p t (c i) -> p c t i", i=PACK))
+                                  in_=z_rows[h][:, :, lo:hi].rearrange("p t (c i) -> p c t i", i=PACK))
 
         def z_quantize(h, lo, hi):
             z_w[h, lo] = keep.tile([P, hi - lo], U32, name="z_w%d_%d" % (h, lo), align_bytes=64)
@@ -247,21 +249,28 @@ def tile_list_tract_county_audit_kernel(
 
         out_banks = {}
 
-        def out_pass(c, h):
-            if h == 0:
-                out_banks[c] = bank(c, [P, N // P, CHUNK])
-            piece, cols = ((0, 0), slice(CHUNK * c, CHUNK * (c + 1))) if h == 0 else ((1, CHUNK * c), slice(0, CHUNK))
+        def out_pass(lo, hi, h):
+            rows = BANK // (hi - lo)
+            first = 0 if h == 0 else lo
             for n in range(N // P):
+                key = (lo, n // rows)
+                if key not in out_banks:
+                    out_banks[key] = bank(len(out_banks), [P, rows, hi - lo])
                 nc.tensor.matmul_mx(
-                    out=out_banks[c][:, n, :], lhsT=w3_w[:, h, P * n : P * (n + 1)].bitcast(FP8X4),
+                    out=out_banks[key][:, n % rows, :], lhsT=w3_w[:, h, P * n : P * (n + 1)].bitcast(FP8X4),
                     lhsT_scale=planes[h][:, W3 + P * n : W3 + P * (n + 1)],
-                    rhs=z_w[piece][:, cols].bitcast(FP8X4), rhs_scale=z_sc[piece][:, cols],
-                    start=(h == 0 and n == 0), stop=(h == 1 and n == N // P - 1))
+                    rhs=z_w[h, first][:, lo - first : hi - first].bitcast(FP8X4),
+                    rhs_scale=z_sc[h, first][:, lo - first : hi - first],
+                    start=(h == 0 and n % rows == 0), stop=(h == 1 and n % rows == rows - 1))
 
-        def store(c):
-            res = keep.tile([P, N // P, CHUNK], F32, name="res%d" % c)
-            nc.scalar.copy(out=res[:], in_=out_banks[c][:])
-            nc.sync.dma_start(out=out[:, CHUNK * c : CHUNK * (c + 1)].rearrange("(n p) m -> p n m", p=P), in_=res[:])
+        def store(lo, hi, copy):
+            rows = BANK // (hi - lo)
+            for group in range(N // P // rows):
+                res = keep.tile([P, rows, hi - lo], F32, name="res%d_%d" % (lo, group))
+                copy(out=res[:], in_=out_banks[lo, group][:])
+                nc.sync.dma_start(
+                    out=out[P * rows * group : P * rows * (group + 1), lo:hi].rearrange("(n p) m -> p n m", p=P),
+                    in_=res[:])
 
         for half in range(2):
             for i in range(PACK):
@@ -270,45 +279,57 @@ def tile_list_tract_county_audit_kernel(
             for half in range(2):
                 x_pass(pair, half, 1)
                 x_pass(pair + 1, half, 1)
-        for i in range(5):
+        for i in range(2 * PACK):
             x_tile(i)
+        w3_w = placed("w3_w", [P, 2, N], U32)
+        nc.sync.dma_start(out=w3_w[:].bitcast(I32),
+                          in_=w3_words.rearrange("a p c i -> p a (c i)").bitcast(I32))
         gather2(0)
-        gather2(1)
         w2_round(0, 0, nc.scalar.copy)
         w2_round(0, 1, nc.scalar.copy)
-        w2_quantize(0, 0)
-        w2_quantize(0, 1)
-        for i in range(5, 2 * PACK):
-            x_tile(i)
-        b_passes(0, 0)
-        b_passes(0, 1)
         w2_round(1, 0, nc.scalar.copy)
-        w2_round(1, 1, nc.scalar.copy)
+        w2_quantize(0, 0)
+        b_passes(0, 0)
+        gather2(1)
+        w2_quantize(0, 1)
+        b_passes(0, 1)
+        w2_round(1, 1, nc.vector.tensor_copy, 0, P // 2)
+        w2_round(1, 1, nc.scalar.copy, P // 2, P)
+        diff_tile(0)
+        diff_tile(1)
         w2_quantize(1, 0)
         b_passes(1, 0)
-        for t in range(PACK):
-            diff_tile(t)
+        diff_tile(2)
         w2_quantize(1, 1)
         b_passes(1, 1)
-        root(0, 0, M)
+        diff_tile(3)
+        for t in range(PACK):
+            root(0, t)
         for t in range(PACK):
             diff_tile(PACK + t)
-        chunks = M // CHUNK
-        for c in range(chunks):
-            root(1, CHUNK * c, CHUNK * (c + 1))
-        z_round(0, 0, M)
+        for t in range(PACK):
+            root(1, t)
+        half, pieces = M // 2, ((0, M // 2), (M // 2, M - CHUNK), (M - CHUNK, M))
+        for t in range(PACK):
+            z_round(0, t, 0, M)
         z_weave(0, 0, M)
-        z_round(1, 0, CHUNK)
+        z_round(1, 0, 0, half)
         z_quantize(0, 0, M)
-        for c in range(chunks):
-            out_pass(c, 0)
-        for step in range(1, chunks + 2):
-            if step <= chunks:
-                z_weave(1, CHUNK * (step - 1), CHUNK * step)
-            if step < chunks:
-                z_round(1, CHUNK * step, CHUNK * (step + 1))
-            if step >= 2:
-                c = step - 2
-                z_quantize(1, CHUNK * c, CHUNK * (c + 1))
-                out_pass(c, 1)
-                store(c)
+        for lo, hi in pieces:
+            out_pass(lo, hi, 0)
+        for t in range(1, PACK):
+            z_round(1, t, 0, half)
+        z_round(1, 0, half, M)
+        z_weave(1, *pieces[0])
+        z_round(1, 1, half, M)
+        z_quantize(1, *pieces[0])
+        out_pass(*pieces[0], 1)
+        store(*pieces[0], nc.scalar.copy)
+        z_round(1, 2, half, M)
+        z_round(1, 3, half, M)
+        z_weave(1, *pieces[1])
+        z_weave(1, *pieces[2])
+        for piece, copy in zip(pieces[1:], (nc.scalar.copy, nc.vector.tensor_copy)):
+            z_quantize(1, *piece)
+            out_pass(*piece, 1)
+            store(*piece, copy)

@@ -24,14 +24,14 @@ CHUNK = 128
 KIB = 1024
 LIVE = 32
 PLACE = {
-    "v2_sc_rows": 0, "g": 0,
-    "w2_raw00_0": 8 * KIB + 64, "tab_w0": 16 * KIB, "tab2_w": 16 * KIB + 64,
-    "w2_raw01_0": 33 * KIB + 64, "tab_w1": 41 * KIB, "w2_raw10_0": 41 * KIB + 64, "w3_w": 66 * KIB,
+    "v2_sc_rows": 0, "w1_w0": 0, "w1_raw0": 4 * KIB, "g": 4 * KIB, "w1_raw1": 16 * KIB + 64,
+    "w2_raw00_0": 8 * KIB + 64, "tab_w0": 16 * KIB, "tab2_w": 18 * KIB + 64,
+    "w2_raw01_0": 34 * KIB + 64, "tab_w1": 42 * KIB, "w2_raw10_0": 42 * KIB + 64, "w3_w": 66 * KIB,
     "x_sb": 66 * KIB, "w2_bf00": 86 * KIB, "w2_bf01": 90 * KIB, "v2_w0": 94 * KIB, "v2_w1": 86 * KIB,
-    "w2_bf10": 16 * KIB + 64, "w2_bf11": 90 * KIB,
-    "w2_raw11_0": 57 * KIB - 64, "w2_raw11_64": 49 * KIB + 64,
+    "w2_bf10": 18 * KIB + 64, "w2_bf11": 90 * KIB,
+    "w1_w1": 55 * KIB, "w2_raw11_0": 58 * KIB - 64, "w2_raw11_64": 50 * KIB + 64,
     "picked": 98 * KIB, "w2_w00": 114 * KIB, "w2_w01": 116 * KIB, "w2_w10": 100 * KIB, "w2_w11": 102 * KIB,
-    "sq0": 45 * KIB + 64, "sq1": 8 * KIB + 64, "e0": 57 * KIB - 64, "e1": 33 * KIB + 64, "r0": 16 * KIB + 64, "r1": 24 * KIB + 64,
+    "sq0": 46 * KIB + 64, "sq1": 8 * KIB + 64, "e0": 58 * KIB - 64, "e1": 34 * KIB + 64, "r0": 18 * KIB + 64, "r1": 26 * KIB + 64,
 }
 
 
@@ -74,12 +74,19 @@ def tile_list_tract_county_audit_kernel(
         tab_sc = keep.tile([P, T], U8, name="tab_sc", align_bytes=64)
         tab2_sc = keep.tile([P, T2], U8, name="tab2_sc", align_bytes=64)
         w1_sc_raw = keep.tile([P, H], U8, name="w1_sc_raw", align_bytes=64)
-        w1_raw = keep.tile([P, 2, 2 * H], U8, name="w1_raw", align_bytes=64)
         planes = [keep.tile([P, S + H + M + N], U8, name="plane%d" % a, align_bytes=64) for a in range(2)]
         V1, W1, V2, W3 = 0, S, S + H, S + H + M
 
         def load_rows(rows, dram):
             nc.sync.dma_start(out=rows.bitcast(I32), in_=dram.bitcast(I32).rearrange("a q c -> (a q) c"))
+
+        w1_raw, w1_w = {}, {}
+
+        def w1_load(h):
+            w1_raw[h] = placed("w1_raw%d" % h, [P, 2, 2 * PASS], U8)
+            nc.sync.dma_start(
+                out=w1_raw[h][:].bitcast(I32),
+                in_=w1_words[:, :, 2 * PASS * h : 2 * PASS * (h + 1)].bitcast(I32).rearrange("a p c -> p a c"))
 
         nc.sync.dma_start(offs_sb[:], offs)
         load_rows(tab_sc[:LIVE, :], tab_scales)
@@ -87,22 +94,18 @@ def tile_list_tract_county_audit_kernel(
         nc.sync.dma_start(offs2_sb[:], offs2)
         load_rows(tab2_sc[:LIVE, :], tab2_scales)
         load_rows(planes[0][:LIVE, W3:], w3_scales)
-        nc.sync.dma_start(out=w1_raw[:].bitcast(I32), in_=w1_words.bitcast(I32).rearrange("a p c -> p a c"))
+        w1_load(0)
         tab_w = [load_words(0)]
         nc.sync.dma_start(pos_sb[:], pos1)
         tab_w.append(load_words(1))
 
-        def clear_dead_rows(tile):
-            nc.vector.memset(tile[32:64, :].bitcast(I32), 0)
-            nc.vector.memset(tile[64:, :].bitcast(I32), 0)
-
-        clear_dead_rows(tab_sc)
+        for dead in (slice(32, 64), slice(64, P)):
+            for tile in (tab_sc, w1_sc_raw, tab2_sc, planes[0][:, W3:]):
+                nc.vector.memset(tile[dead, :].bitcast(I32), 0)
         warm = keep.tile([P, 1], F32, name="warm")
         warm_out = keep.tile([P, 1], F32, name="warm_out")
         nc.vector.memset(warm[:], 1.0)
         nc.scalar.activation(warm_out[:], warm[:], ACT.Abs_reciprocal_sqrt, bias=1.0)
-        for tile in (w1_sc_raw, tab2_sc, planes[0][:, W3:]):
-            clear_dead_rows(tile)
         nc.vector.memset(planes[1][:].bitcast(I32), 0)
 
         v_sc_rows = keep.tile([P, S], U8, name="v_sc_rows", align_bytes=64)
@@ -116,15 +119,18 @@ def tile_list_tract_county_audit_kernel(
         nc.vector.tensor_copy(out=planes[0][:, V2:W3].bitcast(I32), in_=v2_sc_rows[:].bitcast(I32))
         for group in range(1, 8):
             a, q = divmod(group, 4)
-            nc.scalar.dma_start(out=planes[a][32 * q : 32 * q + 4, :].bitcast(I32),
-                                in_=planes[0][4 * group : 4 * group + 4, :].bitcast(I32))
+            queue = nc.sync if a else nc.scalar
+            queue.dma_start(out=planes[a][32 * q : 32 * q + 4, :].bitcast(I32),
+                            in_=planes[0][4 * group : 4 * group + 4, :].bitcast(I32))
+
+        def w1_deal(h, tile):
+            w1_w[h] = tile
+            nc.vector.tensor_copy(out=tile[:].bitcast(U16).rearrange("p a (t m) -> p a t m", t=PACK),
+                                  in_=w1_raw[h][:].bitcast(U16).rearrange("p a (m t) -> p a t m", t=PACK))
+
+        w1_deal(0, placed("w1_w0", [P, 2, 2 * PASS], U8))
         g = placed("g", [P, 2, PACK], F32)
         nc.scalar.dma_start(out=g[:], in_=gain.rearrange("(a p t) -> p a t", a=2, t=PACK))
-
-        w1_w = keep.tile([P, 2, 2 * H], U8, name="w1_w", align_bytes=64)
-        nc.vector.tensor_copy(
-            out=w1_w[:].bitcast(U16).rearrange("p a (h t m) -> p (a h) t m", h=2, t=PACK),
-            in_=w1_raw[:].bitcast(U16).rearrange("p a (h m t) -> p (a h) t m", h=2, t=PACK))
 
         v_w = {}
 
@@ -135,11 +141,13 @@ def tile_list_tract_county_audit_kernel(
 
         gather1(0, 0)
         gather1(0, 1)
+        w1_load(1)
         tab2_w = placed("tab2_w", [P, 2, T2], U32)
         nc.sync.dma_start(out=tab2_w[:].bitcast(I32), in_=tab2_words.rearrange("a p t i -> p a (t i)").bitcast(I32))
         w2_load(0, 0)
         gather1(1, 0)
         gather1(1, 1)
+        w1_deal(1, placed("w1_w1", [P, 2, 2 * PASS], U8))
         w2_load(0, 1)
         w2_load(1, 0)
         w2_load(1, 1, 0, P // 2)
@@ -155,7 +163,7 @@ def tile_list_tract_county_audit_kernel(
                 x_banks[i, half] = bank((2 * i + half) % X_BANKS, [P, BANK])
             nc.tensor.matmul_mx(
                 out=x_banks[i, half][:],
-                lhsT=w1_w[:, a, 2 * P * i : 2 * P * (i + 1)].bitcast(FP4X4),
+                lhsT=w1_w[i // PACK][:, a, 2 * P * (i % PACK) : 2 * P * (i % PACK + 1)].bitcast(FP4X4),
                 lhsT_scale=planes[a][:, W1 + P * i : W1 + P * (i + 1)],
                 rhs=v_w[a, half][:].bitcast(FP8X4), rhs_scale=planes[a][:, BANK * half : BANK * (half + 1)],
                 start=(a == 0), stop=(a == 1))
@@ -249,8 +257,7 @@ def tile_list_tract_county_audit_kernel(
 
         out_banks = {}
 
-        def out_pass(lo, hi, h):
-            rows = BANK // (hi - lo)
+        def out_pass(lo, hi, rows, h):
             first = 0 if h == 0 else lo
             for n in range(N // P):
                 key = (lo, n // rows)
@@ -263,9 +270,8 @@ def tile_list_tract_county_audit_kernel(
                     rhs_scale=z_sc[h, first][:, lo - first : hi - first],
                     start=(h == 0 and n % rows == 0), stop=(h == 1 and n % rows == rows - 1))
 
-        def store(lo, hi, copy):
-            rows = BANK // (hi - lo)
-            for group in range(N // P // rows):
+        def store(lo, hi, rows, *copies):
+            for group, copy in enumerate(copies):
                 res = keep.tile([P, rows, hi - lo], F32, name="res%d_%d" % (lo, group))
                 copy(out=res[:], in_=out_banks[lo, group][:])
                 nc.sync.dma_start(
@@ -309,27 +315,27 @@ def tile_list_tract_county_audit_kernel(
             diff_tile(PACK + t)
         for t in range(PACK):
             root(1, t)
-        half, pieces = M // 2, ((0, M // 2), (M // 2, M - CHUNK), (M - CHUNK, M))
+        half, pieces = M // 2, ((0, M // 2, 2), (M // 2, M - CHUNK, 4), (M - CHUNK, M, 2))
         for t in range(PACK):
             z_round(0, t, 0, M)
         z_weave(0, 0, M)
         z_round(1, 0, 0, half)
         z_quantize(0, 0, M)
-        for lo, hi in pieces:
-            out_pass(lo, hi, 0)
+        for piece in pieces:
+            out_pass(*piece, 0)
         for t in range(1, PACK):
             z_round(1, t, 0, half)
         z_round(1, 0, half, M)
-        z_weave(1, *pieces[0])
+        z_weave(1, *pieces[0][:2])
         z_round(1, 1, half, M)
-        z_quantize(1, *pieces[0])
+        z_quantize(1, *pieces[0][:2])
         out_pass(*pieces[0], 1)
-        store(*pieces[0], nc.scalar.copy)
+        store(*pieces[0], nc.scalar.copy, nc.scalar.copy)
         z_round(1, 2, half, M)
         z_round(1, 3, half, M)
-        z_weave(1, *pieces[1])
-        z_weave(1, *pieces[2])
-        for piece, copy in zip(pieces[1:], (nc.scalar.copy, nc.vector.tensor_copy)):
-            z_quantize(1, *piece)
+        z_weave(1, *pieces[1][:2])
+        z_weave(1, *pieces[2][:2])
+        for piece, copies in zip(pieces[1:], ([nc.scalar.copy], [nc.vector.tensor_copy, nc.scalar.copy])):
+            z_quantize(1, *piece[:2])
             out_pass(*piece, 1)
-            store(*piece, copy)
+            store(*piece, *copies)

@@ -27,11 +27,11 @@ PLACE = {
     "v2_sc_rows": 0, "w1_w0": 0, "w1_raw0": 4 * KIB, "g": 4 * KIB, "w1_raw1": 16 * KIB + 64,
     "w2_raw00_0": 8 * KIB + 64, "tab_w0": 16 * KIB, "tab2_w": 18 * KIB + 64,
     "w2_raw01_0": 34 * KIB + 64, "tab_w1": 42 * KIB, "w2_raw10_0": 42 * KIB + 64, "w3_w": 66 * KIB,
-    "x_sb": 66 * KIB, "w2_bf00": 86 * KIB, "w2_bf01": 90 * KIB, "v2_w0": 94 * KIB, "v2_w1": 86 * KIB,
-    "w2_bf10": 18 * KIB + 64, "w2_bf11": 90 * KIB,
+    "x_sb": 66 * KIB, "w2_bf00": 78 * KIB, "w2_bf01": 82 * KIB, "v2_w0": 94 * KIB, "v2_w1": 78 * KIB,
+    "w2_bf10": 86 * KIB, "w2_bf11": 82 * KIB,
     "w1_w1": 55 * KIB, "w2_raw11_0": 58 * KIB - 64, "w2_raw11_64": 50 * KIB + 64,
     "picked": 98 * KIB, "w2_w00": 114 * KIB, "w2_w01": 116 * KIB, "w2_w10": 100 * KIB, "w2_w11": 102 * KIB,
-    "sq0": 46 * KIB + 64, "sq1": 8 * KIB + 64, "e0": 58 * KIB - 64, "e1": 34 * KIB + 64, "r0": 18 * KIB + 64, "r1": 26 * KIB + 64,
+    "sq0": 42 * KIB + 64, "sq1": 8 * KIB + 64, "e0": 58 * KIB - 64, "e1": 34 * KIB + 64, "r0": 18 * KIB + 64, "r1": 26 * KIB + 64,
 }
 
 
@@ -244,10 +244,10 @@ def tile_list_tract_county_audit_kernel(
                 out=z_rows[h][:, t, lo:hi], in0=e[h][:, t, lo:hi], scalar=g[:, h, t : t + 1],
                 in1=r[h][:, t, lo:hi], op0=ALU.mult, op1=ALU.mult)
 
-        def z_weave(h, lo, hi):
+        def z_weave(h, lo, hi, copy=nc.vector.tensor_copy):
             z_bf[h, lo] = keep.tile([P, hi - lo, PACK], BF16, name="z_bf%d_%d" % (h, lo), align_bytes=64)
-            nc.vector.tensor_copy(out=z_bf[h, lo][:].rearrange("p (c i) t -> p c t i", i=PACK),
-                                  in_=z_rows[h][:, :, lo:hi].rearrange("p t (c i) -> p c t i", i=PACK))
+            copy(out=z_bf[h, lo][:].rearrange("p (c i) t -> p c t i", i=PACK),
+                 in_=z_rows[h][:, :, lo:hi].rearrange("p t (c i) -> p c t i", i=PACK))
 
         def z_quantize(h, lo, hi):
             z_w[h, lo] = keep.tile([P, hi - lo], U32, name="z_w%d_%d" % (h, lo), align_bytes=64)
@@ -258,7 +258,7 @@ def tile_list_tract_county_audit_kernel(
         out_banks = {}
 
         def out_pass(lo, hi, rows, h):
-            first = 0 if h == 0 else lo
+            first = lo // (M // 2) * (M // 2) if h == 0 else lo
             for n in range(N // P):
                 key = (lo, n // rows)
                 if key not in out_banks:
@@ -300,11 +300,11 @@ def tile_list_tract_county_audit_kernel(
         w2_quantize(0, 1)
         b_passes(0, 1)
         w2_round(1, 1, nc.vector.tensor_copy, 0, P // 2)
-        w2_round(1, 1, nc.scalar.copy, P // 2, P)
         diff_tile(0)
         diff_tile(1)
         w2_quantize(1, 0)
         b_passes(1, 0)
+        w2_round(1, 1, nc.vector.tensor_copy, P // 2, P)
         diff_tile(2)
         w2_quantize(1, 1)
         b_passes(1, 1)
@@ -318,11 +318,11 @@ def tile_list_tract_county_audit_kernel(
         half, pieces = M // 2, ((0, M // 2, 2), (M // 2, M - CHUNK, 4), (M - CHUNK, M, 2))
         for t in range(PACK):
             z_round(0, t, 0, M)
-        z_weave(0, 0, M)
+        z_weave(0, 0, half)
+        z_weave(0, half, M, nc.scalar.copy)
         z_round(1, 0, 0, half)
-        z_quantize(0, 0, M)
-        for piece in pieces:
-            out_pass(*piece, 0)
+        z_quantize(0, 0, half)
+        out_pass(*pieces[0], 0)
         for t in range(1, PACK):
             z_round(1, t, 0, half)
         z_round(1, 0, half, M)
@@ -331,6 +331,9 @@ def tile_list_tract_county_audit_kernel(
         z_quantize(1, *pieces[0][:2])
         out_pass(*pieces[0], 1)
         store(*pieces[0], nc.scalar.copy, nc.scalar.copy)
+        z_quantize(0, half, M)
+        for piece in pieces[1:]:
+            out_pass(*piece, 0)
         z_round(1, 2, half, M)
         z_round(1, 3, half, M)
         z_weave(1, *pieces[1][:2])

@@ -20,18 +20,22 @@ P = 128
 PACK = 4
 PASS = 512
 BANK = 512
-CHUNK = 128
 KIB = 1024
 LIVE = 32
+PICK_SLOTS = 7
+EARLY = 2
+X_BANKS = 4
+BIG = 1e38
 PLACE = {
-    "v2_sc_rows": 0, "w1_w0": 0, "w1_raw0": 4 * KIB, "g": 4 * KIB, "w1_raw1": 16 * KIB + 64,
-    "w2_raw00_0": 8 * KIB + 64, "tab_w0": 16 * KIB, "tab2_w": 18 * KIB + 64,
-    "w2_raw01_0": 34 * KIB + 64, "tab_w1": 42 * KIB, "w2_raw10_0": 42 * KIB + 64, "w3_w": 66 * KIB,
-    "x_sb": 66 * KIB, "w2_bf00": 78 * KIB, "w2_bf01": 82 * KIB, "v2_w0": 94 * KIB, "v2_w1": 78 * KIB,
-    "w2_bf10": 86 * KIB, "w2_bf11": 82 * KIB,
-    "w1_w1": 55 * KIB, "w2_raw11_0": 58 * KIB - 64, "w2_raw11_64": 50 * KIB + 64,
-    "picked": 98 * KIB, "w2_w00": 114 * KIB, "w2_w01": 116 * KIB, "w2_w10": 100 * KIB, "w2_w11": 102 * KIB,
-    "sq0": 42 * KIB + 64, "sq1": 8 * KIB + 64, "e0": 58 * KIB - 64, "e1": 34 * KIB + 64, "r0": 18 * KIB + 64, "r1": 26 * KIB + 64,
+    "w1_raw0": 0, "w1_raw1": 0,
+    "w2_raw00": 4 * KIB + 64, "tab_w0": 12 * KIB, "tab2_w": 20 * KIB,
+    "w2_raw01": 38 * KIB + 64, "tab_w1": 46 * KIB, "w2_raw10": 46 * KIB + 64, "w2_raw11": 54 * KIB + 64,
+    "x_sb": 64 * KIB, "w1_w1": 64 * KIB, "g_raw_inv": 67 * KIB, "w3_w": 68 * KIB,
+    "w2_w00": 72 * KIB, "v2_w0": 76 * KIB, "v2_w1": 78 * KIB, "w2_w01": 84 * KIB,
+    "picked": 96 * KIB,
+    "w1_w0": 112 * KIB, "v_w00": 114 * KIB, "v_w01": 116 * KIB, "v_w10": 118 * KIB, "v_w11": 120 * KIB,
+    "w2_bf00": 112 * KIB - 2 * KIB, "w2_bf01": 114 * KIB, "w2_bf10": 118 * KIB, "w2_bf11": 88 * KIB,
+    "r0": 54 * KIB + 64, "r1": 4 * KIB + 64, "w2_w10": 122 * KIB, "w2_w11": 124 * KIB,
 }
 
 
@@ -49,54 +53,57 @@ def tile_list_tract_county_audit_kernel(
         def placed(name, shape, dtype):
             return stage.tile(shape, dtype, name=name, align_bytes=64, offset=PLACE[name])
 
+        def kept(name, shape, dtype):
+            return keep.tile(shape, dtype, name=name, align_bytes=64)
+
         def bank(index, shape):
             return psum.tile(shape, F32, name="bank", tag="bank%d" % index)
 
-        def words(dram, a):
-            return dram[a].rearrange("p t i -> p (t i)").bitcast(I32)
-
         def load_words(a):
             tile = placed("tab_w%d" % a, [P, T], U32)
-            nc.sync.dma_start(out=tile[:].bitcast(I32), in_=words(tab_words, a))
+            nc.sync.dma_start(out=tile[:].bitcast(I32), in_=tab_words[a].rearrange("p t i -> p (t i)").bitcast(I32))
             return tile
 
         w2_raw = {}
 
-        def w2_load(h, a, lo=0, hi=P):
-            tile = placed("w2_raw%d%d_%d" % (h, a, lo), [P, PACK, PACK * (hi - lo)], F32)
-            cols = slice(PASS * h + PACK * lo, PASS * h + PACK * hi)
-            nc.sync.dma_start(out=tile[:], in_=w2[PASS * a : PASS * (a + 1), cols].rearrange("(p j) c -> p j c", j=PACK))
-            w2_raw[h, a, lo] = tile
+        def w2_load(h, a):
+            tile = placed("w2_raw%d%d" % (h, a), [P, PACK, PASS], F32)
+            nc.sync.dma_start(
+                out=tile[:],
+                in_=w2[PASS * a : PASS * (a + 1), PASS * h : PASS * (h + 1)].rearrange("(p j) c -> p j c", j=PACK))
+            w2_raw[h, a] = tile
 
         offs_sb = lists.tile([P, S // 16], U16, name="offs_sb")
         offs2_sb = lists.tile([P, M // 16], U16, name="offs2_sb")
         pos_sb = lists.tile([P, M // 16], U16, name="pos_sb")
-        tab_sc = keep.tile([P, T], U8, name="tab_sc", align_bytes=64)
-        tab2_sc = keep.tile([P, T2], U8, name="tab2_sc", align_bytes=64)
-        w1_sc_raw = keep.tile([P, H], U8, name="w1_sc_raw", align_bytes=64)
-        planes = [keep.tile([P, S + H + M + N], U8, name="plane%d" % a, align_bytes=64) for a in range(2)]
-        V1, W1, V2, W3 = 0, S, S + H, S + H + M
+        tab_sc = kept("tab_sc", [P, T], U8)
+        w1_sc_raw = kept("w1_sc_raw", [P, H], U8)
+        tab2_sc = kept("tab2_sc", [P, T2], U8)
+        planes = [kept("plane%d" % a, [P, S + H + M + N], U8) for a in range(2)]
+        W1, V2, W3 = S, S + H, S + H + M
 
         def load_rows(rows, dram):
             nc.sync.dma_start(out=rows.bitcast(I32), in_=dram.bitcast(I32).rearrange("a q c -> (a q) c"))
 
         w1_raw, w1_w = {}, {}
 
-        def w1_load(h):
+        def w1_load(h, queue):
             w1_raw[h] = placed("w1_raw%d" % h, [P, 2, 2 * PASS], U8)
-            nc.sync.dma_start(
+            queue.dma_start(
                 out=w1_raw[h][:].bitcast(I32),
                 in_=w1_words[:, :, 2 * PASS * h : 2 * PASS * (h + 1)].bitcast(I32).rearrange("a p c -> p a c"))
 
-        nc.sync.dma_start(offs_sb[:], offs)
         load_rows(tab_sc[:LIVE, :], tab_scales)
+        nc.sync.dma_start(offs_sb[:], offs)
         load_rows(w1_sc_raw[:LIVE, :], w1_scales)
-        nc.sync.dma_start(offs2_sb[:], offs2)
         load_rows(tab2_sc[:LIVE, :], tab2_scales)
+        nc.sync.dma_start(offs2_sb[:], offs2)
         load_rows(planes[0][:LIVE, W3:], w3_scales)
-        w1_load(0)
+        w1_load(0, nc.sync)
         tab_w = [load_words(0)]
         nc.sync.dma_start(pos_sb[:], pos1)
+        g = kept("g", [P, 2, PACK], F32)
+        nc.sync.dma_start(out=g[:], in_=gain.rearrange("(a p t) -> p a t", a=2, t=PACK))
         tab_w.append(load_words(1))
 
         for dead in (slice(32, 64), slice(64, P)):
@@ -108,14 +115,14 @@ def tile_list_tract_county_audit_kernel(
         nc.scalar.activation(warm_out[:], warm[:], ACT.Abs_reciprocal_sqrt, bias=1.0)
         nc.vector.memset(planes[1][:].bitcast(I32), 0)
 
-        v_sc_rows = keep.tile([P, S], U8, name="v_sc_rows", align_bytes=64)
+        v_sc_rows = kept("v_sc_rows", [P, S], U8)
         nc.vector.tensor_copy(out=v_sc_rows[:], in_=tab_sc[:].indirect(offs_sb[:]))
         nc.vector.tensor_copy(
             out=planes[0][:, W1:V2].rearrange("p (h t m) -> p h t m", h=2, t=PACK),
             in_=w1_sc_raw[:].rearrange("p (h m t) -> p h t m", h=2, t=PACK))
-        nc.vector.tensor_copy(out=planes[0][:, V1:W1].bitcast(I32), in_=v_sc_rows[:].bitcast(I32))
-        v2_sc_rows = placed("v2_sc_rows", [P, M], U8)
+        v2_sc_rows = kept("v2_sc_rows", [P, M], U8)
         nc.vector.tensor_copy(out=v2_sc_rows[:], in_=tab2_sc[:].indirect(offs2_sb[:]))
+        nc.vector.tensor_copy(out=planes[0][:, :W1].bitcast(I32), in_=v_sc_rows[:].bitcast(I32))
         nc.vector.tensor_copy(out=planes[0][:, V2:W3].bitcast(I32), in_=v2_sc_rows[:].bitcast(I32))
         for group in range(1, 8):
             a, q = divmod(group, 4)
@@ -123,37 +130,33 @@ def tile_list_tract_county_audit_kernel(
             queue.dma_start(out=planes[a][32 * q : 32 * q + 4, :].bitcast(I32),
                             in_=planes[0][4 * group : 4 * group + 4, :].bitcast(I32))
 
-        def w1_deal(h, tile):
-            w1_w[h] = tile
-            nc.vector.tensor_copy(out=tile[:].bitcast(U16).rearrange("p a (t m) -> p a t m", t=PACK),
+        def w1_deal(h):
+            w1_w[h] = placed("w1_w%d" % h, [P, 2, 2 * PASS], U8)
+            nc.vector.tensor_copy(out=w1_w[h][:].bitcast(U16).rearrange("p a (t m) -> p a t m", t=PACK),
                                   in_=w1_raw[h][:].bitcast(U16).rearrange("p a (m t) -> p a t m", t=PACK))
 
-        w1_deal(0, placed("w1_w0", [P, 2, 2 * PASS], U8))
-        g = placed("g", [P, 2, PACK], F32)
-        nc.scalar.dma_start(out=g[:], in_=gain.rearrange("(a p t) -> p a t", a=2, t=PACK))
+        w1_deal(0)
+        w1_load(1, nc.scalar)
 
         v_w = {}
 
         def gather1(a, half):
-            v_w[a, half] = keep.tile([P, BANK], U32, name="v_w%d%d" % (a, half), align_bytes=64)
+            v_w[a, half] = placed("v_w%d%d" % (a, half), [P, BANK], U32)
             nc.vector.tensor_copy(out=v_w[a, half][:],
                                   in_=tab_w[a][:].indirect(offs_sb[:, 32 * half : 32 * (half + 1)]))
 
+        g_inv = kept("g_inv", [P, 2, PACK], F32)
         gather1(0, 0)
         gather1(0, 1)
-        w1_load(1)
+        w2_load(0, 0)
         tab2_w = placed("tab2_w", [P, 2, T2], U32)
         nc.sync.dma_start(out=tab2_w[:].bitcast(I32), in_=tab2_words.rearrange("a p t i -> p a (t i)").bitcast(I32))
-        w2_load(0, 0)
         gather1(1, 0)
         gather1(1, 1)
-        w1_deal(1, placed("w1_w1", [P, 2, 2 * PASS], U8))
         w2_load(0, 1)
         w2_load(1, 0)
-        w2_load(1, 1, 0, P // 2)
-        w2_load(1, 1, P // 2, P)
+        w2_load(1, 1)
 
-        X_BANKS = 8
         x_banks = {}
         x_sb = [stage.tile([P, S], F32, name="x_sb%d" % i, align_bytes=64, offset=PLACE["x_sb"] + 4 * S * i)
                 for i in range(2 * PACK)]
@@ -161,26 +164,31 @@ def tile_list_tract_county_audit_kernel(
         def x_pass(i, half, a):
             if a == 0:
                 x_banks[i, half] = bank((2 * i + half) % X_BANKS, [P, BANK])
+            cols = slice(BANK * half, BANK * (half + 1))
             nc.tensor.matmul_mx(
                 out=x_banks[i, half][:],
                 lhsT=w1_w[i // PACK][:, a, 2 * P * (i % PACK) : 2 * P * (i % PACK + 1)].bitcast(FP4X4),
                 lhsT_scale=planes[a][:, W1 + P * i : W1 + P * (i + 1)],
-                rhs=v_w[a, half][:].bitcast(FP8X4), rhs_scale=planes[a][:, BANK * half : BANK * (half + 1)],
+                rhs=v_w[a, half][:].bitcast(FP8X4), rhs_scale=planes[a][:, cols],
                 start=(a == 0), stop=(a == 1))
-
-        def x_copy(i, half, copy):
-            copy(out=x_sb[i][:, BANK * half : BANK * (half + 1)], in_=x_banks[i, half][:])
-
-        picked = {}
 
         def x_tile(i):
             for half in range(2):
-                if i >= PACK:
+                if i >= EARLY:
                     x_pass(i, half, 0)
                     x_pass(i, half, 1)
-                x_copy(i, half, nc.vector.tensor_copy if (i, half) == (0, 1) else nc.scalar.copy)
+                dst = x_sb[i][:, BANK * half : BANK * (half + 1)]
+                g_col = g[:, i // PACK, i % PACK : i % PACK + 1]
+                if (i, half) == (0, 1):
+                    nc.vector.tensor_scalar(dst, x_banks[i, half][:], g_col, None, ALU.mult)
+                else:
+                    nc.scalar.activation(dst, x_banks[i, half][:], ACT.Copy, scale=g_col)
+
+        picked = {}
+
+        def pick(i):
             picked[i] = stage.tile([P, M], F32, name="picked%d" % i, align_bytes=64,
-                                   offset=PLACE["picked"] + 4 * M * i)
+                                   offset=PLACE["picked"] + 4 * M * (i % PICK_SLOTS))
             nc.vector.tensor_copy(out=picked[i][:], in_=x_sb[i][:].indirect(pos_sb[:]))
 
         v2_w = {}
@@ -191,67 +199,56 @@ def tile_list_tract_county_audit_kernel(
 
         w2_bf, w2_w, w2_sc = {}, {}, {}
 
-        def w2_round(h, a, copy, lo=0, hi=P):
-            if lo == 0:
-                w2_bf[h, a] = placed("w2_bf%d%d" % (h, a), [P, PACK, P, PACK], BF16)
-            dst = w2_bf[h, a][:, :, lo:hi, :].rearrange("p t m j -> p m j t")
-            src = w2_raw[h, a, lo][:].rearrange("p j (m t) -> p m j t", t=PACK)
-            for t in range(0, PACK, 2):
+        def w2_round(h, a, *copies):
+            w2_bf[h, a] = placed("w2_bf%d%d" % (h, a), [P, PACK, P, PACK], BF16)
+            dst = w2_bf[h, a][:].rearrange("p t m j -> p m j t")
+            src = w2_raw[h, a][:].rearrange("p j (m t) -> p m j t", t=PACK)
+            for t, copy in zip((0, 2), copies):
                 copy(out=dst[:, :, :, t : t + 2], in_=src[:, :, :, t : t + 2])
 
         def w2_quantize(h, a):
             w2_w[h, a] = placed("w2_w%d%d" % (h, a), [P, PASS], U32)
-            w2_sc[h, a] = keep.tile([P, PASS], U8, name="w2_sc%d%d" % (h, a), align_bytes=64)
+            w2_sc[h, a] = kept("w2_sc%d%d" % (h, a), [P, PASS], U8)
             nc.vector.quantize_mx(out=w2_w[h, a][:].bitcast(FP8X4), scales=w2_sc[h, a][:],
                                   in_=w2_bf[h, a][:].rearrange("p t m j -> p (t m j)"))
-
-        e = {}
-        sq = {}
 
         b_banks = {}
 
         def b_passes(h, a):
-            first = a == 0
             for t in range(PACK):
-                if first:
-                    b_banks[PACK * h + t] = bank(PACK * h + t, [P, M])
+                if a == 0:
+                    b_banks[PACK * h + t] = bank(PACK * (1 - h) + t, [P, M])
                 cols = slice(P * t, P * (t + 1))
                 nc.tensor.matmul_mx(
                     out=b_banks[PACK * h + t][:],
                     lhsT=w2_w[h, a][:, cols].bitcast(FP8X4), lhsT_scale=w2_sc[h, a][:, cols],
-                    rhs=v2_w[a][:].bitcast(FP8X4), rhs_scale=planes[a][:, V2:W3], start=first, stop=not first)
+                    rhs=v2_w[a][:].bitcast(FP8X4), rhs_scale=planes[a][:, V2:W3], start=(a == 0), stop=(a == 1))
+
+        e = [kept("e%d" % h, [P, PACK, M], F32) for h in range(2)]
+        r = [placed("r%d" % h, [P, PACK, M], F32) for h in range(2)]
 
         def diff_tile(i):
             h, t = divmod(i, PACK)
-            if t == 0:
-                e[h] = placed("e%d" % h, [P, PACK, M], F32)
-            nc.vector.tensor_tensor(out=e[h][:, t, :], in0=b_banks[i][:], in1=picked[i][:], op=ALU.subtract)
-            if t == 0:
-                sq[h] = placed("sq%d" % h, [P, PACK, M], F32)
-            nc.scalar.activation(sq[h][:, t, :], e[h][:, t, :], ACT.Square)
+            nc.vector.scalar_tensor_tensor(out=e[h][:, t, :], in0=b_banks[i][:], scalar=g[:, h, t : t + 1],
+                                           in1=picked[i][:], op0=ALU.mult, op1=ALU.subtract)
+            nc.scalar.activation(r[h][:, t, :], e[h][:, t, :], ACT.Square, scale=g_inv[:, h, t : t + 1])
 
-        r, z_rows, z_bf, z_w, z_sc = {}, {}, {}, {}, {}
+        def root(i):
+            h, t = divmod(i, PACK)
+            nc.scalar.activation(r[h][:, t, :], r[h][:, t, :], ACT.Abs_reciprocal_sqrt, bias=1.0)
 
-        def root(h, t):
-            if t == 0:
-                r[h] = placed("r%d" % h, [P, PACK, M], F32)
-            nc.scalar.activation(r[h][:, t, :], sq[h][:, t, :], ACT.Abs_reciprocal_sqrt, bias=1.0)
+        z_bf, z_w, z_sc = {}, {}, {}
 
-        def z_round(h, t, lo, hi):
-            if h not in z_rows:
-                z_rows[h] = keep.tile([P, PACK, M], BF16, name="z_rows%d" % h, align_bytes=64)
-            nc.vector.scalar_tensor_tensor(
-                out=z_rows[h][:, t, lo:hi], in0=e[h][:, t, lo:hi], scalar=g[:, h, t : t + 1],
-                in1=r[h][:, t, lo:hi], op0=ALU.mult, op1=ALU.mult)
-
-        def z_weave(h, lo, hi, copy=nc.vector.tensor_copy):
-            z_bf[h, lo] = keep.tile([P, hi - lo, PACK], BF16, name="z_bf%d_%d" % (h, lo), align_bytes=64)
-            copy(out=z_bf[h, lo][:].rearrange("p (c i) t -> p c t i", i=PACK),
-                 in_=z_rows[h][:, :, lo:hi].rearrange("p t (c i) -> p c t i", i=PACK))
+        def z_round(h, lo, hi):
+            z_bf[h, lo] = kept("z_bf%d_%d" % (h, lo), [P, hi - lo, PACK], BF16)
+            nc.vector.tensor_tensor(
+                out=z_bf[h, lo][:].rearrange("p (c i) t -> p c t i", i=2),
+                in0=e[h][:, :, lo:hi].rearrange("p t (c i) -> p c t i", i=2),
+                in1=r[h][:, :, lo:hi].rearrange("p t (c i) -> p c t i", i=2), op=ALU.mult)
 
         def z_quantize(h, lo, hi):
-            z_w[h, lo] = keep.tile([P, hi - lo], U32, name="z_w%d_%d" % (h, lo), align_bytes=64)
-            z_sc[h, lo] = keep.tile([P, hi - lo], U8, name="z_sc%d_%d" % (h, lo), align_bytes=64)
+            z_w[h, lo] = kept("z_w%d_%d" % (h, lo), [P, hi - lo], U32)
+            z_sc[h, lo] = kept("z_sc%d_%d" % (h, lo), [P, hi - lo], U8)
             nc.vector.quantize_mx(out=z_w[h, lo][:].bitcast(FP8X4), scales=z_sc[h, lo][:],
                                   in_=z_bf[h, lo][:].rearrange("p m t -> p (m t)"))
 
@@ -262,7 +259,7 @@ def tile_list_tract_county_audit_kernel(
             for n in range(N // P):
                 key = (lo, n // rows)
                 if key not in out_banks:
-                    out_banks[key] = bank(len(out_banks), [P, rows, hi - lo])
+                    out_banks[key] = bank((PACK + len(out_banks)) % 8, [P, rows, hi - lo])
                 nc.tensor.matmul_mx(
                     out=out_banks[key][:, n % rows, :], lhsT=w3_w[:, h, P * n : P * (n + 1)].bitcast(FP8X4),
                     lhsT_scale=planes[h][:, W3 + P * n : W3 + P * (n + 1)],
@@ -278,67 +275,74 @@ def tile_list_tract_county_audit_kernel(
                     out=out[P * rows * group : P * rows * (group + 1), lo:hi].rearrange("(n p) m -> p n m", p=P),
                     in_=res[:])
 
-        for half in range(2):
-            for i in range(PACK):
-                x_pass(i, half, 0)
-        for pair in range(0, PACK, 2):
-            for half in range(2):
-                x_pass(pair, half, 1)
-                x_pass(pair + 1, half, 1)
-        for i in range(2 * PACK):
+        for a in range(2):
+            for i in range(EARLY):
+                for half in range(2):
+                    x_pass(i, half, a)
+        for i in range(PACK):
             x_tile(i)
+        pick(0)
+        w1_deal(1)
+        g_raw_inv = placed("g_raw_inv", [P, 2, PACK], F32)
+        nc.vector.reciprocal(g_raw_inv[:], g[:])
+        w2_round(0, 0, nc.scalar.copy, nc.scalar.copy)
+        for i in range(PACK, 2 * PACK):
+            x_tile(i)
+        w2_round(0, 1, nc.scalar.copy, nc.scalar.copy)
+        w2_round(1, 0, nc.scalar.copy, nc.scalar.copy)
+        pick(1)
+        nc.vector.tensor_scalar(g_inv[:], g_raw_inv[:], BIG, -BIG, ALU.min, ALU.max)
         w3_w = placed("w3_w", [P, 2, N], U32)
         nc.sync.dma_start(out=w3_w[:].bitcast(I32),
                           in_=w3_words.rearrange("a p c i -> p a (c i)").bitcast(I32))
-        gather2(0)
-        w2_round(0, 0, nc.scalar.copy)
-        w2_round(0, 1, nc.scalar.copy)
-        w2_round(1, 0, nc.scalar.copy)
+        pick(2)
+        pick(3)
         w2_quantize(0, 0)
+        gather2(0)
         b_passes(0, 0)
         gather2(1)
+        pick(4)
+        pick(5)
+        pick(6)
         w2_quantize(0, 1)
         b_passes(0, 1)
-        w2_round(1, 1, nc.vector.tensor_copy, 0, P // 2)
+        w2_round(1, 1, nc.scalar.copy, nc.vector.tensor_copy)
         diff_tile(0)
         diff_tile(1)
+        root(0)
+        root(1)
         w2_quantize(1, 0)
         b_passes(1, 0)
-        w2_round(1, 1, nc.vector.tensor_copy, P // 2, P)
         diff_tile(2)
+        diff_tile(3)
+        root(2)
+        root(3)
         w2_quantize(1, 1)
         b_passes(1, 1)
-        diff_tile(3)
-        for t in range(PACK):
-            root(0, t)
-        for t in range(PACK):
-            diff_tile(PACK + t)
-        for t in range(PACK):
-            root(1, t)
-        half, pieces = M // 2, ((0, M // 2, 2), (M // 2, M - CHUNK, 4), (M - CHUNK, M, 2))
-        for t in range(PACK):
-            z_round(0, t, 0, M)
-        z_weave(0, 0, half)
-        z_weave(0, half, M, nc.scalar.copy)
-        z_round(1, 0, 0, half)
+        pick(7)
+        for i in range(PACK, 2 * PACK, 2):
+            diff_tile(i)
+            diff_tile(i + 1)
+            root(i)
+            root(i + 1)
+        half = M // 2
+        pieces = ((0, half, 2), (half, half + P, 4), (half + P, M, 2))
+        z_round(0, 0, half)
+        z_round(0, half, M)
         z_quantize(0, 0, half)
         out_pass(*pieces[0], 0)
-        for t in range(1, PACK):
-            z_round(1, t, 0, half)
-        z_round(1, 0, half, M)
-        z_weave(1, *pieces[0][:2])
-        z_round(1, 1, half, M)
+        z_quantize(0, half, M)
+        out_pass(*pieces[1], 0)
+        out_pass(*pieces[2], 0)
+        z_round(1, *pieces[0][:2])
+        z_round(1, *pieces[1][:2])
         z_quantize(1, *pieces[0][:2])
         out_pass(*pieces[0], 1)
         store(*pieces[0], nc.scalar.copy, nc.scalar.copy)
-        z_quantize(0, half, M)
-        for piece in pieces[1:]:
-            out_pass(*piece, 0)
-        z_round(1, 2, half, M)
-        z_round(1, 3, half, M)
-        z_weave(1, *pieces[1][:2])
-        z_weave(1, *pieces[2][:2])
-        for piece, copies in zip(pieces[1:], ([nc.scalar.copy], [nc.vector.tensor_copy, nc.scalar.copy])):
-            z_quantize(1, *piece[:2])
-            out_pass(*piece, 1)
-            store(*piece, *copies)
+        z_round(1, *pieces[2][:2])
+        z_quantize(1, *pieces[1][:2])
+        out_pass(*pieces[1], 1)
+        store(*pieces[1], nc.scalar.copy)
+        z_quantize(1, *pieces[2][:2])
+        out_pass(*pieces[2], 1)
+        store(*pieces[2], nc.vector.tensor_copy, nc.scalar.copy)

@@ -22,7 +22,7 @@ PASS = 512
 BANK = 512
 KIB = 1024
 LIVE = 32
-PICK_SLOTS = 7
+PICK_SLOTS = 6
 EARLY = 2
 X_BANKS = 4
 BIG = 1e38
@@ -30,12 +30,12 @@ PLACE = {
     "w1_raw0": 0, "w1_raw1": 0,
     "w2_raw00": 4 * KIB + 64, "tab_w0": 12 * KIB, "tab2_w": 20 * KIB,
     "w2_raw01": 38 * KIB + 64, "tab_w1": 46 * KIB, "w2_raw10": 46 * KIB + 64, "w2_raw11": 54 * KIB + 64,
-    "x_sb": 64 * KIB, "w1_w1": 64 * KIB, "g_raw_inv": 67 * KIB, "w3_w": 68 * KIB,
-    "w2_w00": 72 * KIB, "v2_w0": 76 * KIB, "v2_w1": 78 * KIB, "w2_w01": 84 * KIB,
+    "x_sb": 64 * KIB, "w1_w1": 64 * KIB, "g_raw_inv": 67 * KIB, "w3_w": 80 * KIB,
+    "w2_w00": 70 * KIB - 64, "v2_w0": 72 * KIB, "v2_w1": 74 * KIB, "w2_w01": 76 * KIB,
     "picked": 96 * KIB,
     "w1_w0": 112 * KIB, "v_w00": 114 * KIB, "v_w01": 116 * KIB, "v_w10": 118 * KIB, "v_w11": 120 * KIB,
-    "w2_bf00": 112 * KIB - 2 * KIB, "w2_bf01": 114 * KIB, "w2_bf10": 118 * KIB, "w2_bf11": 88 * KIB,
-    "r0": 54 * KIB + 64, "r1": 4 * KIB + 64, "w2_w10": 122 * KIB, "w2_w11": 124 * KIB,
+    "w2_bf00": 126 * KIB, "w2_bf01": 130 * KIB, "w2_bf10": 118 * KIB, "w2_bf11": 134 * KIB,
+    "r0": 46 * KIB + 64, "r1": 4 * KIB + 64, "w2_w10": 122 * KIB, "w2_w11": 102 * KIB,
 }
 
 
@@ -206,6 +206,13 @@ def tile_list_tract_county_audit_kernel(
             for t, copy in zip((0, 2), copies):
                 copy(out=dst[:, :, :, t : t + 2], in_=src[:, :, :, t : t + 2])
 
+        def w2_round_pool(h, a):
+            w2_bf[h, a] = placed("w2_bf%d%d" % (h, a), [P, PACK, P, PACK], BF16)
+            dst = w2_bf[h, a][:].rearrange("p t m j -> p m t j")
+            src = w2_raw[h, a][:].rearrange("p j (m t) -> p m t j", t=PACK)
+            for lo in range(0, P, P // 4):
+                nc.gpsimd.tensor_copy(out=dst[:, lo : lo + P // 4], in_=src[:, lo : lo + P // 4])
+
         def w2_quantize(h, a):
             w2_w[h, a] = placed("w2_w%d%d" % (h, a), [P, PASS], U32)
             w2_sc[h, a] = kept("w2_sc%d%d" % (h, a), [P, PASS], U8)
@@ -285,28 +292,27 @@ def tile_list_tract_county_audit_kernel(
         w1_deal(1)
         g_raw_inv = placed("g_raw_inv", [P, 2, PACK], F32)
         nc.vector.reciprocal(g_raw_inv[:], g[:])
-        w2_round(0, 0, nc.scalar.copy, nc.scalar.copy)
+        w2_round_pool(0, 0)
         for i in range(PACK, 2 * PACK):
             x_tile(i)
-        w2_round(0, 1, nc.scalar.copy, nc.scalar.copy)
+        w2_round_pool(0, 1)
         w2_round(1, 0, nc.scalar.copy, nc.scalar.copy)
         pick(1)
         nc.vector.tensor_scalar(g_inv[:], g_raw_inv[:], BIG, -BIG, ALU.min, ALU.max)
-        w3_w = placed("w3_w", [P, 2, N], U32)
-        nc.sync.dma_start(out=w3_w[:].bitcast(I32),
-                          in_=w3_words.rearrange("a p c i -> p a (c i)").bitcast(I32))
+        w2_round_pool(1, 1)
         pick(2)
-        pick(3)
         w2_quantize(0, 0)
         gather2(0)
         b_passes(0, 0)
         gather2(1)
+        pick(3)
         pick(4)
-        pick(5)
-        pick(6)
+        w3_w = placed("w3_w", [P, 2, N], U32)
+        nc.sync.dma_start(out=w3_w[:].bitcast(I32),
+                          in_=w3_words.rearrange("a p c i -> p a (c i)").bitcast(I32))
         w2_quantize(0, 1)
         b_passes(0, 1)
-        w2_round(1, 1, nc.scalar.copy, nc.vector.tensor_copy)
+        pick(5)
         diff_tile(0)
         diff_tile(1)
         root(0)
@@ -319,6 +325,7 @@ def tile_list_tract_county_audit_kernel(
         root(3)
         w2_quantize(1, 1)
         b_passes(1, 1)
+        pick(6)
         pick(7)
         for i in range(PACK, 2 * PACK, 2):
             diff_tile(i)

@@ -22,8 +22,9 @@ PASS = 512
 BANK = 512
 KIB = 1024
 LIVE = 32
-PICK_SLOTS = 6
+PICK_SLOTS = 5
 EARLY = 2
+FUSED = 6
 X_BANKS = 4
 BIG = 1e38
 PLACE = {
@@ -32,10 +33,13 @@ PLACE = {
     "w2_raw01": 38 * KIB + 64, "tab_w1": 46 * KIB, "w2_raw10": 46 * KIB + 64, "w2_raw11": 54 * KIB + 64,
     "x_sb": 64 * KIB, "w1_w1": 64 * KIB, "g_raw_inv": 67 * KIB, "w3_w": 80 * KIB,
     "w2_w00": 70 * KIB - 64, "v2_w0": 72 * KIB, "v2_w1": 74 * KIB, "w2_w01": 76 * KIB,
-    "picked": 96 * KIB,
+    "picked": 96 * KIB, "z_w0_0": 104 * KIB, "z_w0_256": 103 * KIB, "z_w0_384": 99 * KIB,
+    "z_w1_0": 96 * KIB, "z_w1_256": 97 * KIB, "z_w1_384": 98 * KIB,
+    "z_bf0_0": 88 * KIB, "z_bf0_256": 91 * KIB, "z_bf0_384": 90 * KIB,
+    "z_bf1_0": 88 * KIB, "z_bf1_256": 91 * KIB - 512, "z_bf1_384": 91 * KIB + 512,
     "w1_w0": 112 * KIB, "v_w00": 114 * KIB, "v_w01": 116 * KIB, "v_w10": 118 * KIB, "v_w11": 120 * KIB,
     "w2_bf00": 126 * KIB, "w2_bf01": 130 * KIB, "w2_bf10": 118 * KIB, "w2_bf11": 134 * KIB,
-    "r0": 46 * KIB + 64, "r1": 4 * KIB + 64, "w2_w10": 122 * KIB, "w2_w11": 102 * KIB,
+    "r0": 46 * KIB + 64, "r1": 4 * KIB + 64, "w2_w10": 122 * KIB, "w2_w11": 124 * KIB,
 }
 
 
@@ -146,8 +150,13 @@ def tile_list_tract_county_audit_kernel(
                                   in_=tab_w[a][:].indirect(offs_sb[:, 32 * half : 32 * (half + 1)]))
 
         g_inv = kept("g_inv", [P, 2, PACK], F32)
+        g_raw_inv = kept("g_raw_inv", [P, 2, PACK], F32)
         gather1(0, 0)
+        nc.vector.reciprocal(g_raw_inv[:], g[:])
         gather1(0, 1)
+        g_neg = kept("g_neg", [P, 2, PACK], F32)
+        nc.vector.tensor_scalar(g_neg[:], g[:], -1.0, None, ALU.mult)
+        nc.vector.tensor_scalar(g_inv[:], g_raw_inv[:], BIG, -BIG, ALU.min, ALU.max)
         w2_load(0, 0)
         tab2_w = placed("tab2_w", [P, 2, T2], U32)
         nc.sync.dma_start(out=tab2_w[:].bitcast(I32), in_=tab2_words.rearrange("a p t i -> p a (t i)").bitcast(I32))
@@ -178,7 +187,7 @@ def tile_list_tract_county_audit_kernel(
                     x_pass(i, half, 0)
                     x_pass(i, half, 1)
                 dst = x_sb[i][:, BANK * half : BANK * (half + 1)]
-                g_col = g[:, i // PACK, i % PACK : i % PACK + 1]
+                g_col = (g if i < FUSED else g_neg)[:, i // PACK, i % PACK : i % PACK + 1]
                 if (i, half) == (0, 1):
                     nc.vector.tensor_scalar(dst, x_banks[i, half][:], g_col, None, ALU.mult)
                 else:
@@ -188,7 +197,7 @@ def tile_list_tract_county_audit_kernel(
 
         def pick(i):
             picked[i] = stage.tile([P, M], F32, name="picked%d" % i, align_bytes=64,
-                                   offset=PLACE["picked"] + 4 * M * (i % PICK_SLOTS))
+                                   offset=PLACE["picked"] + 4 * M * (i if i < PICK_SLOTS else 3))
             nc.vector.tensor_copy(out=picked[i][:], in_=x_sb[i][:].indirect(pos_sb[:]))
 
         v2_w = {}
@@ -219,7 +228,7 @@ def tile_list_tract_county_audit_kernel(
             nc.vector.quantize_mx(out=w2_w[h, a][:].bitcast(FP8X4), scales=w2_sc[h, a][:],
                                   in_=w2_bf[h, a][:].rearrange("p t m j -> p (t m j)"))
 
-        b_banks = {}
+        b_banks, b_sb = {}, {}
 
         def b_passes(h, a):
             for t in range(PACK):
@@ -240,6 +249,16 @@ def tile_list_tract_county_audit_kernel(
                                            in1=picked[i][:], op0=ALU.mult, op1=ALU.subtract)
             nc.scalar.activation(r[h][:, t, :], e[h][:, t, :], ACT.Square, scale=g_inv[:, h, t : t + 1])
 
+        def b_copy(i):
+            h, t = divmod(i, PACK)
+            b_sb[i] = kept("b_sb%d" % i, [P, M], F32)
+            nc.scalar.activation(b_sb[i][:], b_banks[i][:], ACT.Copy, scale=g[:, h, t : t + 1])
+
+        def pick_diff(i):
+            h, t = divmod(i, PACK)
+            nc.vector.tensor_tensor(e[h][:, t, :], x_sb[i][:].indirect(pos_sb[:]), b_sb[i][:], ALU.add)
+            nc.scalar.activation(r[h][:, t, :], e[h][:, t, :], ACT.Square, scale=g_inv[:, h, t : t + 1])
+
         def root(i):
             h, t = divmod(i, PACK)
             nc.scalar.activation(r[h][:, t, :], r[h][:, t, :], ACT.Abs_reciprocal_sqrt, bias=1.0)
@@ -247,14 +266,14 @@ def tile_list_tract_county_audit_kernel(
         z_bf, z_w, z_sc = {}, {}, {}
 
         def z_round(h, lo, hi):
-            z_bf[h, lo] = kept("z_bf%d_%d" % (h, lo), [P, hi - lo, PACK], BF16)
+            z_bf[h, lo] = placed("z_bf%d_%d" % (h, lo), [P, hi - lo, PACK], BF16)
             nc.vector.tensor_tensor(
                 out=z_bf[h, lo][:].rearrange("p (c i) t -> p c t i", i=2),
                 in0=e[h][:, :, lo:hi].rearrange("p t (c i) -> p c t i", i=2),
                 in1=r[h][:, :, lo:hi].rearrange("p t (c i) -> p c t i", i=2), op=ALU.mult)
 
         def z_quantize(h, lo, hi):
-            z_w[h, lo] = kept("z_w%d_%d" % (h, lo), [P, hi - lo], U32)
+            z_w[h, lo] = placed("z_w%d_%d" % (h, lo), [P, hi - lo], U32)
             z_sc[h, lo] = kept("z_sc%d_%d" % (h, lo), [P, hi - lo], U8)
             nc.vector.quantize_mx(out=z_w[h, lo][:].bitcast(FP8X4), scales=z_sc[h, lo][:],
                                   in_=z_bf[h, lo][:].rearrange("p m t -> p (m t)"))
@@ -262,7 +281,6 @@ def tile_list_tract_county_audit_kernel(
         out_banks = {}
 
         def out_pass(lo, hi, rows, h):
-            first = lo // (M // 2) * (M // 2) if h == 0 else lo
             for n in range(N // P):
                 key = (lo, n // rows)
                 if key not in out_banks:
@@ -270,8 +288,7 @@ def tile_list_tract_county_audit_kernel(
                 nc.tensor.matmul_mx(
                     out=out_banks[key][:, n % rows, :], lhsT=w3_w[:, h, P * n : P * (n + 1)].bitcast(FP8X4),
                     lhsT_scale=planes[h][:, W3 + P * n : W3 + P * (n + 1)],
-                    rhs=z_w[h, first][:, lo - first : hi - first].bitcast(FP8X4),
-                    rhs_scale=z_sc[h, first][:, lo - first : hi - first],
+                    rhs=z_w[h, lo][:].bitcast(FP8X4), rhs_scale=z_sc[h, lo][:],
                     start=(h == 0 and n % rows == 0), stop=(h == 1 and n % rows == rows - 1))
 
         def store(lo, hi, rows, *copies):
@@ -290,15 +307,12 @@ def tile_list_tract_county_audit_kernel(
             x_tile(i)
         pick(0)
         w1_deal(1)
-        g_raw_inv = placed("g_raw_inv", [P, 2, PACK], F32)
-        nc.vector.reciprocal(g_raw_inv[:], g[:])
         w2_round_pool(0, 0)
         for i in range(PACK, 2 * PACK):
             x_tile(i)
         w2_round_pool(0, 1)
         w2_round(1, 0, nc.scalar.copy, nc.scalar.copy)
         pick(1)
-        nc.vector.tensor_scalar(g_inv[:], g_raw_inv[:], BIG, -BIG, ALU.min, ALU.max)
         w2_round_pool(1, 1)
         pick(2)
         w2_quantize(0, 0)
@@ -306,40 +320,45 @@ def tile_list_tract_county_audit_kernel(
         b_passes(0, 0)
         gather2(1)
         pick(3)
+        w2_quantize(0, 1)
+        b_passes(0, 1)
         pick(4)
         w3_w = placed("w3_w", [P, 2, N], U32)
         nc.sync.dma_start(out=w3_w[:].bitcast(I32),
                           in_=w3_words.rearrange("a p c i -> p a (c i)").bitcast(I32))
-        w2_quantize(0, 1)
-        b_passes(0, 1)
-        pick(5)
         diff_tile(0)
-        diff_tile(1)
         root(0)
+        diff_tile(1)
         root(1)
         w2_quantize(1, 0)
         b_passes(1, 0)
         diff_tile(2)
-        diff_tile(3)
         root(2)
+        diff_tile(3)
         root(3)
         w2_quantize(1, 1)
         b_passes(1, 1)
-        pick(6)
-        pick(7)
-        for i in range(PACK, 2 * PACK, 2):
-            diff_tile(i)
-            diff_tile(i + 1)
-            root(i)
-            root(i + 1)
         half = M // 2
         pieces = ((0, half, 2), (half, half + P, 4), (half + P, M, 2))
-        z_round(0, 0, half)
-        z_round(0, half, M)
-        z_quantize(0, 0, half)
+        pick(5)
+        b_copy(6)
+        b_copy(7)
+        diff_tile(4)
+        root(4)
+        diff_tile(5)
+        root(5)
+        pick_diff(6)
+        root(6)
+        pick_diff(7)
+        root(7)
+        z_round(0, *pieces[0][:2])
+        z_round(0, *pieces[1][:2])
+        z_quantize(0, *pieces[0][:2])
         out_pass(*pieces[0], 0)
-        z_quantize(0, half, M)
+        z_round(0, *pieces[2][:2])
+        z_quantize(0, *pieces[1][:2])
         out_pass(*pieces[1], 0)
+        z_quantize(0, *pieces[2][:2])
         out_pass(*pieces[2], 0)
         z_round(1, *pieces[0][:2])
         z_round(1, *pieces[1][:2])

@@ -29,9 +29,9 @@ X_BANKS = 4
 BIG = 1e38
 PLACE = {
     "w1_raw0": 0, "w1_raw1": 0,
-    "w2_raw00": 4 * KIB + 64, "tab_w0": 12 * KIB, "tab2_w": 20 * KIB,
-    "w2_raw01": 38 * KIB + 64, "tab_w1": 46 * KIB, "w2_raw10": 46 * KIB + 64, "w2_raw11": 54 * KIB + 64,
-    "x_sb": 64 * KIB, "w1_w1": 64 * KIB, "g_raw_inv": 67 * KIB, "w3_w": 80 * KIB,
+    "w2_raw00_0": 4 * KIB + 64, "tab_w0": 12 * KIB, "tab2_w": 20 * KIB,
+    "w2_raw01_0": 36 * KIB + 64, "tab_w1": 44 * KIB, "w2_raw10_0": 46 * KIB + 64, "w2_raw11_0": 54 * KIB + 64, "w2_raw11_64": 58 * KIB + 64,
+    "x_sb": 64 * KIB, "w1_w1": 44 * KIB + 64, "w3_w": 80 * KIB,
     "w2_w00": 70 * KIB - 64, "v2_w0": 72 * KIB, "v2_w1": 74 * KIB, "w2_w01": 76 * KIB,
     "picked": 96 * KIB, "z_w0_0": 104 * KIB, "z_w0_256": 103 * KIB, "z_w0_384": 99 * KIB,
     "z_w1_0": 96 * KIB, "z_w1_256": 97 * KIB, "z_w1_384": 98 * KIB,
@@ -70,12 +70,11 @@ def tile_list_tract_county_audit_kernel(
 
         w2_raw = {}
 
-        def w2_load(h, a):
-            tile = placed("w2_raw%d%d" % (h, a), [P, PACK, PASS], F32)
-            nc.sync.dma_start(
-                out=tile[:],
-                in_=w2[PASS * a : PASS * (a + 1), PASS * h : PASS * (h + 1)].rearrange("(p j) c -> p j c", j=PACK))
-            w2_raw[h, a] = tile
+        def w2_load(h, a, lo=0, hi=P):
+            tile = placed("w2_raw%d%d_%d" % (h, a, lo), [P, PACK, PACK * (hi - lo)], F32)
+            cols = slice(PASS * h + PACK * lo, PASS * h + PACK * hi)
+            nc.sync.dma_start(out=tile[:], in_=w2[PASS * a : PASS * (a + 1), cols].rearrange("(p j) c -> p j c", j=PACK))
+            w2_raw[h, a, lo] = tile
 
         offs_sb = lists.tile([P, S // 16], U16, name="offs_sb")
         offs2_sb = lists.tile([P, M // 16], U16, name="offs2_sb")
@@ -162,9 +161,11 @@ def tile_list_tract_county_audit_kernel(
         nc.sync.dma_start(out=tab2_w[:].bitcast(I32), in_=tab2_words.rearrange("a p t i -> p a (t i)").bitcast(I32))
         gather1(1, 0)
         gather1(1, 1)
+        w1_deal(1)
         w2_load(0, 1)
         w2_load(1, 0)
-        w2_load(1, 1)
+        w2_load(1, 1, 0, P // 2)
+        w2_load(1, 1, P // 2, P)
 
         x_banks = {}
         x_sb = [stage.tile([P, S], F32, name="x_sb%d" % i, align_bytes=64, offset=PLACE["x_sb"] + 4 * S * i)
@@ -188,10 +189,7 @@ def tile_list_tract_county_audit_kernel(
                     x_pass(i, half, 1)
                 dst = x_sb[i][:, BANK * half : BANK * (half + 1)]
                 g_col = (g if i < FUSED else g_neg)[:, i // PACK, i % PACK : i % PACK + 1]
-                if (i, half) == (0, 1):
-                    nc.vector.tensor_scalar(dst, x_banks[i, half][:], g_col, None, ALU.mult)
-                else:
-                    nc.scalar.activation(dst, x_banks[i, half][:], ACT.Copy, scale=g_col)
+                nc.scalar.activation(dst, x_banks[i, half][:], ACT.Copy, scale=g_col)
 
         picked = {}
 
@@ -211,15 +209,16 @@ def tile_list_tract_county_audit_kernel(
         def w2_round(h, a, *copies):
             w2_bf[h, a] = placed("w2_bf%d%d" % (h, a), [P, PACK, P, PACK], BF16)
             dst = w2_bf[h, a][:].rearrange("p t m j -> p m j t")
-            src = w2_raw[h, a][:].rearrange("p j (m t) -> p m j t", t=PACK)
+            src = w2_raw[h, a, 0][:].rearrange("p j (m t) -> p m j t", t=PACK)
             for t, copy in zip((0, 2), copies):
                 copy(out=dst[:, :, :, t : t + 2], in_=src[:, :, :, t : t + 2])
 
-        def w2_round_pool(h, a):
-            w2_bf[h, a] = placed("w2_bf%d%d" % (h, a), [P, PACK, P, PACK], BF16)
-            dst = w2_bf[h, a][:].rearrange("p t m j -> p m t j")
-            src = w2_raw[h, a][:].rearrange("p j (m t) -> p m t j", t=PACK)
-            for lo in range(0, P, P // 4):
+        def w2_round_pool(h, a, first=0, last=P):
+            if first == 0:
+                w2_bf[h, a] = placed("w2_bf%d%d" % (h, a), [P, PACK, P, PACK], BF16)
+            dst = w2_bf[h, a][:, :, first:last, :].rearrange("p t m j -> p m t j")
+            src = w2_raw[h, a, first][:].rearrange("p j (m t) -> p m t j", t=PACK)
+            for lo in range(0, last - first, P // 4):
                 nc.gpsimd.tensor_copy(out=dst[:, lo : lo + P // 4], in_=src[:, lo : lo + P // 4])
 
         def w2_quantize(h, a):
@@ -306,14 +305,14 @@ def tile_list_tract_county_audit_kernel(
         for i in range(PACK):
             x_tile(i)
         pick(0)
-        w1_deal(1)
         w2_round_pool(0, 0)
         for i in range(PACK, 2 * PACK):
             x_tile(i)
         w2_round_pool(0, 1)
         w2_round(1, 0, nc.scalar.copy, nc.scalar.copy)
         pick(1)
-        w2_round_pool(1, 1)
+        w2_round_pool(1, 1, 0, P // 2)
+        w2_round_pool(1, 1, P // 2, P)
         pick(2)
         w2_quantize(0, 0)
         gather2(0)
@@ -368,7 +367,7 @@ def tile_list_tract_county_audit_kernel(
         z_round(1, *pieces[2][:2])
         z_quantize(1, *pieces[1][:2])
         out_pass(*pieces[1], 1)
-        store(*pieces[1], nc.scalar.copy)
         z_quantize(1, *pieces[2][:2])
         out_pass(*pieces[2], 1)
-        store(*pieces[2], nc.vector.tensor_copy, nc.scalar.copy)
+        store(*pieces[1], nc.vector.tensor_copy)
+        store(*pieces[2], nc.scalar.copy, nc.vector.tensor_copy)

@@ -33,10 +33,10 @@ PLACE = {
     "w2_raw01_0": 36 * KIB + 64, "tab_w1": 44 * KIB, "w2_raw10_0": 46 * KIB + 64, "w2_raw11_0": 54 * KIB + 64, "w2_raw11_64": 58 * KIB + 64,
     "x_sb": 64 * KIB, "w1_w1": 44 * KIB + 64, "w3_w": 80 * KIB,
     "w2_w00": 70 * KIB - 64, "v2_w0": 72 * KIB, "v2_w1": 74 * KIB, "w2_w01": 76 * KIB,
-    "picked": 96 * KIB, "z_w0_0": 104 * KIB, "z_w0_256": 103 * KIB, "z_w0_384": 99 * KIB,
+    "picked": 96 * KIB, "z_w0_0": 104 * KIB, "z_w0_256": 103 * KIB, "z_w0_384": 138 * KIB, "sq_last": 138 * KIB,
     "z_w1_0": 96 * KIB, "z_w1_256": 97 * KIB, "z_w1_384": 98 * KIB,
     "z_bf0_0": 88 * KIB, "z_bf0_256": 91 * KIB, "z_bf0_384": 90 * KIB,
-    "z_bf1_0": 88 * KIB, "z_bf1_256": 91 * KIB - 512, "z_bf1_384": 91 * KIB + 512,
+    "z_bf1_0": 88 * KIB, "z_bf1_256": 90 * KIB, "z_bf1_384": 88 * KIB,
     "w1_w0": 112 * KIB, "v_w00": 114 * KIB, "v_w01": 116 * KIB, "v_w10": 118 * KIB, "v_w11": 120 * KIB,
     "w2_bf00": 126 * KIB, "w2_bf01": 130 * KIB, "w2_bf10": 118 * KIB, "w2_bf11": 134 * KIB,
     "r0": 46 * KIB + 64, "r1": 4 * KIB + 64, "w2_w10": 122 * KIB, "w2_w11": 124 * KIB,
@@ -253,10 +253,10 @@ def tile_list_tract_county_audit_kernel(
             b_sb[i] = kept("b_sb%d" % i, [P, M], F32)
             nc.scalar.activation(b_sb[i][:], b_banks[i][:], ACT.Copy, scale=g[:, h, t : t + 1])
 
-        def pick_diff(i):
+        def pick_diff(i, square=None):
             h, t = divmod(i, PACK)
             nc.vector.tensor_tensor(e[h][:, t, :], x_sb[i][:].indirect(pos_sb[:]), b_sb[i][:], ALU.add)
-            nc.scalar.activation(r[h][:, t, :], e[h][:, t, :], ACT.Square, scale=g_inv[:, h, t : t + 1])
+            nc.scalar.activation(r[h][:, t, :] if square is None else square, e[h][:, t, :], ACT.Square, scale=g_inv[:, h, t : t + 1])
 
         def root(i):
             h, t = divmod(i, PACK)
@@ -348,8 +348,9 @@ def tile_list_tract_county_audit_kernel(
         root(5)
         pick_diff(6)
         root(6)
-        pick_diff(7)
-        root(7)
+        sq_last = placed("sq_last", [P, M], F32)
+        pick_diff(7, sq_last[:])
+        nc.scalar.activation(r[1][:, PACK - 1, :], sq_last[:], ACT.Abs_reciprocal_sqrt, bias=1.0)
         z_round(0, *pieces[0][:2])
         z_round(0, *pieces[1][:2])
         z_quantize(0, *pieces[0][:2])
@@ -357,13 +358,13 @@ def tile_list_tract_county_audit_kernel(
         z_round(0, *pieces[2][:2])
         z_quantize(0, *pieces[1][:2])
         out_pass(*pieces[1], 0)
-        z_quantize(0, *pieces[2][:2])
-        out_pass(*pieces[2], 0)
         z_round(1, *pieces[0][:2])
-        z_round(1, *pieces[1][:2])
+        z_quantize(0, *pieces[2][:2])
         z_quantize(1, *pieces[0][:2])
         out_pass(*pieces[0], 1)
+        out_pass(*pieces[2], 0)
         store(*pieces[0], nc.scalar.copy, nc.scalar.copy)
+        z_round(1, *pieces[1][:2])
         z_round(1, *pieces[2][:2])
         z_quantize(1, *pieces[1][:2])
         out_pass(*pieces[1], 1)

@@ -90,9 +90,9 @@ def tile_list_tract_county_audit_kernel(
 
         w1_raw, w1_w = {}, {}
 
-        def w1_load(h, queue):
+        def w1_load(h):
             w1_raw[h] = placed("w1_raw%d" % h, [P, 2, 2 * PASS], U8)
-            queue.dma_start(
+            nc.sync.dma_start(
                 out=w1_raw[h][:].bitcast(I32),
                 in_=w1_words[:, :, 2 * PASS * h : 2 * PASS * (h + 1)].bitcast(I32).rearrange("a p c -> p a c"))
 
@@ -102,7 +102,7 @@ def tile_list_tract_county_audit_kernel(
         load_rows(tab2_sc[:LIVE, :], tab2_scales)
         nc.sync.dma_start(offs2_sb[:], offs2)
         load_rows(planes[0][:LIVE, W3:], w3_scales)
-        w1_load(0, nc.sync)
+        w1_load(0)
         tab_w = [load_words(0)]
         nc.sync.dma_start(pos_sb[:], pos1)
         g = kept("g", [P, 2, PACK], F32)
@@ -129,9 +129,8 @@ def tile_list_tract_county_audit_kernel(
         nc.vector.tensor_copy(out=planes[0][:, V2:W3].bitcast(I32), in_=v2_sc_rows[:].bitcast(I32))
         for group in range(1, 8):
             a, q = divmod(group, 4)
-            queue = nc.sync if a else nc.scalar
-            queue.dma_start(out=planes[a][32 * q : 32 * q + 4, :].bitcast(I32),
-                            in_=planes[0][4 * group : 4 * group + 4, :].bitcast(I32))
+            nc.sync.dma_start(out=planes[a][32 * q : 32 * q + 4, :].bitcast(I32),
+                              in_=planes[0][4 * group : 4 * group + 4, :].bitcast(I32))
 
         def w1_deal(h):
             w1_w[h] = placed("w1_w%d" % h, [P, 2, 2 * PASS], U8)
@@ -139,7 +138,7 @@ def tile_list_tract_county_audit_kernel(
                                   in_=w1_raw[h][:].bitcast(U16).rearrange("p a (m t) -> p a t m", t=PACK))
 
         w1_deal(0)
-        w1_load(1, nc.scalar)
+        w1_load(1)
 
         v_w = {}
 

@@ -34,12 +34,12 @@ PLACE = {
     "x_sb": 64 * KIB, "w1_w1": 44 * KIB + 64, "w3_w": 80 * KIB,
     "w2_w00": 70 * KIB - 64, "v2_w0": 72 * KIB, "v2_w1": 74 * KIB, "w2_w01": 76 * KIB,
     "picked": 96 * KIB, "z_w0_0": 104 * KIB, "z_w0_256": 103 * KIB, "z_w0_384": 138 * KIB, "sq_last": 138 * KIB,
-    "z_w1_0": 96 * KIB, "z_w1_256": 97 * KIB, "z_w1_384": 98 * KIB,
+    "z_w1_0": 96 * KIB, "z_w1_256": 97 * KIB, "z_w1_384": 100 * KIB,
     "z_bf0_0": 88 * KIB, "z_bf0_256": 91 * KIB, "z_bf0_384": 90 * KIB,
     "z_bf1_0": 88 * KIB, "z_bf1_256": 90 * KIB, "z_bf1_384": 88 * KIB,
     "w1_w0": 112 * KIB, "v_w00": 114 * KIB, "v_w01": 116 * KIB, "v_w10": 118 * KIB, "v_w11": 120 * KIB,
-    "w2_bf00": 126 * KIB, "w2_bf01": 130 * KIB, "w2_bf10": 118 * KIB, "w2_bf11": 134 * KIB,
-    "r0": 46 * KIB + 64, "r1": 4 * KIB + 64, "w2_w10": 122 * KIB, "w2_w11": 124 * KIB,
+    "w2_bf00": 0, "w2_bf01": 0, "w2_bf10": 118 * KIB, "w2_bf11": 0,
+    "r0": 46 * KIB + 64, "r1": 4 * KIB + 64, "w2_w10": 98 * KIB, "w2_w11": 124 * KIB,
 }
 
 
@@ -328,10 +328,10 @@ def tile_list_tract_county_audit_kernel(
         root(0)
         diff_tile(1)
         root(1)
-        w2_quantize(1, 0)
-        b_passes(1, 0)
         diff_tile(2)
         root(2)
+        w2_quantize(1, 0)
+        b_passes(1, 0)
         diff_tile(3)
         root(3)
         w2_quantize(1, 1)

@@ -1,3 +1,4 @@
+import math
 from contextlib import ExitStack
 
 import concourse.mybir as mybir
@@ -20,27 +21,11 @@ P = 128
 PACK = 4
 PASS = 512
 BANK = 512
-KIB = 1024
-LIVE = 32
-PICK_SLOTS = 5
-EARLY = 2
-FUSED = 6
+ROWS = 32
 X_BANKS = 4
+FUSED = (2, 3)
 BIG = 1e38
-PLACE = {
-    "w1_raw0": 0, "w1_raw1": 0,
-    "w2_raw00_0": 4 * KIB + 64, "tab_w0": 12 * KIB, "tab2_w": 20 * KIB,
-    "w2_raw01_0": 36 * KIB + 64, "tab_w1": 44 * KIB, "w2_raw10_0": 46 * KIB + 64, "w2_raw11_0": 54 * KIB + 64, "w2_raw11_64": 58 * KIB + 64,
-    "x_sb": 64 * KIB, "w1_w1": 44 * KIB + 64, "w3_w": 80 * KIB,
-    "w2_w00": 70 * KIB - 64, "v2_w0": 72 * KIB, "v2_w1": 74 * KIB, "w2_w01": 76 * KIB,
-    "picked": 96 * KIB, "z_w0_0": 104 * KIB, "z_w0_256": 103 * KIB, "z_w0_384": 138 * KIB, "sq_last": 138 * KIB,
-    "z_w1_0": 96 * KIB, "z_w1_256": 97 * KIB, "z_w1_384": 100 * KIB,
-    "z_bf0_0": 88 * KIB, "z_bf0_256": 91 * KIB, "z_bf0_384": 90 * KIB,
-    "z_bf1_0": 88 * KIB, "z_bf1_256": 90 * KIB, "z_bf1_384": 88 * KIB,
-    "w1_w0": 112 * KIB, "v_w00": 114 * KIB, "v_w01": 116 * KIB, "v_w10": 118 * KIB, "v_w11": 120 * KIB,
-    "w2_bf00": 0, "w2_bf01": 0, "w2_bf10": 118 * KIB, "w2_bf11": 0,
-    "r0": 46 * KIB + 64, "r1": 4 * KIB + 64, "w2_w10": 98 * KIB, "w2_w11": 124 * KIB,
-}
+W1, V2, W3, JOINED = S, S + H, S + H + M, S + H + M + N
 
 
 def tile_list_tract_county_audit_kernel(
@@ -50,324 +35,301 @@ def tile_list_tract_county_audit_kernel(
     nc = tc.nc
     with ExitStack() as ctx:
         lists = ctx.enter_context(tc.tile_pool(name="lists", bufs=1))
-        keep = ctx.enter_context(tc.tile_pool(name="keep", bufs=1))
-        stage = ctx.enter_context(tc.tile_pool(name="stage", bufs=1))
+        sbuf = ctx.enter_context(tc.tile_pool(name="sbuf", bufs=1))
         psum = ctx.enter_context(tc.psum_pool(name="psum", bufs=1))
+        width = {F32: 4, U32: 4, BF16: 2, U8: 1}
+        start = {"free": 0}
 
-        def placed(name, shape, dtype):
-            return stage.tile(shape, dtype, name=name, align_bytes=64, offset=PLACE[name])
+        def fresh(name, shape, dtype, room=0):
+            start[name] = start["free"]
+            size = max(room, math.prod(shape[1:]) * width[dtype])
+            start["free"] = start[name] + 256 * math.ceil(size / 256)
+            return sbuf.tile(shape, dtype, name=name, align_bytes=64, offset=start[name])
 
-        def kept(name, shape, dtype):
-            return keep.tile(shape, dtype, name=name, align_bytes=64)
+        def over(earlier, name, shape, dtype, shift=0):
+            start[name] = start[earlier] + shift
+            return sbuf.tile(shape, dtype, name=name, align_bytes=64, offset=start[name])
 
         def bank(index, shape):
             return psum.tile(shape, F32, name="bank", tag="bank%d" % index)
 
-        def load_words(a):
-            tile = placed("tab_w%d" % a, [P, T], U32)
-            nc.sync.dma_start(out=tile[:].bitcast(I32), in_=tab_words[a].rearrange("p t i -> p (t i)").bitcast(I32))
-            return tile
+        def load(tile, dram):
+            nc.sync.dma_start(out=tile.bitcast(I32), in_=dram.bitcast(I32))
 
-        w2_raw = {}
+        def load_rows(rows, dram):
+            nc.sync.dma_start(out=rows.bitcast(I32), in_=dram.bitcast(I32).rearrange("a q c -> q a c"))
 
-        def w2_load(h, a, lo=0, hi=P):
-            tile = placed("w2_raw%d%d_%d" % (h, a, lo), [P, PACK, PACK * (hi - lo)], F32)
-            cols = slice(PASS * h + PACK * lo, PASS * h + PACK * hi)
-            nc.sync.dma_start(out=tile[:], in_=w2[PASS * a : PASS * (a + 1), cols].rearrange("(p j) c -> p j c", j=PACK))
-            w2_raw[h, a, lo] = tile
+        def w1_half(h):
+            return w1_words[:, :, 2 * PASS * h : 2 * PASS * (h + 1)].rearrange("a p c -> p a c")
 
+        def w2_cols(h, a, first, last):
+            cols = slice(PASS * h + PACK * first, PASS * h + PACK * last)
+            return w2[PASS * a : PASS * (a + 1), cols].rearrange("(p j) c -> p j c", j=PACK)
+
+        chunk = 4 * PACK * PASS
         offs_sb = lists.tile([P, S // 16], U16, name="offs_sb")
         offs2_sb = lists.tile([P, M // 16], U16, name="offs2_sb")
         pos_sb = lists.tile([P, M // 16], U16, name="pos_sb")
-        tab_sc = kept("tab_sc", [P, T], U8)
-        w1_sc_raw = kept("w1_sc_raw", [P, H], U8)
-        tab2_sc = kept("tab2_sc", [P, T2], U8)
-        planes = [kept("plane%d" % a, [P, S + H + M + N], U8) for a in range(2)]
-        W1, V2, W3 = S, S + H, S + H + M
+        tab_sc = fresh("tab_sc", [P, T], U8)
+        w1_sc = fresh("w1_sc", [P, H], U8)
+        tab2_sc = fresh("tab2_sc", [P, T2], U8)
+        joined = fresh("joined", [P, JOINED], U8)
+        planes = fresh("planes", [P, 2, JOINED], U8)
+        w1_raw = [fresh("w1_raw0", [P, 2, 2 * PASS], U8, room=chunk)]
+        tab_w = [fresh("tab_w%d" % a, [P, T], U32) for a in range(2)]
+        g = fresh("g", [P, 2, PACK], F32)
 
-        def load_rows(rows, dram):
-            nc.sync.dma_start(out=rows.bitcast(I32), in_=dram.bitcast(I32).rearrange("a q c -> (a q) c"))
-
-        w1_raw, w1_w = {}, {}
-
-        def w1_load(h):
-            w1_raw[h] = placed("w1_raw%d" % h, [P, 2, 2 * PASS], U8)
-            nc.sync.dma_start(
-                out=w1_raw[h][:].bitcast(I32),
-                in_=w1_words[:, :, 2 * PASS * h : 2 * PASS * (h + 1)].bitcast(I32).rearrange("a p c -> p a c"))
-
-        load_rows(tab_sc[:LIVE, :], tab_scales)
+        load_rows(tab_sc[:ROWS, :], tab_scales)
         nc.sync.dma_start(offs_sb[:], offs)
-        load_rows(w1_sc_raw[:LIVE, :], w1_scales)
-        load_rows(tab2_sc[:LIVE, :], tab2_scales)
+        load_rows(w1_sc[:ROWS, :], w1_scales)
+        load_rows(tab2_sc[:ROWS, :], tab2_scales)
         nc.sync.dma_start(offs2_sb[:], offs2)
-        load_rows(planes[0][:LIVE, W3:], w3_scales)
-        w1_load(0)
-        tab_w = [load_words(0)]
+        load_rows(joined[:ROWS, W3:], w3_scales)
+        load(w1_raw[0][:], w1_half(0))
+        load(tab_w[0][:], tab_words[0].rearrange("p t i -> p (t i)"))
         nc.sync.dma_start(pos_sb[:], pos1)
-        g = kept("g", [P, 2, PACK], F32)
         nc.sync.dma_start(out=g[:], in_=gain.rearrange("(a p t) -> p a t", a=2, t=PACK))
-        tab_w.append(load_words(1))
+        load(tab_w[1][:], tab_words[1].rearrange("p t i -> p (t i)"))
 
-        for dead in (slice(32, 64), slice(64, P)):
-            for tile in (tab_sc, w1_sc_raw, tab2_sc, planes[0][:, W3:]):
-                nc.vector.memset(tile[dead, :].bitcast(I32), 0)
-        warm = keep.tile([P, 1], F32, name="warm")
-        warm_out = keep.tile([P, 1], F32, name="warm_out")
+        for tile in (tab_sc, w1_sc, tab2_sc):
+            for idle in (slice(32, 64), slice(64, P)):
+                nc.vector.memset(tile[idle, :].bitcast(I32), 0)
+        warm = fresh("warm", [P, 1], F32)
+        warm_out = fresh("warm_out", [P, 1], F32)
         nc.vector.memset(warm[:], 1.0)
         nc.scalar.activation(warm_out[:], warm[:], ACT.Abs_reciprocal_sqrt, bias=1.0)
-        nc.vector.memset(planes[1][:].bitcast(I32), 0)
+        nc.gpsimd.memset(planes[:].bitcast(I32), 0)
 
-        v_sc_rows = kept("v_sc_rows", [P, S], U8)
-        nc.vector.tensor_copy(out=v_sc_rows[:], in_=tab_sc[:].indirect(offs_sb[:]))
-        nc.vector.tensor_copy(
-            out=planes[0][:, W1:V2].rearrange("p (h t m) -> p h t m", h=2, t=PACK),
-            in_=w1_sc_raw[:].rearrange("p (h m t) -> p h t m", h=2, t=PACK))
-        v2_sc_rows = kept("v2_sc_rows", [P, M], U8)
-        nc.vector.tensor_copy(out=v2_sc_rows[:], in_=tab2_sc[:].indirect(offs2_sb[:]))
-        nc.vector.tensor_copy(out=planes[0][:, :W1].bitcast(I32), in_=v_sc_rows[:].bitcast(I32))
-        nc.vector.tensor_copy(out=planes[0][:, V2:W3].bitcast(I32), in_=v2_sc_rows[:].bitcast(I32))
-        for group in range(1, 8):
-            a, q = divmod(group, 4)
-            nc.sync.dma_start(out=planes[a][32 * q : 32 * q + 4, :].bitcast(I32),
-                              in_=planes[0][4 * group : 4 * group + 4, :].bitcast(I32))
+        nc.gpsimd.tensor_copy(
+            out=joined[:, W1:V2].rearrange("p (h t m) -> p h t m", h=2, t=PACK),
+            in_=w1_sc[:].rearrange("p (h m t) -> p h t m", h=2, t=PACK))
+        v_sc = fresh("v_sc", [P, S], U8)
+        v2_sc = fresh("v2_sc", [P, M], U8, room=4 * PASS)
+        nc.vector.tensor_copy(out=v_sc[:], in_=tab_sc[:].indirect(offs_sb[:]))
+        nc.vector.tensor_copy(out=v2_sc[:], in_=tab2_sc[:].indirect(offs2_sb[:]))
+        nc.vector.tensor_copy(out=joined[:ROWS, :W1].bitcast(I32), in_=v_sc[:ROWS, :].bitcast(I32))
+        nc.vector.tensor_copy(out=joined[:ROWS, V2:W3].bitcast(I32), in_=v2_sc[:ROWS, :].bitcast(I32))
+        for q in range(4):
+            nc.sync.dma_start(out=planes[32 * q : 32 * q + 4, :, :].bitcast(I32),
+                              in_=joined[8 * q : 8 * q + 8, :].bitcast(I32))
 
-        def w1_deal(h):
-            w1_w[h] = placed("w1_w%d" % h, [P, 2, 2 * PASS], U8)
-            nc.vector.tensor_copy(out=w1_w[h][:].bitcast(U16).rearrange("p a (t m) -> p a t m", t=PACK),
+        w1_w = {}
+
+        def w1_deal(h, tile):
+            w1_w[h] = tile
+            nc.vector.tensor_copy(out=tile[:].bitcast(U16).rearrange("p a (t m) -> p a t m", t=PACK),
                                   in_=w1_raw[h][:].bitcast(U16).rearrange("p a (m t) -> p a t m", t=PACK))
 
-        w1_deal(0)
-        w1_load(1)
+        w1_raw.append(over("v2_sc", "w1_raw1", [P, 2, 2 * PASS], U8))
+        load(w1_raw[1][:], w1_half(1))
+        w1_deal(0, over("tab2_sc", "w1_w0", [P, 2, 2 * PASS], U8))
 
         v_w = {}
 
         def gather1(a, half):
-            v_w[a, half] = placed("v_w%d%d" % (a, half), [P, BANK], U32)
+            v_w[a, half] = fresh("v_w%d%d" % (a, half), [P, BANK], U32)
             nc.vector.tensor_copy(out=v_w[a, half][:],
                                   in_=tab_w[a][:].indirect(offs_sb[:, 32 * half : 32 * (half + 1)]))
 
-        g_inv = kept("g_inv", [P, 2, PACK], F32)
-        g_raw_inv = kept("g_raw_inv", [P, 2, PACK], F32)
+        w2_raw = {}
+
+        def w2_load(h, a, earlier, shift=0, first=0, last=P):
+            tile = over(earlier, "w2_raw%d%d_%d" % (h, a, first), [P, PACK, PACK * (last - first)], F32, shift)
+            nc.sync.dma_start(out=tile[:], in_=w2_cols(h, a, first, last))
+            w2_raw[h, a, first] = tile
+
+        tab2_w = {}
+
+        def tab2_load(a, earlier, shift):
+            tab2_w[a] = over(earlier, "tab2_w%d" % a, [P, T2], U32, shift)
+            load(tab2_w[a][:], tab2_words[a].rearrange("p t i -> p (t i)"))
+
+        w2_load(0, 0, "w1_raw0")
         gather1(0, 0)
-        nc.vector.reciprocal(g_raw_inv[:], g[:])
         gather1(0, 1)
-        g_neg = kept("g_neg", [P, 2, PACK], F32)
-        nc.vector.tensor_scalar(g_neg[:], g[:], -1.0, None, ALU.mult)
+        g_raw_inv = fresh("g_raw_inv", [P, 2, PACK], F32)
+        g_inv = fresh("g_inv", [P, 2, PACK], F32)
+        nc.vector.reciprocal(g_raw_inv[:], g[:])
         nc.vector.tensor_scalar(g_inv[:], g_raw_inv[:], BIG, -BIG, ALU.min, ALU.max)
-        w2_load(0, 0)
-        tab2_w = placed("tab2_w", [P, 2, T2], U32)
-        nc.sync.dma_start(out=tab2_w[:].bitcast(I32), in_=tab2_words.rearrange("a p t i -> p a (t i)").bitcast(I32))
+        g_neg = fresh("g_neg", [P, 2, PACK], F32)
+        nc.vector.tensor_scalar(g_neg[:], g[:], -1.0, None, ALU.mult)
+        w2_load(0, 1, "tab_w0")
+        tab2_load(0, "tab_w0", chunk)
         gather1(1, 0)
         gather1(1, 1)
-        w1_deal(1)
-        w2_load(0, 1)
-        w2_load(1, 0)
-        w2_load(1, 1, 0, P // 2)
-        w2_load(1, 1, P // 2, P)
+        tab2_load(1, "tab_w1", 0)
+        w2_load(1, 0, "tab_w1", chunk)
+        w1_deal(1, fresh("w1_w1", [P, 2, 2 * PASS], U8))
 
-        x_banks = {}
-        x_sb = [stage.tile([P, S], F32, name="x_sb%d" % i, align_bytes=64, offset=PLACE["x_sb"] + 4 * S * i)
-                for i in range(2 * PACK)]
-
-        def x_pass(i, half, a):
-            if a == 0:
-                x_banks[i, half] = bank((2 * i + half) % X_BANKS, [P, BANK])
-            cols = slice(BANK * half, BANK * (half + 1))
-            nc.tensor.matmul_mx(
-                out=x_banks[i, half][:],
-                lhsT=w1_w[i // PACK][:, a, 2 * P * (i % PACK) : 2 * P * (i % PACK + 1)].bitcast(FP4X4),
-                lhsT_scale=planes[a][:, W1 + P * i : W1 + P * (i + 1)],
-                rhs=v_w[a, half][:].bitcast(FP8X4), rhs_scale=planes[a][:, cols],
-                start=(a == 0), stop=(a == 1))
+        x_sb = [fresh("x_sb%d" % i, [P, S], F32) for i in range(2 * PACK)]
 
         def x_tile(i):
+            banks = [bank((2 * i + half) % X_BANKS, [P, BANK]) for half in range(2)]
+            for a in range(2):
+                for half in range(2):
+                    nc.tensor.matmul_mx(
+                        out=banks[half][:],
+                        lhsT=w1_w[i // PACK][:, a, 2 * P * (i % PACK) : 2 * P * (i % PACK + 1)].bitcast(FP4X4),
+                        lhsT_scale=planes[:, a, W1 + P * i : W1 + P * (i + 1)],
+                        rhs=v_w[a, half][:].bitcast(FP8X4),
+                        rhs_scale=planes[:, a, BANK * half : BANK * (half + 1)],
+                        start=(a == 0), stop=(a == 1))
             for half in range(2):
-                if i >= EARLY:
-                    x_pass(i, half, 0)
-                    x_pass(i, half, 1)
-                dst = x_sb[i][:, BANK * half : BANK * (half + 1)]
-                g_col = (g if i < FUSED else g_neg)[:, i // PACK, i % PACK : i % PACK + 1]
-                nc.scalar.activation(dst, x_banks[i, half][:], ACT.Copy, scale=g_col)
+                nc.scalar.activation(x_sb[i][:, BANK * half : BANK * (half + 1)], banks[half][:], ACT.Copy,
+                                     scale=(g_neg if i in FUSED else g)[:, i // PACK, i % PACK : i % PACK + 1])
 
         picked = {}
 
-        def pick(i):
-            picked[i] = stage.tile([P, M], F32, name="picked%d" % i, align_bytes=64,
-                                   offset=PLACE["picked"] + 4 * M * (i if i < PICK_SLOTS else 3))
+        def pick(i, earlier=None, shift=0):
+            name = "picked%d" % i
+            picked[i] = over(earlier, name, [P, M], F32, shift) if earlier else fresh(name, [P, M], F32)
             nc.vector.tensor_copy(out=picked[i][:], in_=x_sb[i][:].indirect(pos_sb[:]))
 
         v2_w = {}
 
-        def gather2(a):
-            v2_w[a] = placed("v2_w%d" % a, [P, M], U32)
-            nc.vector.tensor_copy(out=v2_w[a][:], in_=tab2_w[:, a, :].indirect(offs2_sb[:]))
+        def gather2(a, tile):
+            v2_w[a] = tile
+            nc.vector.tensor_copy(out=v2_w[a][:], in_=tab2_w[a][:].indirect(offs2_sb[:]))
 
-        w2_bf, w2_w, w2_sc = {}, {}, {}
-
-        def w2_round(h, a, *copies):
-            w2_bf[h, a] = placed("w2_bf%d%d" % (h, a), [P, PACK, P, PACK], BF16)
-            dst = w2_bf[h, a][:].rearrange("p t m j -> p m j t")
-            src = w2_raw[h, a, 0][:].rearrange("p j (m t) -> p m j t", t=PACK)
-            for t, copy in zip((0, 2), copies):
+        def w2_round(copy, rounded, h, a, first=0, last=P):
+            dst = rounded[:, :, first:last, :].rearrange("p t m j -> p m j t")
+            src = w2_raw[h, a, first][:].rearrange("p j (m t) -> p m j t", t=PACK)
+            for t in (0, 2):
                 copy(out=dst[:, :, :, t : t + 2], in_=src[:, :, :, t : t + 2])
 
-        def w2_round_pool(h, a, first=0, last=P):
-            if first == 0:
-                w2_bf[h, a] = placed("w2_bf%d%d" % (h, a), [P, PACK, P, PACK], BF16)
-            dst = w2_bf[h, a][:, :, first:last, :].rearrange("p t m j -> p m t j")
-            src = w2_raw[h, a, first][:].rearrange("p j (m t) -> p m t j", t=PACK)
-            for lo in range(0, last - first, P // 4):
-                nc.gpsimd.tensor_copy(out=dst[:, lo : lo + P // 4], in_=src[:, lo : lo + P // 4])
+        def w2_round_pool(rounded, h, a):
+            nc.gpsimd.tensor_copy(out=rounded.rearrange("p t m j -> p m t j"),
+                                  in_=w2_raw[h, a, 0][:].rearrange("p j (m t) -> p m t j", t=PACK))
 
-        def w2_quantize(h, a):
-            w2_w[h, a] = placed("w2_w%d%d" % (h, a), [P, PASS], U32)
-            w2_sc[h, a] = kept("w2_sc%d%d" % (h, a), [P, PASS], U8)
-            nc.vector.quantize_mx(out=w2_w[h, a][:].bitcast(FP8X4), scales=w2_sc[h, a][:],
-                                  in_=w2_bf[h, a][:].rearrange("p t m j -> p (t m j)"))
+        def quantize(name, values, columns, earlier=None, shift=0):
+            shape = [P, columns]
+            words = over(earlier, name + "_w", shape, U32, shift) if earlier else fresh(name + "_w", shape, U32)
+            scales = fresh(name + "_sc", [P, columns], U8)
+            nc.vector.quantize_mx(out=words[:].bitcast(FP8X4), scales=scales[:], in_=values)
+            return words, scales
 
-        b_banks, b_sb = {}, {}
+        b_banks = {}
 
-        def b_passes(h, a):
+        def b_passes(h, a, words, scales):
             for t in range(PACK):
                 if a == 0:
                     b_banks[PACK * h + t] = bank(PACK * (1 - h) + t, [P, M])
                 cols = slice(P * t, P * (t + 1))
                 nc.tensor.matmul_mx(
-                    out=b_banks[PACK * h + t][:],
-                    lhsT=w2_w[h, a][:, cols].bitcast(FP8X4), lhsT_scale=w2_sc[h, a][:, cols],
-                    rhs=v2_w[a][:].bitcast(FP8X4), rhs_scale=planes[a][:, V2:W3], start=(a == 0), stop=(a == 1))
+                    out=b_banks[PACK * h + t][:], lhsT=words[:, cols].bitcast(FP8X4), lhsT_scale=scales[:, cols],
+                    rhs=v2_w[a][:].bitcast(FP8X4), rhs_scale=planes[:, a, V2:W3], start=(a == 0), stop=(a == 1))
 
-        e = [kept("e%d" % h, [P, PACK, M], F32) for h in range(2)]
-        r = [placed("r%d" % h, [P, PACK, M], F32) for h in range(2)]
+        e = [fresh("e%d" % h, [P, PACK, M], F32) for h in range(2)]
+        r = {}
 
-        def diff_tile(i):
+        def diff(i):
             h, t = divmod(i, PACK)
             nc.vector.scalar_tensor_tensor(out=e[h][:, t, :], in0=b_banks[i][:], scalar=g[:, h, t : t + 1],
                                            in1=picked[i][:], op0=ALU.mult, op1=ALU.subtract)
-            nc.scalar.activation(r[h][:, t, :], e[h][:, t, :], ACT.Square, scale=g_inv[:, h, t : t + 1])
 
-        def b_copy(i):
+        def pick_diff(i, b_sb):
             h, t = divmod(i, PACK)
-            b_sb[i] = kept("b_sb%d" % i, [P, M], F32)
-            nc.scalar.activation(b_sb[i][:], b_banks[i][:], ACT.Copy, scale=g[:, h, t : t + 1])
+            nc.scalar.activation(b_sb[:], b_banks[i][:], ACT.Copy, scale=g[:, h, t : t + 1])
+            nc.vector.tensor_tensor(e[h][:, t, :], x_sb[i][:].indirect(pos_sb[:]), b_sb[:], ALU.add)
 
-        def pick_diff(i, square=None):
-            h, t = divmod(i, PACK)
-            nc.vector.tensor_tensor(e[h][:, t, :], x_sb[i][:].indirect(pos_sb[:]), b_sb[i][:], ALU.add)
-            nc.scalar.activation(r[h][:, t, :] if square is None else square, e[h][:, t, :], ACT.Square, scale=g_inv[:, h, t : t + 1])
+        def roots(h, lo, hi, tile):
+            r[h, lo] = tile
+            for t in range(PACK):
+                nc.scalar.activation(tile[:, t, :], e[h][:, t, lo:hi], ACT.Square, scale=g_inv[:, h, t : t + 1])
+                if t % 2:
+                    nc.scalar.activation(tile[:, t - 1 : t + 1, :], tile[:, t - 1 : t + 1, :],
+                                         ACT.Abs_reciprocal_sqrt, bias=1.0)
 
-        def root(i):
-            h, t = divmod(i, PACK)
-            nc.scalar.activation(r[h][:, t, :], r[h][:, t, :], ACT.Abs_reciprocal_sqrt, bias=1.0)
-
-        z_bf, z_w, z_sc = {}, {}, {}
-
-        def z_round(h, lo, hi):
-            z_bf[h, lo] = placed("z_bf%d_%d" % (h, lo), [P, hi - lo, PACK], BF16)
+        def z_round(h, lo, hi, roots_from, earlier=None):
+            name = "z_bf%d_%d" % (h, lo)
+            shape = [P, hi - lo, PACK]
+            z_bf = over(earlier, name, shape, BF16) if earlier else fresh(name, shape, BF16)
             nc.vector.tensor_tensor(
-                out=z_bf[h, lo][:].rearrange("p (c i) t -> p c t i", i=2),
+                out=z_bf[:].rearrange("p (c i) t -> p c t i", i=2),
                 in0=e[h][:, :, lo:hi].rearrange("p t (c i) -> p c t i", i=2),
-                in1=r[h][:, :, lo:hi].rearrange("p t (c i) -> p c t i", i=2), op=ALU.mult)
-
-        def z_quantize(h, lo, hi):
-            z_w[h, lo] = placed("z_w%d_%d" % (h, lo), [P, hi - lo], U32)
-            z_sc[h, lo] = kept("z_sc%d_%d" % (h, lo), [P, hi - lo], U8)
-            nc.vector.quantize_mx(out=z_w[h, lo][:].bitcast(FP8X4), scales=z_sc[h, lo][:],
-                                  in_=z_bf[h, lo][:].rearrange("p m t -> p (m t)"))
+                in1=r[h, roots_from][:, :, lo - roots_from : hi - roots_from].rearrange("p t (c i) -> p c t i", i=2),
+                op=ALU.mult)
+            return z_bf[:].rearrange("p m t -> p (m t)")
 
         out_banks = {}
 
-        def out_pass(lo, hi, rows, h):
+        def out_passes(lo, hi, rows, h, words, scales):
             for n in range(N // P):
                 key = (lo, n // rows)
                 if key not in out_banks:
                     out_banks[key] = bank((PACK + len(out_banks)) % 8, [P, rows, hi - lo])
                 nc.tensor.matmul_mx(
                     out=out_banks[key][:, n % rows, :], lhsT=w3_w[:, h, P * n : P * (n + 1)].bitcast(FP8X4),
-                    lhsT_scale=planes[h][:, W3 + P * n : W3 + P * (n + 1)],
-                    rhs=z_w[h, lo][:].bitcast(FP8X4), rhs_scale=z_sc[h, lo][:],
+                    lhsT_scale=planes[:, h, W3 + P * n : W3 + P * (n + 1)],
+                    rhs=words.bitcast(FP8X4), rhs_scale=scales,
                     start=(h == 0 and n % rows == 0), stop=(h == 1 and n % rows == rows - 1))
 
         def store(lo, hi, rows, *copies):
             for group, copy in enumerate(copies):
-                res = keep.tile([P, rows, hi - lo], F32, name="res%d_%d" % (lo, group))
+                res = fresh("res%d_%d" % (lo, group), [P, rows, hi - lo], F32)
                 copy(out=res[:], in_=out_banks[lo, group][:])
                 nc.sync.dma_start(
                     out=out[P * rows * group : P * rows * (group + 1), lo:hi].rearrange("(n p) m -> p n m", p=P),
                     in_=res[:])
 
+        first_bf = fresh("first_bf", [P, 2, PACK, P, PACK], BF16)
+        w2_round_pool(first_bf[:, 0], 0, 0)
+        w2_load(1, 1, "w2_raw00_0", 0, 0, P // 2)
+        w2_load(1, 1, "w2_raw00_0", chunk // 2, P // 2, P)
+        w2_round_pool(first_bf[:, 1], 0, 1)
+        w3_w = over("w2_raw01_0", "w3_w", [P, 2, N], U32)
+        load(w3_w[:], w3_words.rearrange("a p c i -> p a (c i)"))
+
+        for i in (0, 1, 4, 5):
+            x_tile(i)
+            pick(i)
+        x_tile(6)
+        gather2(0, fresh("v2_w0", [P, M], U32))
+        words, scales = quantize("w2_first", first_bf[:].rearrange("p a t m j -> p (a t m j)"), 2 * PASS)
+        gather2(1, over("first_bf", "v2_w1", [P, M], U32, chunk // 2))
+        pick(6, "first_bf", 3 * chunk // 4)
         for a in range(2):
-            for i in range(EARLY):
-                for half in range(2):
-                    x_pass(i, half, a)
-        for i in range(PACK):
+            b_passes(0, a, words[:, PASS * a : PASS * (a + 1)], scales[:, PASS * a : PASS * (a + 1)])
+        for i in (2, 3, 7):
             x_tile(i)
-        pick(0)
-        w2_round_pool(0, 0)
+
+        third_bf = over("first_bf", "third_bf", [P, PACK, P, PACK], BF16)
+        w2_round_pool(third_bf[:], 1, 0)
+        last_bf = fresh("last_bf", [P, PACK, P, PACK], BF16)
+        w2_round(nc.scalar.copy, last_bf[:], 1, 1, 0, P // 2)
+        w2_round(nc.scalar.copy, last_bf[:], 1, 1, P // 2, P)
+        diff(0)
+        diff(1)
+        pick_diff(2, fresh("b_sb2", [P, M], F32))
+        words, scales = quantize("w2_third", third_bf[:].rearrange("p t m j -> p (t m j)"), PASS, "picked1")
+        b_passes(1, 0, words[:], scales[:])
+        words, scales = quantize("w2_last", last_bf[:].rearrange("p t m j -> p (t m j)"), PASS, "third_bf", chunk // 4)
+        b_passes(1, 1, words[:], scales[:])
+        pick_diff(3, over("third_bf", "b_sb3", [P, M], F32))
+        pick(7, "last_bf")
+        roots(0, 0, M, over("w2_raw11_0", "r0", [P, PACK, M], F32))
         for i in range(PACK, 2 * PACK):
-            x_tile(i)
-        w2_round_pool(0, 1)
-        w2_round(1, 0, nc.scalar.copy, nc.scalar.copy)
-        pick(1)
-        w2_round_pool(1, 1, 0, P // 2)
-        w2_round_pool(1, 1, P // 2, P)
-        pick(2)
-        w2_quantize(0, 0)
-        gather2(0)
-        b_passes(0, 0)
-        gather2(1)
-        pick(3)
-        w2_quantize(0, 1)
-        b_passes(0, 1)
-        pick(4)
-        w3_w = placed("w3_w", [P, 2, N], U32)
-        nc.sync.dma_start(out=w3_w[:].bitcast(I32),
-                          in_=w3_words.rearrange("a p c i -> p a (c i)").bitcast(I32))
-        diff_tile(0)
-        root(0)
-        diff_tile(1)
-        root(1)
-        diff_tile(2)
-        root(2)
-        w2_quantize(1, 0)
-        b_passes(1, 0)
-        diff_tile(3)
-        root(3)
-        w2_quantize(1, 1)
-        b_passes(1, 1)
+            diff(i)
+
         half = M // 2
-        pieces = ((0, half, 2), (half, half + P, 4), (half + P, M, 2))
-        pick(5)
-        b_copy(6)
-        b_copy(7)
-        diff_tile(4)
-        root(4)
-        diff_tile(5)
-        root(5)
-        pick_diff(6)
-        root(6)
-        sq_last = placed("sq_last", [P, M], F32)
-        pick_diff(7, sq_last[:])
-        nc.scalar.activation(r[1][:, PACK - 1, :], sq_last[:], ACT.Abs_reciprocal_sqrt, bias=1.0)
-        z_round(0, *pieces[0][:2])
-        z_round(0, *pieces[1][:2])
-        z_quantize(0, *pieces[0][:2])
-        out_pass(*pieces[0], 0)
-        z_round(0, *pieces[2][:2])
-        z_quantize(0, *pieces[1][:2])
-        out_pass(*pieces[1], 0)
-        z_round(1, *pieces[0][:2])
-        z_quantize(0, *pieces[2][:2])
-        z_quantize(1, *pieces[0][:2])
-        out_pass(*pieces[0], 1)
-        out_pass(*pieces[2], 0)
-        store(*pieces[0], nc.scalar.copy, nc.scalar.copy)
-        z_round(1, *pieces[1][:2])
-        z_round(1, *pieces[2][:2])
-        z_quantize(1, *pieces[1][:2])
-        out_pass(*pieces[1], 1)
-        z_quantize(1, *pieces[2][:2])
-        out_pass(*pieces[2], 1)
-        store(*pieces[1], nc.vector.tensor_copy)
-        store(*pieces[2], nc.scalar.copy, nc.vector.tensor_copy)
+        for lo in (0, half):
+            roots(1, lo, lo + half, fresh("r1_%d" % lo, [P, PACK, half], F32))
+
+        low = [z_round(h, 0, half, 0) for h in range(2)]
+        for h in range(2):
+            words, scales = quantize("z_low%d" % h, low[h], half)
+            out_passes(0, half, 2, h, words[:], scales[:])
+        store(0, half, 2, nc.scalar.copy, nc.scalar.copy)
+
+        pieces = ((half, half + P, 4), (half + P, M, 2))
+        high = z_round(0, half, M, 0, "z_bf0_0")
+        last = [z_round(1, half, half + P, half)]
+        words, scales = quantize("z_high", high, half)
+        for lo, hi, rows in pieces:
+            out_passes(lo, hi, rows, 0, words[:, lo - half : hi - half], scales[:, lo - half : hi - half])
+        last.append(z_round(1, half + P, M, half))
+        copies = ((nc.scalar.copy,), (nc.scalar.copy, nc.vector.tensor_copy))
+        for (lo, hi, rows), values, copy in zip(pieces, last, copies):
+            words, scales = quantize("z_last%d" % lo, values, hi - lo)
+            out_passes(lo, hi, rows, 1, words[:], scales[:])
+            store(lo, hi, rows, *copy)

@@ -57,7 +57,7 @@ def tile_list_tract_county_audit_kernel(
             nc.sync.dma_start(out=tile.bitcast(I32), in_=dram.bitcast(I32))
 
         def load_rows(rows, dram):
-            nc.sync.dma_start(out=rows.bitcast(I32), in_=dram.bitcast(I32).rearrange("a q c -> q a c"))
+            nc.sync.dma_start(out=rows.bitcast(I32), in_=dram.bitcast(I32).rearrange("a q c -> (a q) c"))
 
         def w1_half(h):
             return w1_words[:, :, 2 * PASS * h : 2 * PASS * (h + 1)].rearrange("a p c -> p a c")
@@ -73,8 +73,8 @@ def tile_list_tract_county_audit_kernel(
         tab_sc = fresh("tab_sc", [P, T], U8)
         w1_sc = fresh("w1_sc", [P, H], U8)
         tab2_sc = fresh("tab2_sc", [P, T2], U8)
-        joined = fresh("joined", [P, JOINED], U8)
-        planes = fresh("planes", [P, 2, JOINED], U8)
+        planes = [fresh("plane%d" % a, [P, JOINED], U8) for a in range(2)]
+        joined = planes[0]
         w1_raw = [fresh("w1_raw0", [P, 2, 2 * PASS], U8, room=chunk)]
         tab_w = [fresh("tab_w%d" % a, [P, T], U32) for a in range(2)]
         g = fresh("g", [P, 2, PACK], F32)
@@ -91,14 +91,16 @@ def tile_list_tract_county_audit_kernel(
         nc.sync.dma_start(out=g[:], in_=gain.rearrange("(a p t) -> p a t", a=2, t=PACK))
         load(tab_w[1][:], tab_words[1].rearrange("p t i -> p (t i)"))
 
-        for tile in (tab_sc, w1_sc, tab2_sc):
-            for idle in (slice(32, 64), slice(64, P)):
+        for idle in (slice(32, 64), slice(64, P)):
+            for tile in (tab_sc, tab2_sc):
                 nc.vector.memset(tile[idle, :].bitcast(I32), 0)
+            for tile in (w1_sc, joined[:, W3:]):
+                nc.gpsimd.memset(tile[idle, :].bitcast(I32), 0)
         warm = fresh("warm", [P, 1], F32)
         warm_out = fresh("warm_out", [P, 1], F32)
         nc.vector.memset(warm[:], 1.0)
         nc.scalar.activation(warm_out[:], warm[:], ACT.Abs_reciprocal_sqrt, bias=1.0)
-        nc.gpsimd.memset(planes[:].bitcast(I32), 0)
+        nc.gpsimd.memset(planes[1][:].bitcast(I32), 0)
 
         nc.gpsimd.tensor_copy(
             out=joined[:, W1:V2].rearrange("p (h t m) -> p h t m", h=2, t=PACK),
@@ -107,11 +109,12 @@ def tile_list_tract_county_audit_kernel(
         v2_sc = fresh("v2_sc", [P, M], U8, room=4 * PASS)
         nc.vector.tensor_copy(out=v_sc[:], in_=tab_sc[:].indirect(offs_sb[:]))
         nc.vector.tensor_copy(out=v2_sc[:], in_=tab2_sc[:].indirect(offs2_sb[:]))
-        nc.vector.tensor_copy(out=joined[:ROWS, :W1].bitcast(I32), in_=v_sc[:ROWS, :].bitcast(I32))
-        nc.vector.tensor_copy(out=joined[:ROWS, V2:W3].bitcast(I32), in_=v2_sc[:ROWS, :].bitcast(I32))
-        for q in range(4):
-            nc.sync.dma_start(out=planes[32 * q : 32 * q + 4, :, :].bitcast(I32),
-                              in_=joined[8 * q : 8 * q + 8, :].bitcast(I32))
+        nc.vector.tensor_copy(out=joined[:, :W1].bitcast(I32), in_=v_sc[:].bitcast(I32))
+        nc.vector.tensor_copy(out=joined[:, V2:W3].bitcast(I32), in_=v2_sc[:].bitcast(I32))
+        for group in range(1, 8):
+            a, q = divmod(group, 4)
+            nc.sync.dma_start(out=planes[a][32 * q : 32 * q + 4, :].bitcast(I32),
+                              in_=joined[4 * group : 4 * group + 4, :].bitcast(I32))
 
         w1_w = {}
 
@@ -170,9 +173,9 @@ def tile_list_tract_county_audit_kernel(
                     nc.tensor.matmul_mx(
                         out=banks[half][:],
                         lhsT=w1_w[i // PACK][:, a, 2 * P * (i % PACK) : 2 * P * (i % PACK + 1)].bitcast(FP4X4),
-                        lhsT_scale=planes[:, a, W1 + P * i : W1 + P * (i + 1)],
+                        lhsT_scale=planes[a][:, W1 + P * i : W1 + P * (i + 1)],
                         rhs=v_w[a, half][:].bitcast(FP8X4),
-                        rhs_scale=planes[:, a, BANK * half : BANK * (half + 1)],
+                        rhs_scale=planes[a][:, BANK * half : BANK * (half + 1)],
                         start=(a == 0), stop=(a == 1))
             for half in range(2):
                 nc.scalar.activation(x_sb[i][:, BANK * half : BANK * (half + 1)], banks[half][:], ACT.Copy,
@@ -217,7 +220,7 @@ def tile_list_tract_county_audit_kernel(
                 cols = slice(P * t, P * (t + 1))
                 nc.tensor.matmul_mx(
                     out=b_banks[PACK * h + t][:], lhsT=words[:, cols].bitcast(FP8X4), lhsT_scale=scales[:, cols],
-                    rhs=v2_w[a][:].bitcast(FP8X4), rhs_scale=planes[:, a, V2:W3], start=(a == 0), stop=(a == 1))
+                    rhs=v2_w[a][:].bitcast(FP8X4), rhs_scale=planes[a][:, V2:W3], start=(a == 0), stop=(a == 1))
 
         e = [fresh("e%d" % h, [P, PACK, M], F32) for h in range(2)]
         r = {}
@@ -260,7 +263,7 @@ def tile_list_tract_county_audit_kernel(
                     out_banks[key] = bank((PACK + len(out_banks)) % 8, [P, rows, hi - lo])
                 nc.tensor.matmul_mx(
                     out=out_banks[key][:, n % rows, :], lhsT=w3_w[:, h, P * n : P * (n + 1)].bitcast(FP8X4),
-                    lhsT_scale=planes[:, h, W3 + P * n : W3 + P * (n + 1)],
+                    lhsT_scale=planes[h][:, W3 + P * n : W3 + P * (n + 1)],
                     rhs=words.bitcast(FP8X4), rhs_scale=scales,
                     start=(h == 0 and n % rows == 0), stop=(h == 1 and n % rows == rows - 1))
 

@@ -23,7 +23,7 @@ PASS = 512
 BANK = 512
 ROWS = 32
 X_BANKS = 4
-FUSED = (2, 3)
+POOL_PIECE = P // 4
 BIG = 1e38
 W1, V2, W3, JOINED = S, S + H, S + H + M, S + H + M + N
 
@@ -77,6 +77,7 @@ def tile_list_tract_county_audit_kernel(
         joined = planes[0]
         w1_raw = [fresh("w1_raw0", [P, 2, 2 * PASS], U8, room=chunk)]
         tab_w = [fresh("tab_w%d" % a, [P, T], U32) for a in range(2)]
+        first_bf = fresh("first_bf", [P, PACK, P, PACK], BF16)
         g = fresh("g", [P, 2, PACK], F32)
 
         load_rows(tab_sc[:ROWS, :], tab_scales)
@@ -154,13 +155,11 @@ def tile_list_tract_county_audit_kernel(
         g_inv = fresh("g_inv", [P, 2, PACK], F32)
         nc.vector.reciprocal(g_raw_inv[:], g[:])
         nc.vector.tensor_scalar(g_inv[:], g_raw_inv[:], BIG, -BIG, ALU.min, ALU.max)
-        g_neg = fresh("g_neg", [P, 2, PACK], F32)
-        nc.vector.tensor_scalar(g_neg[:], g[:], -1.0, None, ALU.mult)
-        w2_load(0, 1, "tab_w0")
-        tab2_load(0, "tab_w0", chunk)
+        tab2_load(0, "tab_w0", 0)
+        tab2_load(1, "tab_w0", chunk)
         gather1(1, 0)
         gather1(1, 1)
-        tab2_load(1, "tab_w1", 0)
+        w2_load(0, 1, "tab_w1")
         w2_load(1, 0, "tab_w1", chunk)
         w1_deal(1, fresh("w1_w1", [P, 2, 2 * PASS], U8))
 
@@ -179,7 +178,7 @@ def tile_list_tract_county_audit_kernel(
                         start=(a == 0), stop=(a == 1))
             for half in range(2):
                 nc.scalar.activation(x_sb[i][:, BANK * half : BANK * (half + 1)], banks[half][:], ACT.Copy,
-                                     scale=(g_neg if i in FUSED else g)[:, i // PACK, i % PACK : i % PACK + 1])
+                                     scale=g[:, i // PACK, i % PACK : i % PACK + 1])
 
         picked = {}
 
@@ -194,15 +193,17 @@ def tile_list_tract_county_audit_kernel(
             v2_w[a] = tile
             nc.vector.tensor_copy(out=v2_w[a][:], in_=tab2_w[a][:].indirect(offs2_sb[:]))
 
-        def w2_round(copy, rounded, h, a, first=0, last=P):
-            dst = rounded[:, :, first:last, :].rearrange("p t m j -> p m j t")
-            src = w2_raw[h, a, first][:].rearrange("p j (m t) -> p m j t", t=PACK)
+        def w2_round_scalar(rounded, raw):
+            dst = rounded.rearrange("p t m j -> p m j t")
+            src = raw.rearrange("p j (m t) -> p m j t", t=PACK)
             for t in (0, 2):
-                copy(out=dst[:, :, :, t : t + 2], in_=src[:, :, :, t : t + 2])
+                nc.scalar.copy(out=dst[:, :, :, t : t + 2], in_=src[:, :, :, t : t + 2])
 
-        def w2_round_pool(rounded, h, a):
-            nc.gpsimd.tensor_copy(out=rounded.rearrange("p t m j -> p m t j"),
-                                  in_=w2_raw[h, a, 0][:].rearrange("p j (m t) -> p m t j", t=PACK))
+        def w2_round_pool(rounded, raw):
+            dst = rounded.rearrange("p t m j -> p m t j")
+            src = raw.rearrange("p j (m t) -> p m t j", t=PACK)
+            for lo in range(0, dst.shape[1], POOL_PIECE):
+                nc.gpsimd.tensor_copy(out=dst[:, lo : lo + POOL_PIECE], in_=src[:, lo : lo + POOL_PIECE])
 
         def quantize(name, values, columns, earlier=None, shift=0):
             shape = [P, columns]
@@ -229,29 +230,15 @@ def tile_list_tract_county_audit_kernel(
             h, t = divmod(i, PACK)
             nc.vector.scalar_tensor_tensor(out=e[h][:, t, :], in0=b_banks[i][:], scalar=g[:, h, t : t + 1],
                                            in1=picked[i][:], op0=ALU.mult, op1=ALU.subtract)
+            nc.scalar.activation(r[h][:, t, :], e[h][:, t, :], ACT.Square, scale=g_inv[:, h, t : t + 1])
+            nc.scalar.activation(r[h][:, t, :], r[h][:, t, :], ACT.Abs_reciprocal_sqrt, bias=1.0)
 
-        def pick_diff(i, b_sb):
-            h, t = divmod(i, PACK)
-            nc.scalar.activation(b_sb[:], b_banks[i][:], ACT.Copy, scale=g[:, h, t : t + 1])
-            nc.vector.tensor_tensor(e[h][:, t, :], x_sb[i][:].indirect(pos_sb[:]), b_sb[:], ALU.add)
-
-        def roots(h, lo, hi, tile):
-            r[h, lo] = tile
-            for t in range(PACK):
-                nc.scalar.activation(tile[:, t, :], e[h][:, t, lo:hi], ACT.Square, scale=g_inv[:, h, t : t + 1])
-                if t % 2:
-                    nc.scalar.activation(tile[:, t - 1 : t + 1, :], tile[:, t - 1 : t + 1, :],
-                                         ACT.Abs_reciprocal_sqrt, bias=1.0)
-
-        def z_round(h, lo, hi, roots_from, earlier=None):
-            name = "z_bf%d_%d" % (h, lo)
-            shape = [P, hi - lo, PACK]
-            z_bf = over(earlier, name, shape, BF16) if earlier else fresh(name, shape, BF16)
+        def z_round(h, lo, hi):
+            z_bf = fresh("z_bf%d_%d" % (h, lo), [P, hi - lo, PACK], BF16)
             nc.vector.tensor_tensor(
                 out=z_bf[:].rearrange("p (c i) t -> p c t i", i=2),
                 in0=e[h][:, :, lo:hi].rearrange("p t (c i) -> p c t i", i=2),
-                in1=r[h, roots_from][:, :, lo - roots_from : hi - roots_from].rearrange("p t (c i) -> p c t i", i=2),
-                op=ALU.mult)
+                in1=r[h][:, :, lo:hi].rearrange("p t (c i) -> p c t i", i=2), op=ALU.mult)
             return z_bf[:].rearrange("p m t -> p (m t)")
 
         out_banks = {}
@@ -275,64 +262,57 @@ def tile_list_tract_county_audit_kernel(
                     out=out[P * rows * group : P * rows * (group + 1), lo:hi].rearrange("(n p) m -> p n m", p=P),
                     in_=res[:])
 
-        first_bf = fresh("first_bf", [P, 2, PACK, P, PACK], BF16)
-        w2_round_pool(first_bf[:, 0], 0, 0)
+        def w2_quantize(h, a, rounded, *earlier):
+            words, scales = quantize("w2_%d%d" % (h, a), rounded[:].rearrange("p t m j -> p (t m j)"), PASS, *earlier)
+            b_passes(h, a, words[:], scales[:])
+
+        rounded_shape = [P, PACK, P, PACK]
+        w2_round_pool(first_bf[:], w2_raw[0, 0, 0][:])
         w2_load(1, 1, "w2_raw00_0", 0, 0, P // 2)
         w2_load(1, 1, "w2_raw00_0", chunk // 2, P // 2, P)
-        w2_round_pool(first_bf[:, 1], 0, 1)
-        w3_w = over("w2_raw01_0", "w3_w", [P, 2, N], U32)
-        load(w3_w[:], w3_words.rearrange("a p c i -> p a (c i)"))
 
-        for i in (0, 1, 4, 5):
+        for i in range(2 * PACK):
             x_tile(i)
+        for i in range(3):
             pick(i)
-        x_tile(6)
-        gather2(0, fresh("v2_w0", [P, M], U32))
-        words, scales = quantize("w2_first", first_bf[:].rearrange("p a t m j -> p (a t m j)"), 2 * PASS)
-        gather2(1, over("first_bf", "v2_w1", [P, M], U32, chunk // 2))
-        pick(6, "first_bf", 3 * chunk // 4)
-        for a in range(2):
-            b_passes(0, a, words[:, PASS * a : PASS * (a + 1)], scales[:, PASS * a : PASS * (a + 1)])
-        for i in (2, 3, 7):
-            x_tile(i)
+        gather2(0, over("x_sb2", "v2_w0", [P, M], U32))
+        w2_quantize(0, 0, first_bf, "x_sb1")
+        w3_w = over("tab2_w0", "w3_w", [P, 2, N], U32)
+        load(w3_w[:], w3_words.rearrange("a p c i -> p a (c i)"))
+        gather2(1, over("x_sb2", "v2_w1", [P, M], U32, 4 * M))
+        second_bf = over("first_bf", "second_bf", rounded_shape, BF16)
+        w2_round_pool(second_bf[:], w2_raw[0, 1, 0][:])
+        for i in range(3, 6):
+            pick(i)
+        w2_quantize(0, 1, second_bf, "x_sb5")
+        pick(6, "second_bf", chunk // 4)
 
-        third_bf = over("first_bf", "third_bf", [P, PACK, P, PACK], BF16)
-        w2_round_pool(third_bf[:], 1, 0)
-        last_bf = fresh("last_bf", [P, PACK, P, PACK], BF16)
-        w2_round(nc.scalar.copy, last_bf[:], 1, 1, 0, P // 2)
-        w2_round(nc.scalar.copy, last_bf[:], 1, 1, P // 2, P)
-        diff(0)
-        diff(1)
-        pick_diff(2, fresh("b_sb2", [P, M], F32))
-        words, scales = quantize("w2_third", third_bf[:].rearrange("p t m j -> p (t m j)"), PASS, "picked1")
-        b_passes(1, 0, words[:], scales[:])
-        words, scales = quantize("w2_last", last_bf[:].rearrange("p t m j -> p (t m j)"), PASS, "third_bf", chunk // 4)
-        b_passes(1, 1, words[:], scales[:])
-        pick_diff(3, over("third_bf", "b_sb3", [P, M], F32))
+        third_bf = over("v_w10", "third_bf", rounded_shape, BF16)
+        w2_round_scalar(third_bf[:], w2_raw[1, 0, 0][:])
+        last_bf = over("second_bf", "last_bf", rounded_shape, BF16, -chunk // 4)
+        w2_round_pool(last_bf[:, :, : P // 2, :], w2_raw[1, 1, 0][:])
+        w2_round_scalar(last_bf[:, :, P // 2 :, :], w2_raw[1, 1, P // 2][:])
+
+        r[0] = over("w2_raw11_0", "r0", [P, PACK, M], F32)
+        r[1] = fresh("r1", [P, PACK, M], F32)
+        for i in range(3):
+            diff(i)
+        w2_quantize(1, 0, third_bf, "picked1")
+        diff(3)
+        w2_quantize(1, 1, last_bf)
         pick(7, "last_bf")
-        roots(0, 0, M, over("w2_raw11_0", "r0", [P, PACK, M], F32))
         for i in range(PACK, 2 * PACK):
             diff(i)
 
-        half = M // 2
-        for lo in (0, half):
-            roots(1, lo, lo + half, fresh("r1_%d" % lo, [P, PACK, half], F32))
-
-        low = [z_round(h, 0, half, 0) for h in range(2)]
-        for h in range(2):
-            words, scales = quantize("z_low%d" % h, low[h], half)
-            out_passes(0, half, 2, h, words[:], scales[:])
-        store(0, half, 2, nc.scalar.copy, nc.scalar.copy)
-
-        pieces = ((half, half + P, 4), (half + P, M, 2))
-        high = z_round(0, half, M, 0, "z_bf0_0")
-        last = [z_round(1, half, half + P, half)]
-        words, scales = quantize("z_high", high, half)
+        pieces = ((0, M // 2, 2), (M // 2, M // 2 + P, 4), (M // 2 + P, M, 2))
+        words, scales = quantize("z_first", z_round(0, 0, M), M)
         for lo, hi, rows in pieces:
-            out_passes(lo, hi, rows, 0, words[:, lo - half : hi - half], scales[:, lo - half : hi - half])
-        last.append(z_round(1, half + P, M, half))
-        copies = ((nc.scalar.copy,), (nc.scalar.copy, nc.vector.tensor_copy))
-        for (lo, hi, rows), values, copy in zip(pieces, last, copies):
-            words, scales = quantize("z_last%d" % lo, values, hi - lo)
+            out_passes(lo, hi, rows, 0, words[:, lo:hi], scales[:, lo:hi])
+        copies = ((nc.scalar.copy, nc.scalar.copy), (nc.vector.tensor_copy,), (nc.scalar.copy, nc.vector.tensor_copy))
+        rounded = [z_round(1, *pieces[0][:2])]
+        for k, (lo, hi, rows) in enumerate(pieces):
+            if k + 1 < len(pieces):
+                rounded.append(z_round(1, *pieces[k + 1][:2]))
+            words, scales = quantize("z_last%d" % lo, rounded[k], hi - lo)
             out_passes(lo, hi, rows, 1, words[:], scales[:])
-            store(lo, hi, rows, *copy)
+            store(lo, hi, rows, *copies[k])

@@ -22,8 +22,8 @@ PACK = 4
 PASS = 512
 BANK = 512
 ROWS = 32
-X_BANKS = 4
-POOL_PIECE = P // 4
+X_BANKS = 3
+FUSED = 3
 BIG = 1e38
 W1, V2, W3, JOINED = S, S + H, S + H + M, S + H + M + N
 
@@ -77,7 +77,7 @@ def tile_list_tract_county_audit_kernel(
         joined = planes[0]
         w1_raw = [fresh("w1_raw0", [P, 2, 2 * PASS], U8, room=chunk)]
         tab_w = [fresh("tab_w%d" % a, [P, T], U32) for a in range(2)]
-        first_bf = fresh("first_bf", [P, PACK, P, PACK], BF16)
+        first_bf = fresh("first_bf", [P, PACK, P, PACK], BF16, room=3 * chunk // 4)
         g = fresh("g", [P, 2, PACK], F32)
 
         load_rows(tab_sc[:ROWS, :], tab_scales)
@@ -156,17 +156,22 @@ def tile_list_tract_county_audit_kernel(
         nc.vector.reciprocal(g_raw_inv[:], g[:])
         nc.vector.tensor_scalar(g_inv[:], g_raw_inv[:], BIG, -BIG, ALU.min, ALU.max)
         tab2_load(0, "tab_w0", 0)
-        tab2_load(1, "tab_w0", chunk)
+        g_neg = fresh("g_neg", [P, 2, PACK], F32)
+        nc.vector.tensor_scalar(g_neg[:], g[:], -1.0, None, ALU.mult)
+        w2_load(0, 1, "tab_w0", chunk)
         gather1(1, 0)
         gather1(1, 1)
-        w2_load(0, 1, "tab_w1")
+        tab2_load(1, "tab_w1", 0)
         w2_load(1, 0, "tab_w1", chunk)
         w1_deal(1, fresh("w1_w1", [P, 2, 2 * PASS], U8))
 
         x_sb = [fresh("x_sb%d" % i, [P, S], F32) for i in range(2 * PACK)]
 
+        x_done = []
+
         def x_tile(i):
-            banks = [bank((2 * i + half) % X_BANKS, [P, BANK]) for half in range(2)]
+            banks = [bank((2 * len(x_done) + half) % X_BANKS, [P, BANK]) for half in range(2)]
+            x_done.append(i)
             for a in range(2):
                 for half in range(2):
                     nc.tensor.matmul_mx(
@@ -178,7 +183,7 @@ def tile_list_tract_county_audit_kernel(
                         start=(a == 0), stop=(a == 1))
             for half in range(2):
                 nc.scalar.activation(x_sb[i][:, BANK * half : BANK * (half + 1)], banks[half][:], ACT.Copy,
-                                     scale=g[:, i // PACK, i % PACK : i % PACK + 1])
+                                     scale=(g_neg if i == FUSED else g)[:, i // PACK, i % PACK : i % PACK + 1])
 
         picked = {}
 
@@ -200,10 +205,8 @@ def tile_list_tract_county_audit_kernel(
                 nc.scalar.copy(out=dst[:, :, :, t : t + 2], in_=src[:, :, :, t : t + 2])
 
         def w2_round_pool(rounded, raw):
-            dst = rounded.rearrange("p t m j -> p m t j")
-            src = raw.rearrange("p j (m t) -> p m t j", t=PACK)
-            for lo in range(0, dst.shape[1], POOL_PIECE):
-                nc.gpsimd.tensor_copy(out=dst[:, lo : lo + POOL_PIECE], in_=src[:, lo : lo + POOL_PIECE])
+            nc.gpsimd.tensor_copy(out=rounded.rearrange("p t m j -> p m t j"),
+                                  in_=raw.rearrange("p j (m t) -> p m t j", t=PACK))
 
         def quantize(name, values, columns, earlier=None, shift=0):
             shape = [P, columns]
@@ -226,15 +229,22 @@ def tile_list_tract_county_audit_kernel(
         e = [fresh("e%d" % h, [P, PACK, M], F32) for h in range(2)]
         r = {}
 
+        def square(i):
+            h, t = divmod(i, PACK)
+            nc.scalar.activation(r[h][:, t, :], e[h][:, t, :], ACT.Square, scale=g_inv[:, h, t : t + 1])
+
+        def root(i):
+            h, t = divmod(i, PACK)
+            nc.scalar.activation(r[h][:, t, :], r[h][:, t, :], ACT.Abs_reciprocal_sqrt, bias=1.0)
+
         def diff(i):
             h, t = divmod(i, PACK)
             nc.vector.scalar_tensor_tensor(out=e[h][:, t, :], in0=b_banks[i][:], scalar=g[:, h, t : t + 1],
                                            in1=picked[i][:], op0=ALU.mult, op1=ALU.subtract)
-            nc.scalar.activation(r[h][:, t, :], e[h][:, t, :], ACT.Square, scale=g_inv[:, h, t : t + 1])
-            nc.scalar.activation(r[h][:, t, :], r[h][:, t, :], ACT.Abs_reciprocal_sqrt, bias=1.0)
 
-        def z_round(h, lo, hi):
-            z_bf = fresh("z_bf%d_%d" % (h, lo), [P, hi - lo, PACK], BF16)
+        def z_round(h, lo, hi, earlier=None):
+            name, shape = "z_bf%d_%d" % (h, lo), [P, hi - lo, PACK]
+            z_bf = over(earlier, name, shape, BF16) if earlier else fresh(name, shape, BF16)
             nc.vector.tensor_tensor(
                 out=z_bf[:].rearrange("p (c i) t -> p c t i", i=2),
                 in0=e[h][:, :, lo:hi].rearrange("p t (c i) -> p c t i", i=2),
@@ -271,41 +281,51 @@ def tile_list_tract_county_audit_kernel(
         w2_load(1, 1, "w2_raw00_0", 0, 0, P // 2)
         w2_load(1, 1, "w2_raw00_0", chunk // 2, P // 2, P)
 
-        for i in range(2 * PACK):
+        plain = [i for i in range(2 * PACK) if i != FUSED]
+        for i in plain + [FUSED]:
             x_tile(i)
-        for i in range(3):
+        for i in plain[:5]:
             pick(i)
-        gather2(0, over("x_sb2", "v2_w0", [P, M], U32))
-        w2_quantize(0, 0, first_bf, "x_sb1")
+        gather2(0, fresh("v2_w0", [P, M], U32))
+        w2_quantize(0, 0, first_bf)
         w3_w = over("tab2_w0", "w3_w", [P, 2, N], U32)
         load(w3_w[:], w3_words.rearrange("a p c i -> p a (c i)"))
-        gather2(1, over("x_sb2", "v2_w1", [P, M], U32, 4 * M))
+        gather2(1, fresh("v2_w1", [P, M], U32))
         second_bf = over("first_bf", "second_bf", rounded_shape, BF16)
         w2_round_pool(second_bf[:], w2_raw[0, 1, 0][:])
-        for i in range(3, 6):
-            pick(i)
         w2_quantize(0, 1, second_bf, "x_sb5")
-        pick(6, "second_bf", chunk // 4)
+        pick(6, "second_bf")
 
         third_bf = over("v_w10", "third_bf", rounded_shape, BF16)
         w2_round_scalar(third_bf[:], w2_raw[1, 0, 0][:])
-        last_bf = over("second_bf", "last_bf", rounded_shape, BF16, -chunk // 4)
+        last_bf = over("second_bf", "last_bf", rounded_shape, BF16, chunk // 4)
         w2_round_pool(last_bf[:, :, : P // 2, :], w2_raw[1, 1, 0][:])
-        w2_round_scalar(last_bf[:, :, P // 2 :, :], w2_raw[1, 1, P // 2][:])
+        w2_round_pool(last_bf[:, :, P // 2 :, :], w2_raw[1, 1, P // 2][:])
 
-        r[0] = over("w2_raw11_0", "r0", [P, PACK, M], F32)
+        r[0] = over("w2_raw10_0", "r0", [P, PACK, M], F32)
         r[1] = fresh("r1", [P, PACK, M], F32)
-        for i in range(3):
+        for i in range(FUSED):
             diff(i)
+        square(0)
+        square(1)
+        b_sb = over("w2_raw11_0", "b_sb", [P, M], F32)
+        nc.scalar.activation(b_sb[:], b_banks[FUSED][:], ACT.Copy, scale=g[:, 0, FUSED : FUSED + 1])
         w2_quantize(1, 0, third_bf, "picked1")
-        diff(3)
+        nc.vector.tensor_tensor(e[0][:, FUSED, :], x_sb[FUSED][:].indirect(pos_sb[:]), b_sb[:], ALU.add)
         w2_quantize(1, 1, last_bf)
         pick(7, "last_bf")
         for i in range(PACK, 2 * PACK):
             diff(i)
+        for i in range(2 * PACK):
+            if i == PACK:
+                square(i)
+                square(i + 1)
+            root(i)
+            if i % PACK + 2 < PACK:
+                square(i + 2)
 
         pieces = ((0, M // 2, 2), (M // 2, M // 2 + P, 4), (M // 2 + P, M, 2))
-        words, scales = quantize("z_first", z_round(0, 0, M), M)
+        words, scales = quantize("z_first", z_round(0, 0, M, "picked6"), M)
         for lo, hi, rows in pieces:
             out_passes(lo, hi, rows, 0, words[:, lo:hi], scales[:, lo:hi])
         copies = ((nc.scalar.copy, nc.scalar.copy), (nc.vector.tensor_copy,), (nc.scalar.copy, nc.vector.tensor_copy))

@@ -229,13 +229,13 @@ def tile_list_tract_county_audit_kernel(
         e = [fresh("e%d" % h, [P, PACK, M], F32) for h in range(2)]
         r = {}
 
-        def square(i):
+        def square(i, cols=slice(0, M)):
             h, t = divmod(i, PACK)
-            nc.scalar.activation(r[h][:, t, :], e[h][:, t, :], ACT.Square, scale=g_inv[:, h, t : t + 1])
+            nc.scalar.activation(r[h][:, t, cols], e[h][:, t, cols], ACT.Square, scale=g_inv[:, h, t : t + 1])
 
-        def root(i):
+        def root(i, cols=slice(0, M)):
             h, t = divmod(i, PACK)
-            nc.scalar.activation(r[h][:, t, :], r[h][:, t, :], ACT.Abs_reciprocal_sqrt, bias=1.0)
+            nc.scalar.activation(r[h][:, t, cols], r[h][:, t, cols], ACT.Abs_reciprocal_sqrt, bias=1.0)
 
         def diff(i):
             h, t = divmod(i, PACK)
@@ -294,7 +294,7 @@ def tile_list_tract_county_audit_kernel(
         second_bf = over("first_bf", "second_bf", rounded_shape, BF16)
         w2_round_pool(second_bf[:], w2_raw[0, 1, 0][:])
         w2_quantize(0, 1, second_bf, "x_sb5")
-        pick(6, "second_bf")
+        pick(6, "w2_raw01_0")
 
         third_bf = over("v_w10", "third_bf", rounded_shape, BF16)
         w2_round_scalar(third_bf[:], w2_raw[1, 0, 0][:])
@@ -302,37 +302,54 @@ def tile_list_tract_county_audit_kernel(
         w2_round_pool(last_bf[:, :, : P // 2, :], w2_raw[1, 1, 0][:])
         w2_round_pool(last_bf[:, :, P // 2 :, :], w2_raw[1, 1, P // 2][:])
 
-        r[0] = over("w2_raw10_0", "r0", [P, PACK, M], F32)
+        r[0] = over("w2_raw10_0", "r0", [P, PACK, M], F32, -chunk // 4)
         r[1] = fresh("r1", [P, PACK, M], F32)
         for i in range(FUSED):
             diff(i)
+        b_sb = over("w2_raw10_0", "b_sb", [P, M], F32, 3 * chunk // 4)
+        nc.scalar.activation(b_sb[:], b_banks[FUSED][:], ACT.Copy, scale=g[:, 0, FUSED : FUSED + 1])
         square(0)
         square(1)
-        b_sb = over("w2_raw11_0", "b_sb", [P, M], F32)
-        nc.scalar.activation(b_sb[:], b_banks[FUSED][:], ACT.Copy, scale=g[:, 0, FUSED : FUSED + 1])
         w2_quantize(1, 0, third_bf, "picked1")
         nc.vector.tensor_tensor(e[0][:, FUSED, :], x_sb[FUSED][:].indirect(pos_sb[:]), b_sb[:], ALU.add)
         w2_quantize(1, 1, last_bf)
-        pick(7, "last_bf")
+        pick(7, "w2_raw11_64")
         for i in range(PACK, 2 * PACK):
             diff(i)
-        for i in range(2 * PACK):
-            if i == PACK:
-                square(i)
-                square(i + 1)
+        for i in range(PACK):
             root(i)
-            if i % PACK + 2 < PACK:
+            if i + 2 < PACK:
                 square(i + 2)
+        for step in (square, root):
+            step(4)
+            step(5)
+        lower, upper = slice(0, M // 2), slice(M // 2, M)
+        squares = fresh("squares", [P, M // 2], F32)
+        square(6, lower)
+        nc.scalar.activation(squares[:], e[1][:, 3, lower], ACT.Square, scale=g_inv[:, 1, 3:4])
+        root(6, lower)
+        nc.scalar.activation(r[1][:, 3, lower], squares[:], ACT.Abs_reciprocal_sqrt, bias=1.0)
+        for step in (square, root):
+            step(6, upper)
+            step(7, upper)
 
-        pieces = ((0, M // 2, 2), (M // 2, M // 2 + P, 4), (M // 2 + P, M, 2))
-        words, scales = quantize("z_first", z_round(0, 0, M, "picked6"), M)
-        for lo, hi, rows in pieces:
-            out_passes(lo, hi, rows, 0, words[:, lo:hi], scales[:, lo:hi])
-        copies = ((nc.scalar.copy, nc.scalar.copy), (nc.vector.tensor_copy,), (nc.scalar.copy, nc.vector.tensor_copy))
-        rounded = [z_round(1, *pieces[0][:2])]
-        for k, (lo, hi, rows) in enumerate(pieces):
-            if k + 1 < len(pieces):
-                rounded.append(z_round(1, *pieces[k + 1][:2]))
-            words, scales = quantize("z_last%d" % lo, rounded[k], hi - lo)
-            out_passes(lo, hi, rows, 1, words[:], scales[:])
-            store(lo, hi, rows, *copies[k])
+        half, quarter = M // 2, M // 4
+        first_lower = z_round(0, 0, half, "picked6")
+        first_upper = z_round(0, half, M, "picked7")
+        words, scales = quantize("z0_lower", first_lower, half)
+        out_passes(0, half, 1, 0, words[:], scales[:])
+        last_lower = z_round(1, 0, half)
+        words, scales = quantize("z0_upper", first_upper, half, "squares")
+        out_passes(half, half + quarter, 4, 0, words[:, :quarter], scales[:, :quarter])
+        out_passes(half + quarter, M, 2, 0, words[:, quarter:], scales[:, quarter:])
+        words, scales = quantize("z1_lower", last_lower, half)
+        out_passes(0, half, 1, 1, words[:], scales[:])
+        store(0, half, 1, *[nc.scalar.copy] * 4)
+        third = z_round(1, half, half + quarter)
+        fourth = z_round(1, half + quarter, M)
+        words, scales = quantize("z1_third", third, quarter)
+        out_passes(half, half + quarter, 4, 1, words[:], scales[:])
+        store(half, half + quarter, 4, nc.vector.tensor_copy)
+        words, scales = quantize("z1_fourth", fourth, quarter)
+        out_passes(half + quarter, M, 2, 1, words[:], scales[:])
+        store(half + quarter, M, 2, nc.scalar.copy, nc.vector.tensor_copy)

import math
from contextlib import ExitStack

import concourse.mybir as mybir

K, H, N, T, S, T2, M = 1024, 1024, 512, 4096, 1024, 2048, 512
FLOPS = 2 * K * H * S + 2 * K * H * M + 2 * H * N * M

F32 = mybir.dt.float32
BF16 = mybir.dt.bfloat16
I32 = mybir.dt.int32
U32 = mybir.dt.uint32
U16 = mybir.dt.uint16
U8 = mybir.dt.uint8
FP8X4 = mybir.dt.float8_e4m3fn_x4
FP4X4 = mybir.dt.float4_e2m1fn_x4
ALU = mybir.AluOpType
ACT = mybir.ActivationFunctionType

P = 128
PACK = 4
PASS = 512
BANK = 512
ROWS = 32
X_BANKS = 3
FUSED = 3
BIG = 1e38
W1, V2, W3, JOINED = S, S + H, S + H + M, S + H + M + N


def tile_list_tract_county_audit_kernel(
    tc, tab_words, tab_scales, offs, pos1, tab2_words, tab2_scales, offs2,
    w1_words, w1_scales, w2, gain, w3_words, w3_scales, out,
):
    nc = tc.nc
    with ExitStack() as ctx:
        lists = ctx.enter_context(tc.tile_pool(name="lists", bufs=1))
        sbuf = ctx.enter_context(tc.tile_pool(name="sbuf", bufs=1))
        psum = ctx.enter_context(tc.psum_pool(name="psum", bufs=1))
        width = {F32: 4, U32: 4, BF16: 2, U8: 1}
        start = {"free": 0}

        def fresh(name, shape, dtype, room=0):
            start[name] = start["free"]
            size = max(room, math.prod(shape[1:]) * width[dtype])
            start["free"] = start[name] + 256 * math.ceil(size / 256)
            return sbuf.tile(shape, dtype, name=name, align_bytes=64, offset=start[name])

        def over(earlier, name, shape, dtype, shift=0):
            start[name] = start[earlier] + shift
            return sbuf.tile(shape, dtype, name=name, align_bytes=64, offset=start[name])

        def bank(index, shape):
            return psum.tile(shape, F32, name="bank", tag="bank%d" % index)

        def load(tile, dram):
            nc.sync.dma_start(out=tile.bitcast(I32), in_=dram.bitcast(I32))

        def load_rows(rows, dram):
            nc.sync.dma_start(out=rows.bitcast(I32), in_=dram.bitcast(I32).rearrange("a q c -> (a q) c"))

        def w1_half(h):
            return w1_words[:, :, 2 * PASS * h : 2 * PASS * (h + 1)].rearrange("a p c -> p a c")

        def w2_cols(h, a, first, last):
            cols = slice(PASS * h + PACK * first, PASS * h + PACK * last)
            return w2[PASS * a : PASS * (a + 1), cols].rearrange("(p j) c -> p j c", j=PACK)

        chunk = 4 * PACK * PASS
        offs_sb = lists.tile([P, S // 16], U16, name="offs_sb")
        offs2_sb = lists.tile([P, M // 16], U16, name="offs2_sb")
        pos_sb = lists.tile([P, M // 16], U16, name="pos_sb")
        tab_sc = fresh("tab_sc", [P, T], U8)
        w1_sc = fresh("w1_sc", [P, H], U8)
        tab2_sc = fresh("tab2_sc", [P, T2], U8)
        planes = [fresh("plane%d" % a, [P, JOINED], U8) for a in range(2)]
        joined = planes[0]
        w1_raw = [fresh("w1_raw0", [P, 2, 2 * PASS], U8, room=chunk)]
        tab_w = [fresh("tab_w%d" % a, [P, T], U32) for a in range(2)]
        first_bf = fresh("first_bf", [P, PACK, P, PACK], BF16, room=3 * chunk // 4)
        g = fresh("g", [P, 2, PACK], F32)

        load_rows(tab_sc[:ROWS, :], tab_scales)
        nc.sync.dma_start(offs_sb[:], offs)
        load_rows(w1_sc[:ROWS, :], w1_scales)
        load_rows(tab2_sc[:ROWS, :], tab2_scales)
        nc.sync.dma_start(offs2_sb[:], offs2)
        load_rows(joined[:ROWS, W3:], w3_scales)
        load(w1_raw[0][:], w1_half(0))
        load(tab_w[0][:], tab_words[0].rearrange("p t i -> p (t i)"))
        nc.sync.dma_start(pos_sb[:], pos1)
        nc.sync.dma_start(out=g[:], in_=gain.rearrange("(a p t) -> p a t", a=2, t=PACK))
        load(tab_w[1][:], tab_words[1].rearrange("p t i -> p (t i)"))

        for idle in (slice(32, 64), slice(64, P)):
            for tile in (tab_sc, tab2_sc):
                nc.vector.memset(tile[idle, :].bitcast(I32), 0)
            for tile in (w1_sc, joined[:, W3:]):
                nc.gpsimd.memset(tile[idle, :].bitcast(I32), 0)
        warm = fresh("warm", [P, 1], F32)
        warm_out = fresh("warm_out", [P, 1], F32)
        nc.vector.memset(warm[:], 1.0)
        nc.scalar.activation(warm_out[:], warm[:], ACT.Abs_reciprocal_sqrt, bias=1.0)
        nc.gpsimd.memset(planes[1][:].bitcast(I32), 0)

        nc.gpsimd.tensor_copy(
            out=joined[:, W1:V2].rearrange("p (h t m) -> p h t m", h=2, t=PACK),
            in_=w1_sc[:].rearrange("p (h m t) -> p h t m", h=2, t=PACK))
        v_sc = fresh("v_sc", [P, S], U8)
        v2_sc = fresh("v2_sc", [P, M], U8, room=4 * PASS)
        nc.vector.tensor_copy(out=v_sc[:], in_=tab_sc[:].indirect(offs_sb[:]))
        nc.vector.tensor_copy(out=v2_sc[:], in_=tab2_sc[:].indirect(offs2_sb[:]))
        nc.vector.tensor_copy(out=joined[:, :W1].bitcast(I32), in_=v_sc[:].bitcast(I32))
        nc.vector.tensor_copy(out=joined[:, V2:W3].bitcast(I32), in_=v2_sc[:].bitcast(I32))
        for group in range(1, 8):
            a, q = divmod(group, 4)
            nc.sync.dma_start(out=planes[a][32 * q : 32 * q + 4, :].bitcast(I32),
                              in_=joined[4 * group : 4 * group + 4, :].bitcast(I32))

        w1_w = {}

        def w1_deal(h, tile):
            w1_w[h] = tile
            nc.vector.tensor_copy(out=tile[:].bitcast(U16).rearrange("p a (t m) -> p a t m", t=PACK),
                                  in_=w1_raw[h][:].bitcast(U16).rearrange("p a (m t) -> p a t m", t=PACK))

        w1_raw.append(over("v2_sc", "w1_raw1", [P, 2, 2 * PASS], U8))
        load(w1_raw[1][:], w1_half(1))
        w1_deal(0, over("tab2_sc", "w1_w0", [P, 2, 2 * PASS], U8))

        v_w = {}

        def gather1(a, half):
            v_w[a, half] = fresh("v_w%d%d" % (a, half), [P, BANK], U32)
            nc.vector.tensor_copy(out=v_w[a, half][:],
                                  in_=tab_w[a][:].indirect(offs_sb[:, 32 * half : 32 * (half + 1)]))

        w2_raw = {}

        def w2_load(h, a, earlier, shift=0, first=0, last=P):
            tile = over(earlier, "w2_raw%d%d_%d" % (h, a, first), [P, PACK, PACK * (last - first)], F32, shift)
            nc.sync.dma_start(out=tile[:], in_=w2_cols(h, a, first, last))
            w2_raw[h, a, first] = tile

        tab2_w = {}

        def tab2_load(a, earlier, shift):
            tab2_w[a] = over(earlier, "tab2_w%d" % a, [P, T2], U32, shift)
            load(tab2_w[a][:], tab2_words[a].rearrange("p t i -> p (t i)"))

        w2_load(0, 0, "w1_raw0")
        gather1(0, 0)
        gather1(0, 1)
        g_raw_inv = fresh("g_raw_inv", [P, 2, PACK], F32)
        g_inv = fresh("g_inv", [P, 2, PACK], F32)
        nc.vector.reciprocal(g_raw_inv[:], g[:])
        nc.vector.tensor_scalar(g_inv[:], g_raw_inv[:], BIG, -BIG, ALU.min, ALU.max)
        tab2_load(0, "tab_w0", 0)
        g_neg = fresh("g_neg", [P, 2, PACK], F32)
        nc.vector.tensor_scalar(g_neg[:], g[:], -1.0, None, ALU.mult)
        w2_load(0, 1, "tab_w0", chunk)
        gather1(1, 0)
        gather1(1, 1)
        tab2_load(1, "tab_w1", 0)
        w2_load(1, 0, "tab_w1", chunk)
        w1_deal(1, fresh("w1_w1", [P, 2, 2 * PASS], U8))

        x_sb = [fresh("x_sb%d" % i, [P, S], F32) for i in range(2 * PACK)]

        x_done = []

        def x_tile(i):
            banks = [bank((2 * len(x_done) + half) % X_BANKS, [P, BANK]) for half in range(2)]
            x_done.append(i)
            for a in range(2):
                for half in range(2):
                    nc.tensor.matmul_mx(
                        out=banks[half][:],
                        lhsT=w1_w[i // PACK][:, a, 2 * P * (i % PACK) : 2 * P * (i % PACK + 1)].bitcast(FP4X4),
                        lhsT_scale=planes[a][:, W1 + P * i : W1 + P * (i + 1)],
                        rhs=v_w[a, half][:].bitcast(FP8X4),
                        rhs_scale=planes[a][:, BANK * half : BANK * (half + 1)],
                        start=(a == 0), stop=(a == 1))
            for half in range(2):
                nc.scalar.activation(x_sb[i][:, BANK * half : BANK * (half + 1)], banks[half][:], ACT.Copy,
                                     scale=(g_neg if i == FUSED else g)[:, i // PACK, i % PACK : i % PACK + 1])

        picked = {}

        def pick(i, earlier=None, shift=0):
            name = "picked%d" % i
            picked[i] = over(earlier, name, [P, M], F32, shift) if earlier else fresh(name, [P, M], F32)
            nc.vector.tensor_copy(out=picked[i][:], in_=x_sb[i][:].indirect(pos_sb[:]))

        v2_w = {}

        def gather2(a, tile):
            v2_w[a] = tile
            nc.vector.tensor_copy(out=v2_w[a][:], in_=tab2_w[a][:].indirect(offs2_sb[:]))

        def w2_round_scalar(rounded, raw):
            dst = rounded.rearrange("p t m j -> p m j t")
            src = raw.rearrange("p j (m t) -> p m j t", t=PACK)
            for t in (0, 2):
                nc.scalar.copy(out=dst[:, :, :, t : t + 2], in_=src[:, :, :, t : t + 2])

        def w2_round_pool(rounded, raw):
            nc.gpsimd.tensor_copy(out=rounded.rearrange("p t m j -> p m t j"),
                                  in_=raw.rearrange("p j (m t) -> p m t j", t=PACK))

        def quantize(name, values, columns, earlier=None, shift=0):
            shape = [P, columns]
            words = over(earlier, name + "_w", shape, U32, shift) if earlier else fresh(name + "_w", shape, U32)
            scales = fresh(name + "_sc", [P, columns], U8)
            nc.vector.quantize_mx(out=words[:].bitcast(FP8X4), scales=scales[:], in_=values)
            return words, scales

        b_banks = {}

        def b_passes(h, a, words, scales):
            for t in range(PACK):
                if a == 0:
                    b_banks[PACK * h + t] = bank(PACK * (1 - h) + t, [P, M])
                cols = slice(P * t, P * (t + 1))
                nc.tensor.matmul_mx(
                    out=b_banks[PACK * h + t][:], lhsT=words[:, cols].bitcast(FP8X4), lhsT_scale=scales[:, cols],
                    rhs=v2_w[a][:].bitcast(FP8X4), rhs_scale=planes[a][:, V2:W3], start=(a == 0), stop=(a == 1))

        e = [fresh("e%d" % h, [P, PACK, M], F32) for h in range(2)]
        r = {}

        def square(i, cols=slice(0, M)):
            h, t = divmod(i, PACK)
            nc.scalar.activation(r[h][:, t, cols], e[h][:, t, cols], ACT.Square, scale=g_inv[:, h, t : t + 1])

        def root(i, cols=slice(0, M)):
            h, t = divmod(i, PACK)
            nc.scalar.activation(r[h][:, t, cols], r[h][:, t, cols], ACT.Abs_reciprocal_sqrt, bias=1.0)

        def diff(i):
            h, t = divmod(i, PACK)
            nc.vector.scalar_tensor_tensor(out=e[h][:, t, :], in0=b_banks[i][:], scalar=g[:, h, t : t + 1],
                                           in1=picked[i][:], op0=ALU.mult, op1=ALU.subtract)

        def z_round(h, lo, hi, earlier=None):
            name, shape = "z_bf%d_%d" % (h, lo), [P, hi - lo, PACK]
            z_bf = over(earlier, name, shape, BF16) if earlier else fresh(name, shape, BF16)
            nc.vector.tensor_tensor(
                out=z_bf[:].rearrange("p (c i) t -> p c t i", i=2),
                in0=e[h][:, :, lo:hi].rearrange("p t (c i) -> p c t i", i=2),
                in1=r[h][:, :, lo:hi].rearrange("p t (c i) -> p c t i", i=2), op=ALU.mult)
            return z_bf[:].rearrange("p m t -> p (m t)")

        out_banks = {}

        def out_passes(lo, hi, rows, h, words, scales):
            for n in range(N // P):
                key = (lo, n // rows)
                if key not in out_banks:
                    out_banks[key] = bank((PACK + len(out_banks)) % 8, [P, rows, hi - lo])
                nc.tensor.matmul_mx(
                    out=out_banks[key][:, n % rows, :], lhsT=w3_w[:, h, P * n : P * (n + 1)].bitcast(FP8X4),
                    lhsT_scale=planes[h][:, W3 + P * n : W3 + P * (n + 1)],
                    rhs=words.bitcast(FP8X4), rhs_scale=scales,
                    start=(h == 0 and n % rows == 0), stop=(h == 1 and n % rows == rows - 1))

        def store(lo, hi, rows, *copies):
            for group, copy in enumerate(copies):
                res = fresh("res%d_%d" % (lo, group), [P, rows, hi - lo], F32)
                copy(out=res[:], in_=out_banks[lo, group][:])
                nc.sync.dma_start(
                    out=out[P * rows * group : P * rows * (group + 1), lo:hi].rearrange("(n p) m -> p n m", p=P),
                    in_=res[:])

        def w2_quantize(h, a, rounded, *earlier):
            words, scales = quantize("w2_%d%d" % (h, a), rounded[:].rearrange("p t m j -> p (t m j)"), PASS, *earlier)
            b_passes(h, a, words[:], scales[:])

        rounded_shape = [P, PACK, P, PACK]
        w2_round_pool(first_bf[:], w2_raw[0, 0, 0][:])
        w2_load(1, 1, "w2_raw00_0", 0, 0, P // 2)
        w2_load(1, 1, "w2_raw00_0", chunk // 2, P // 2, P)

        plain = [i for i in range(2 * PACK) if i != FUSED]
        for i in plain + [FUSED]:
            x_tile(i)
        for i in plain[:5]:
            pick(i)
        gather2(0, fresh("v2_w0", [P, M], U32))
        w2_quantize(0, 0, first_bf)
        w3_w = over("tab2_w0", "w3_w", [P, 2, N], U32)
        load(w3_w[:], w3_words.rearrange("a p c i -> p a (c i)"))
        gather2(1, fresh("v2_w1", [P, M], U32))
        second_bf = over("first_bf", "second_bf", rounded_shape, BF16)
        w2_round_pool(second_bf[:], w2_raw[0, 1, 0][:])
        w2_quantize(0, 1, second_bf, "x_sb5")
        pick(6, "w2_raw01_0")

        third_bf = over("v_w10", "third_bf", rounded_shape, BF16)
        w2_round_scalar(third_bf[:], w2_raw[1, 0, 0][:])
        last_bf = over("second_bf", "last_bf", rounded_shape, BF16, chunk // 4)
        w2_round_pool(last_bf[:, :, : P // 2, :], w2_raw[1, 1, 0][:])
        w2_round_pool(last_bf[:, :, P // 2 :, :], w2_raw[1, 1, P // 2][:])

        r[0] = over("w2_raw10_0", "r0", [P, PACK, M], F32, -chunk // 4)
        r[1] = fresh("r1", [P, PACK, M], F32)
        for i in range(FUSED):
            diff(i)
        b_sb = over("w2_raw10_0", "b_sb", [P, M], F32, 3 * chunk // 4)
        nc.scalar.activation(b_sb[:], b_banks[FUSED][:], ACT.Copy, scale=g[:, 0, FUSED : FUSED + 1])
        square(0)
        square(1)
        w2_quantize(1, 0, third_bf, "picked1")
        nc.vector.tensor_tensor(e[0][:, FUSED, :], x_sb[FUSED][:].indirect(pos_sb[:]), b_sb[:], ALU.add)
        w2_quantize(1, 1, last_bf)
        pick(7, "w2_raw11_64")
        for i in range(PACK, 2 * PACK):
            diff(i)
        for i in range(PACK):
            root(i)
            if i + 2 < PACK:
                square(i + 2)
        for step in (square, root):
            step(4)
            step(5)
        lower, upper = slice(0, M // 2), slice(M // 2, M)
        squares = fresh("squares", [P, M // 2], F32)
        square(6, lower)
        nc.scalar.activation(squares[:], e[1][:, 3, lower], ACT.Square, scale=g_inv[:, 1, 3:4])
        root(6, lower)
        nc.scalar.activation(r[1][:, 3, lower], squares[:], ACT.Abs_reciprocal_sqrt, bias=1.0)
        for step in (square, root):
            step(6, upper)
            step(7, upper)

        half, quarter = M // 2, M // 4
        first_lower = z_round(0, 0, half, "picked6")
        first_upper = z_round(0, half, M, "picked7")
        words, scales = quantize("z0_lower", first_lower, half)
        out_passes(0, half, 1, 0, words[:], scales[:])
        last_lower = z_round(1, 0, half)
        words, scales = quantize("z0_upper", first_upper, half, "squares")
        out_passes(half, half + quarter, 4, 0, words[:, :quarter], scales[:, :quarter])
        out_passes(half + quarter, M, 2, 0, words[:, quarter:], scales[:, quarter:])
        words, scales = quantize("z1_lower", last_lower, half)
        out_passes(0, half, 1, 1, words[:], scales[:])
        store(0, half, 1, *[nc.scalar.copy] * 4)
        third = z_round(1, half, half + quarter)
        fourth = z_round(1, half + quarter, M)
        words, scales = quantize("z1_third", third, quarter)
        out_passes(half, half + quarter, 4, 1, words[:], scales[:])
        store(half, half + quarter, 4, nc.vector.tensor_copy)
        words, scales = quantize("z1_fourth", fourth, quarter)
        out_passes(half + quarter, M, 2, 1, words[:], scales[:])
        store(half + quarter, M, 2, nc.scalar.copy, nc.vector.tensor_copy)
